import numpy as np, ml_dtypes
CORES = [48,51,52,55]
N = 4
BF = ml_dtypes.bfloat16
L, H, M, E, HO, RO, C, R, ST, QO = 4096, 2048, 256, 16, 3, 5, 32, 96, 341, 4096
def parts(rng):
    v = rng.integers(0, 256, (N, 8, 16, L)); m = np.argsort(rng.random((N, 8, H)), axis=-1) + H
    return v, m, rng.integers(0, 1024, (N, 8, 16, 1)), rng.integers(0, 2048, (N, 8, 16, E // 16)), rng.integers(780, 1081, (N, 8, 1))
def joined(rng, n):
    p = np.tile(np.arange(L), (N, 8, 1))
    for r in range(N):
        for g in range(8):
            o = rng.permutation(L); s = int(n[r, g]); p[r, g, o[:s]] = o[s:2 * s]; p[r, g, o[s:2 * s]] = o[:s]
    return p
def left(rng, n):
    p = np.tile(np.arange(L), (N, 8, 1))
    for r in range(N):
        for g in range(8):
            s = int(n[r, g]); a, b = rng.permutation(H)[s:], H + rng.permutation(H)[s:]; p[r, g, a] = b; p[r, g, b] = a
    return p
def shares(rng):
    return (rng.choice(np.array([0.0, 0.1, 0.25, 0.4, 0.475]), (N, 8)) * L).astype(np.int64)
def first_hop(v, w, k):
    u = np.add.reduce(w[:, None] * np.roll(v, 8, axis=0), axis=0) & (L - 1)
    return (((u * u) >> 5)[:, None] + u[:, None] * np.ascontiguousarray(k.T).reshape(1, -1)) & (L - 1)
def plant(rng, v, w, k, a, ok):
    pool = rng.integers(0, 256, (16, H)); src, to = [], []
    for j, cs in enumerate(first_hop(pool, w, k).tolist()):
        if len(to) == len(a): break
        for c in cs:
            if ok[c]:
                ok[c] = False; src.append(j); to.append(c); break
    x = pool[:, src]; v[:, a[:len(to)]] = x
    v[:, to] = np.clip(np.roll(x, 8, axis=0) + rng.integers(-2, 3, x.shape), 0, 255)
    return np.array(to, np.int64)
def pack(v, p, m, w, k, t):
    return {"rec": np.ascontiguousarray(v.reshape(N, 128, L)).astype(np.float32).astype(BF), "pr": p.astype(np.int32), "mt": m.astype(np.int32),
            "w": w.reshape(N, 128, 1).astype(np.int32), "kk": np.ascontiguousarray(k.reshape(N, 128, E // 16)).astype(np.int32), "th": t.astype(np.int32)}
def setup_inputs(rng):
    v, m, w, k, t = parts(rng)
    return pack(v, joined(rng, shares(rng)), m, w, k, t)
def setup_inputs_room(rng):
    v, m, w, k, t0 = parts(rng)
    n = rng.choice(np.array([0, 1, C - 1, C, R - 1, R, R + 1, M - 1, M, M + 1, H]), (N, 8))
    n[0] = R; n[0, 6:] = np.array([1, M - 1]); n[1] = np.array([R, R + 1, R - 1, R, C, M, M + 1, 0]); n[N - 1] = R; n[N - 1, 6:] = np.array([C - 1, H])
    n[2] = rng.choice(np.array([M, M + 1, 2 * M]), 8); n[2, :2] = np.array([M, M + 1])
    t = np.where(rng.random((N, 8, 1)) < 0.5, 0, t0); t[0, :6] = 0; t[1, :4] = 0; t[N - 1, :6] = 0; t[2] = t0[2]; t[1, 5] = t0[1, 5]
    p = left(rng, n); every = np.arange(L)
    for g in range(8):
        a = np.nonzero(p[2, g, :H] == every[:H])[0][:M]
        plant(rng, v[2, g], w[2, g, :, 0], k[2, g], a, ((every >= H) & (p[2, g] != every)).tolist())
    o = rng.permutation(H); a = o[:M // 2]; ok = np.zeros(L, bool); ok[o[M // 2:]] = True
    s = np.concatenate([a, plant(rng, v[1, 5], w[1, 5, :, 0], k[1, 5], a, ok.tolist())])
    rest = np.setdiff1d(every[:H], s); b = H + rng.permutation(H)[:len(rest)]
    p[1, 5] = every; p[1, 5, rest] = b; p[1, 5, b] = rest
    return pack(v, p, m, w, k, t)
def setup_inputs_ties(rng):
    v, m, w, k, t = parts(rng); v = 64 * rng.integers(0, 4, v.shape); t = 64 * rng.integers(10, 17, t.shape)
    v[:, 1::2] = v[:, 1::2][..., rng.integers(0, 64, L)]
    return pack(v, joined(rng, shares(rng)), m, w, k, t)
def setup_inputs_alike(rng):
    v, m, w, k, t = parts(rng); n = shares(rng); n[:, 0] = 0; p = joined(rng, n)
    w[:, 0] = 0; t[:, 0] = 1600
    for r in range(1, N):
        t[r, 0] = 4095; v[r, 0] = rng.integers(0, 40 if r % 2 == 0 else 120, (16, L))
        v[r, 0, :, 0] = 255; v[r, 0, :, 1] = 0
    v[1, 0, :, 1:] = 0
    k[:, 1] = k[:, 1, :1, :1]; t[:, 1] = 1200
    v[:, 2] = rng.integers(0, 256, (N, 1, 1)); v[::2, 2] = rng.integers(0, 256, (v[::2, 2].shape[0], 16, 1)); t[:, 2] = 1
    v[:, 3] = v[:, 3][..., rng.integers(0, 8, L)]
    m[:, 4] = H + np.arange(H); p[:, 4] = np.arange(L); o = rng.permutation(H)[:H // 2]; p[:, 4, o] = o + H; p[:, 4, o + H] = o
    for z in (v, m, w, k, t, p): z[:, 5] = z[:1, 5]
    k[:, 6] = 0; t[:, 6] = 1300
    for r in range(N):
        old = v[r, 6].copy(); c, j = np.unique(first_hop(old, w[r, 6, :, 0], k[r, 6])[:, 0], return_index=True); v[r, 6][:, c] = old[:, j]
    o = np.arange(20, H - 20); p[:, 7] = np.arange(L)
    for r in range(N):
        b = H + rng.permutation(H)[:H - 40]; p[r, 7, o] = b; p[r, 7, b] = o
    return pack(v, p, m, w, k, t)
def setup_inputs_ends(rng):
    v, m, w, k, t = parts(rng)
    v = np.where(rng.random((N, 8, 1, L)) < 0.5, rng.choice(np.array([0, 0, 1, 254, 255, 255]), v.shape), v)
    w[:, ::2] = rng.choice(np.array([1, 1022, 1023]), (N, 4, 16, 1)); k[:, 1::2] = rng.choice(np.array([0, 1, 2046, 2047]), (N, 4, 16, E // 16))
    t = rng.choice(np.array([1, 4080, 4081, 4094, 4095]), t.shape); t[0, 0] = 4095; t[N - 1, 1] = 4095
    v[:, 3, :, ::7] = 255; v[:, 3, :, 1::7] = 0
    v[:, 4] = rng.integers(240, 256, (N, 16, L)); v[:, 4, :, ::9] = 255; t[:, 4] = 4080
    w[:, 4] = rng.integers(1022, 1024, (N, 16, 1)); w[::2, 4] = 1023
    return pack(v, joined(rng, shares(rng)), m, w, k, t)
def setup_inputs_spread(rng):
    v, m, w, k, t = parts(rng)
    v = (rng.random((N, 8, 16, L)) * np.exp2(8 * rng.random((N, 8, 1, L)))).astype(np.int64); w = np.exp2(10 * rng.random(w.shape)).astype(np.int64)
    k = np.exp2(11 * rng.random(k.shape)).astype(np.int64); t = np.minimum(np.exp2(7 + 5 * rng.random(t.shape)).astype(np.int64), 4095)
    return pack(np.minimum(v, 255), joined(rng, shares(rng)), m, np.minimum(w, 1023), np.minimum(k, 2047), t)
def check_inputs(d):
    bad = []; v = np.asarray(d["rec"]).astype(np.float32)
    if not np.all((v >= 0) & (v <= 255) & (v == np.floor(v))): bad.append("rec: whole numbers from 0 to 255")
    for k, lo, hi in (("pr", 0, L - 1), ("mt", H, L - 1), ("w", 0, 1023), ("kk", 0, 2047), ("th", 0, 4095)):
        if np.min(d[k]) < lo or np.max(d[k]) > hi: bad.append("range of " + k)
    p = np.clip(np.asarray(d["pr"]).astype(np.int64), 0, L - 1)
    if not np.all(np.take_along_axis(p, p, -1) == np.arange(L)): bad.append("pr: a partner's partner is the leaf itself")
    if not np.all(np.sort(np.asarray(d["mt"]), axis=-1) == np.arange(H, L)): bad.append("mt: each leaf of the second half once")
    return bad
def reference(rec, pr, mt, w, kk, th):
    G = N * 8; g = np.arange(G)[:, None]; X = (np.arange(16) + 8) & 15
    q = np.ascontiguousarray(np.asarray(rec).astype(np.float32).astype(np.int32).reshape(G, 16, L).transpose(0, 2, 1))
    p = pr.astype(np.int64).reshape(G, L); first = mt.astype(np.int64).reshape(G, H)
    m = np.zeros((G, L), np.int64); m[:, :H] = first; m[g, first] = np.arange(H)
    wv = w.astype(np.int64).reshape(G, 1, 16); kv = np.ascontiguousarray(kk.astype(np.int64).reshape(G, 16, E // 16).transpose(0, 2, 1)).reshape(G, 1, E)
    t0 = th.astype(np.int64).reshape(G); J = np.repeat(t0[:, None], L, axis=1); lane = np.arange(M)
    for t in range(RO):
        order = (ST * t + np.arange(H)) & (H - 1)
        loose = (p[:, order] == order).astype(np.int64); place = np.add.accumulate(loose, axis=1) - 1
        gi, ci = np.nonzero((loose == 1) & (place < M))
        a = np.zeros((G, M), np.int64); live = np.zeros((G, M), bool); a[gi, place[gi, ci]] = order[ci]; live[gi, place[gi, ci]] = True
        A = q[g, a][:, :, X]; y = A; bd = np.full((G, M), 1 << 20); bc = np.zeros((G, M), np.int64)
        for h in range(HO):
            u = np.add.reduce(wv * y, axis=2) & (L - 1)
            c = (((u * u) >> 5)[:, :, None] + kv * u[:, :, None]) & (L - 1)
            D = np.add.reduce(np.abs(q[g[:, :, None], c] - A[:, :, None, :]), axis=3)
            D = np.where(c == a[:, :, None], 4095, D)
            e = np.argmin(D, axis=2)[:, :, None]
            D = np.take_along_axis(D, e, 2)[:, :, 0]; c = np.take_along_axis(c, e, 2)[:, :, 0]
            bc = np.where(D < bd, c, bc); bd = np.where(D < bd, D, bd)
            y = (A + q[g, m[g, p[g, c]]]) >> 1
        prop = live & (bd < J[g, bc]); key = M * bd + lane
        least = np.full((G, L), 1 << 30); gi, li = np.nonzero(prop)
        np.minimum.at(least, (gi, a[gi, li]), key[gi, li]); np.minimum.at(least, (gi, bc[gi, li]), key[gi, li])
        stand = prop & (least[g, a] == key) & (least[g, bc] == key)
        gi, li = np.nonzero(stand); sa, sc, sd = a[gi, li], bc[gi, li], bd[gi, li]
        old = p[gi, sc]; p[gi, old] = old; J[gi, old] = t0[gi]
        p[gi, sa] = sc; p[gi, sc] = sa; J[gi, sa] = sd; J[gi, sc] = sd
        va, vc = q[gi, sa], q[gi, sc]
        q[gi, sa] = va + np.clip(vc[:, X] - va, -1, 1); q[gi, sc] = vc + np.clip(va[:, X] - vc, -1, 1)
        no = live & (p[g, a] == a); place = np.add.accumulate(no.astype(np.int64), axis=1) - 1
        gi, li = np.nonzero(no & (place < R)); s = np.zeros((G, R), np.int64); has = np.zeros((G, R), bool)
        s[gi, place[gi, li]] = a[gi, li]; has[gi, place[gi, li]] = True
        v = q[g, s]; come = np.zeros_like(v); there = np.zeros_like(has); i = np.arange(G)
        for d in range(1, N):
            src = ((i // 8 - d) % N) * 8 + ((i - d) & 7); b = slice((d - 1) * C, d * C)
            come[:, b] = v[src, b]; there[:, b] = has[src, b]
        gi, k = np.nonzero(has & there); q[gi, s[gi, k]] = come[gi, k]
        gi, k = np.nonzero(has[:, 1::2]); x, z = s[gi, 2 * k], s[gi, 2 * k + 1]; mx, mz = m[gi, x], m[gi, z]
        m[gi, x] = mz; m[gi, z] = mx; m[gi, mx] = z; m[gi, mz] = x
        hx, hz, hmx, hmz = q[gi, x, 8:], q[gi, z, 8:], q[gi, mx, 8:], q[gi, mz, 8:]
        q[gi, x, 8:] = hz; q[gi, z, 8:] = hx; q[gi, mx, 8:] = hmz; q[gi, mz, 8:] = hmx
    yq = np.ascontiguousarray(q[:, :QO].transpose(0, 2, 1)).reshape(N, 128, QO)
    return {"yq": yq.astype(np.float32).astype(BF), "yp": p.reshape(N, 8, L).astype(np.float32), "ym": np.ascontiguousarray(m[:, :H]).reshape(N, 8, H).astype(np.float32)}

@@ -1,0 +1,791 @@
+from concourse.bass import DstId, RemoteDMATransfer
+from concourse.mybir import AluOpType as A, AxisListType as AX, ActivationFunctionType as F
+
+RO, HO, STEP, NR = 5, 3, 341, 4
+WD = 4352
+NS = (2, 2)
+SR = (1, 1)
+S_IND = 4
+V_PAIR = 7
+LOOK, SKEW, SAME, CROSS, PE = 400.0, 0.0, 60.0, 120.0, 0.5
+B20 = float(1 << 20)
+TAG = float(1 << 21)
+BIG = 12582912.0
+M64 = 1.5 * 2.0 ** 29
+M4096 = 1.5 * 2.0 ** 35
+M2 = 1.5 * 2.0 ** 24
+
+SCRATCH = {}
+
+
+def _decl(dt_, spec):
+    for item in spec.split():
+        name, n = item.split(":")
+        SCRATCH[name] = ("sbuf", [128] + [int(x) for x in n.split("x")], dt_)
+
+
+_decl("bfloat16", "Q:4352 K1:4352 K2:4352 BITS:4096 FL:2048 XG:4096 AB:4096 AREP:4096 SBQ:5x768 LAND:5x96 "
+      "WX:512 NRB:256 QAM:256 GS2:256 LOB:256 BL64:136 SELLO:128 "
+      "IDb:128 nIDb:128 I65:136 BLKb:128 XP:128 BO:24 MRH:408 NRM:256 KSEL:128 DM:128 ROT:384 "
+      "UP:128 nUP:128 LOW:128 TRI:128 TRIx:128 TRIB:128 TMB:128 B2:144 B5:144 WM:512 CST:128 ONES:256 "
+      "X2:256 QA:256 QC:256 AX_:256 Y2:256 EQ:256 GB:256 U1:512 U2:256 GK:256 SGN:512 JUNK:512 FW:128 CTX:128 "
+      "IND:16x128 JB3:16x16 IND2:256 RF:16 R5:96 TQ:96 QM:192")
+_decl("float32", "ST:4352 MT:4096 MPP:4096 MPU:4096 AV:256 JF:256 MR:256 MG:256 DJ:128 COL:64 IDf:128 BLKf:128 DIFF:136 "
+      "M17:272 RS17:136 RESET:256 RM:256 Q8:8 SEL:512 SELT:8 KEEP:128 SHIFT:128 PO:128 MSW:384 TMP:512 BLD:1152 "
+      "A2:256 GSA:256 GSC:256 RP:512 T1:256 UM:256 SQ:256 CF:256 PM:6x144 STP:272 CS:6x136 XE:512 GM:256 "
+      "SC:768 YS:256 SM:832 LS:16 VV:512 SG:768 SGK:96 GMM:192 SW:288 PFW:136 KR:192")
+_decl("int32", "FLI:256 SI:256 CI:256 IB:400 BD:32 PI:32")
+_decl("uint16", "C16:256 L16:176 P16:384")
+for _b in range(8):
+    SCRATCH["ps%d" % _b] = ("psum", [128, 512], "float32")
+NDMA = 32
+SEMAPHORES = ["ev", "es", "et", "eg", "sent"] + ["arr%d" % t for t in range(RO)] + ["d%d" % i for i in range(NDMA)]
+
+
+def build(g, T, topo, core):
+    ops = []
+    rank = T.rank_of(core)
+    bonus = [0.0]
+
+    def r(name, lo=0, hi=None, step=1, row=None, p=None):
+        if hi is None:
+            hi = T[name].shape[1]
+        ps_ = slice(None) if p is None else p
+        if row is not None:
+            ps_ = slice(row, 128, 16)
+        return (T[name][ps_, lo:hi:step], name, lo, hi, row, (hi - lo + step - 1) // step)
+
+    def r3(name, i, lo=0, hi=None):
+        w = T[name].shape[2]
+        if hi is None:
+            hi = w
+        return (T[name][:, i, lo:hi], name, i * w + lo, i * w + hi, None, hi - lo)
+
+    def r3s(name, i0, i1, lo, hi, step=1):
+        w = T[name].shape[2]
+        return (T[name][:, i0:i1, lo:hi:step], name, i0 * w, i1 * w, None, (i1 - i0) * ((hi - lo + step - 1) // step))
+
+    def ind(win, off):
+        return (win[0].indirect(off[0]), win, off, 16 * off[5])
+
+    def isind(x):
+        return len(x) == 4
+
+    def regs(*xs):
+        out = []
+        for x in xs:
+            if isinstance(x, tuple):
+                out += [x[1], x[2]] if isind(x) else [x]
+        return out
+
+    def ap(x):
+        return x[0] if isinstance(x, tuple) else x
+
+    def two(x):
+        return not isind(x) and x[1][:2] != "ps" and SCRATCH[x[1]][2] in ("bfloat16", "uint16")
+
+    def add(eng, fns, reads, writes, cost, **kw):
+        o = dict(eng=eng, fns=fns, reads=reads, writes=writes, cost=cost, acc=False, sem=None, lat=0.0, bonus=bonus[0])
+        o.update(kw)
+        ops.append(o)
+
+    def vop(fn, out, ins, f):
+        rd, wr = regs(*ins), [out]
+        if isind(out):
+            rd, wr = rd + [out[2]], [out[1]]
+            c = 50 + 3.8 * out[3]
+        elif isind(ins[0]):
+            c = 50 + 1.56 * out[5]
+        else:
+            c = 20 + max(64, f * out[5])
+        add("v", [fn], rd, wr, c)
+
+    def cp(out, a):
+        vop(lambda: g.vector.tensor_copy(out[0], a[0]), out, [a], 0.5 if two(out) and two(a) else 1)
+
+    def tt(out, a, b, op):
+        f = 1 if isind(a) or a[1][:2] == "ps" or b[1][:2] == "ps" else 2
+        vop(lambda: g.vector.tensor_tensor(out[0], a[0], b[0], op), out, [a, b], f)
+
+    def ts(out, a, s1, op0, s2=None, op1=None):
+        f = 0.5 if two(out) and two(a) else 1
+        if op1 is None:
+            vop(lambda: g.vector.tensor_scalar(out[0], a[0], ap(s1), None, op0), out, [a, s1], f)
+        else:
+            vop(lambda: g.vector.tensor_scalar(out[0], a[0], ap(s1), ap(s2), op0, op1), out, [a, s1, s2], f)
+
+    def scan(out, d0, d1, op0, op1):
+        vop(lambda: g.vector.tensor_tensor_scan(out[0], d0[0], d1[0], 0.0, op0, op1), out, [d0, d1], 1)
+
+    def mset(out, v):
+        add("v", [lambda: g.vector.memset(out[0], v)], [], [out], 20 + max(64, out[5] * (0.5 if two(out) else 1)))
+
+    def act(out, a, fn=F.Identity, bias=None, scale=None, accum=None):
+        kw = {}
+        if bias is not None:
+            kw["bias"] = ap(bias)
+        if scale is not None:
+            kw["scale"] = ap(scale)
+        if accum is not None:
+            kw["accum_out"] = accum[0]
+        c = 65 + 1.56 * out[5] if isind(a) else 40 + max(64, out[5])
+        add("s", [lambda: g.scalar.activation(out[0], a[0], fn, **kw)], regs(a, bias, scale),
+            [out] + ([accum] if accum else []), c + (20 if accum else 0))
+
+    def mm(items, acc=False):
+        fns, rd, wr, c = [], [], [], 30.0
+        for (o, l, rr, st, sp) in items:
+            fns.append(lambda o=o, l=l, rr=rr, st=st, sp=sp: g.tensor.matmul(o[0], l[0], rr[0], st, sp))
+            rd += [l, rr]
+            wr.append(o)
+            c += PE * max(64, rr[5]) * (1 if two(l) else 4)
+        add("t", fns, rd, wr, c, acc=acc)
+
+    def iota(out, pat, base=0, cm=0):
+        if SCRATCH[out[1]][2] == "int32":
+            fn = lambda: g.iota(out[0], pat, base, cm)
+        else:
+            fn = lambda: g.iota(out[0], pat, base, cm, allow_small_or_imprecise_dtypes=True)
+        add("g", [fn], [], [out], 130 + 2 * out[5])
+
+    nd = [0]
+
+    def dma(q, out, a, rd, wr, lat, slow=False):
+        sem = "d%d" % nd[0]
+        nd[0] += 1
+        if slow:
+            fn = lambda: g.dma_start(out, a, allow_slow_non_contiguous=True)
+        else:
+            fn = lambda: {"g": g, "y": g.sync, "s": g.scalar}[q].dma_start(out, a)
+        add(q, [fn], rd, wr, 100.0, sem=sem, val=16, lat=lat)
+
+    def ps(b, lo=0, hi=512, step=1):
+        return r("ps%d" % b, lo, hi, step)
+
+    def col(i):
+        return r("COL", i, i + 1)
+
+    def sm(lo, n=16):
+        return r("SM", lo, lo + n)
+
+    def oh(f):
+        return col(16 + f)
+
+    bonus[0] = 20000.0
+    dma("y", T.IB[:, 0:256], T.pr[:], [], [r("IB", 0, 256)], 2000)
+    dma("g", T.IB[:, 384:385], T.w[:], [], [r("IB", 384, 388)], 2000, True)
+    dma("g", T.IB[:, 388:389], T.kk[:], [], [r("IB", 388, 392)], 2000, True)
+    mset(r("IB", 392, 396), 0)
+    dma("g", T.IB[4:128:16, 392:393], T.th[:], [], [r("IB", 392, 396)], 2000, True)
+    dma("y", T.IB[:, 256:384], T.mt[:], [], [r("IB", 256, 384)], 2000)
+    dma("s", T.Q[:, 0:2048], T.rec[:, 0:2048], [], [r("Q", 0, 2048)], 4500)
+    dma("y", T.Q[:, 2048:4096], T.rec[:, 2048:4096], [], [r("Q", 2048, 4096)], 4500)
+    JB3 = (T.JB3[:], "JB3", 0, 256, None, 256)
+    bonus[0] = 9000.0
+    iota(r("JF"), [[1, 256]])
+    iota(r("PI", 0, 1), [[0, 1]], 0, 1)
+    iota(r("MR"), [[0, 16], [1, 16]])
+    iota(r("MG"), [[1, 16], [0, 16]])
+    iota(r("DJ"), [[1, 128]], 0, -1)
+    iota(JB3, [[1, 256]])
+    iota(r("M17", 0, 136), [[0, 8], [1, 17]])
+    iota(r("M17", 136, 272), [[1, 8], [0, 17]])
+    bonus[0] = 0.0
+    mset(r("FL"), 0.0)
+    mset(r("AB", 0, 1088), 0.0)
+    for j in range(4):
+        act(r("ST", 1088 * j, 1088 * j + 1088), r("AB", 0, 1088), F.Copy)
+    for j in range(2):
+        act(r("MT", 1024 * j, 1024 * j + 1024), r("AB", 0, 1024), F.Copy)
+    PF, PR, PG, PG16 = col(0), col(1), col(2), col(3)
+    ts(r("PI", 1, 2), r("PI", 0, 1), 15, A.bitwise_and)
+    ts(r("PI", 2, 3), r("PI", 0, 1), 4, A.logical_shift_right)
+    cp(r("COL", 0, 3), r("PI", 0, 3))
+    ts(PG16, PG, 16.0, A.mult, 15.0, A.add)
+    ts(r("COL", 16, 32), r("JF", 0, 16), PR, A.is_equal)
+    DJ = r("DJ")
+    pf, idb, lob, jb, mf = (r("BLD", 0, 256), r("BLD", 256, 512), r("BLD", 512, 768), r("BLD", 768, 1024),
+                            r("BLD", 1024, 1152))
+    cp(pf, r("IB", 0, 256))
+    ts(col(4), PR, 256.0, A.mult)
+    ts(idb, r("JF"), col(4), A.add)
+    tt(r("LOB"), pf, idb, A.is_equal)
+    for j in range(8):
+        dma("ys"[j % 2], T.FL[16 * j + 5:16 * j + 6, :], T.LOB[16 * j:16 * j + 8, :], [r("LOB")], [r("FL", row=j)], 2000)
+    cp(lob, r("LOB"))
+    dma("y", T.ST[5:128:16, 0:4096], lob[0], [lob], [r("ST", 0, 4096, row=5)], 2500)
+    dma("s", T.ST[0:128:16, 0:4096], idb[0], [idb], [r("ST", 0, 4096, row=0)], 2500)
+    cp(mf, r("IB", 256, 384))
+    dma("y", T.ST[2:128:16, 0:2048], mf[0], [mf], [r("ST", 0, 2048, row=2)], 2500)
+    dma("y", T.ST[1:128:16, 0:4096], pf[0], [pf], [r("ST", 0, 4096, row=1)], 2500)
+    ts(r("IDb"), DJ, 0.0, A.is_equal)
+    ts(r("IDf"), DJ, 0.0, A.is_equal)
+    ts(r("BLKb"), r("MG", 0, 128), PG, A.is_equal)
+    ts(r("BLKf"), r("MG", 0, 128), PG, A.is_equal)
+    cp(r("COL", 5, 8), r("IB", 384, 396, 4))
+    mm([(ps(7, 0, 1), r("BLKf"), col(7), True, True)])
+    ts(jb, r("JF"), 0.0, A.mult, ps(7, 0, 1), A.add)
+    dma("y", T.ST[4:128:16, 0:4096], jb[0], [jb], [r("ST", 0, 4096, row=4)], 2500)
+    ts(r("B2"), r("JF", 0, 144), PG16, A.is_equal)
+    ts(r("B5"), r("B2"), oh(5), A.mult)
+    ts(r("TRI"), DJ, 0.0, A.is_ge)
+    ts(r("TRIx"), DJ, 0.0, A.is_gt)
+    tt(r("TRIB"), r("TRI"), r("BLKb"), A.mult)
+    tt(r("TMB"), r("TRIB"), r("BLKb"), A.subtract)
+    mset(r("ONES"), 1.0)
+    mset(r("Q", 4096, WD), 0.0)
+    LW = sm(0)
+    for j in range(3):
+        ts(sm(16 * j), r("JF", 0, 256, 16), PR, A.add, 4096.0, A.add)
+    ts(col(8), PR, 8.0, A.is_ge)
+    ts(col(9), col(8), -16.0, A.mult, 8.0, A.add)
+    ts(r("XP"), DJ, col(9), A.is_equal)
+    ts(r("nIDb"), r("IDb"), -1.0, A.mult)
+    tt(col(12), PF, PG, A.add)
+    ts(r("I65"), r("JF", 0, 136), col(12), A.is_equal, 262144.0, A.mult)
+    ts(r("TMP", 0, 128), r("IDf"), col(6), A.mult)
+    mm([(ps(7, 0, 128), r("BLKf"), r("TMP", 0, 128), True, True)])
+    ts(r("SI", 0, 128), ps(7, 0, 128), col(5), A.mult, 2048.0, A.add)
+    ts(r("SI", 128, 256), r("SI", 0, 128), 4095, A.bitwise_and)
+    ts(r("TMP", 128, 256), r("SI", 128, 256), -2048.0, A.add, 0.5, A.mult)
+    ts(r("TMP", 0, 128), r("BLKf"), col(5), A.mult, 0.5, A.mult)
+    ts(r("WM", 0, 256), r("TMP", 0, 256), M64 / 2, A.add, M64 / 2, A.subtract)
+    tt(r("WM", 256, 512), r("TMP", 0, 256), r("WM", 0, 256), A.subtract)
+    mm([(ps(7), r("XP"), r("WM"), True, True)])
+    act(r("WX"), ps(7), F.Copy, scale=2.0)
+    ts(col(10), PF, 0.0, A.is_equal, -2048.0, A.mult)
+    ts(col(11), PF, 1.0, A.is_equal, 0.5, A.mult)
+    ts(r("CST"), r("ONES", 0, 128), col(10), A.mult, col(11), A.add)
+    ts(r("Q8"), r("JF", 0, 8), PG, A.is_equal)
+    for j, v in enumerate((128.0, -64.0)):
+        ts(r("BO", 8 * j, 8 * j + 8), r("Q8"), v, A.mult)
+    for h in range(HO):
+        ts(r("MRH", 136 * h, 136 * h + 136), r("M17", 0, 136), 16.0 * h, A.add)
+        for k in range(1, 8, 2):
+            ts(r("MRH", 136 * h + 17 * k, 136 * h + 17 * k + 17), r("M17", 0, 17), 16.0 * h + 0.5, A.add)
+    mset(r("MRH", 16, 408, 17), TAG)
+    ts(r("TMP", 256, 393), r("JF", 0, 137), -1.0, A.add, col(12), A.is_equal)
+    tt(r("DIFF"), r("TMP", 256, 392), r("TMP", 257, 393), A.subtract)
+    ts(r("RS17"), r("M17", 0, 136), 0.0, A.is_equal, 2.0 ** 26, A.mult)
+    ts(r("RESET"), r("MR"), 0.0, A.is_equal, 2.0 ** 26, A.mult)
+    ts(r("RM"), r("MR"), PR, A.is_equal)
+    ts(r("NRM"), r("MR"), PR, A.not_equal, 2.0 ** 25, A.mult)
+    for j in range(4):
+        ts(r("SEL", 128 * j, 128 * j + 128), r("BLKf"), oh(j), A.mult)
+    SELID, SELP, SELM, SELMP = [r("SEL", 128 * j, 128 * j + 128) for j in range(4)]
+    ts(r("BL64"), r("M17", 136, 272), PG, A.is_equal, 64.0, A.mult)
+    mset(r("QAM"), 0.0)
+    ts(r("SELT"), r("Q8"), oh(4), A.mult)
+    mset(r3s("PM", 0, 6, 0, 1), -2.0)
+    mset(col(14), 2047.5)
+    mset(col(15), -0.5)
+    mset(r("PFW", 128, 136), 4096.0)
+    ts(col(13), PG, 8.0 - S_IND, A.is_ge, 128.0, A.mult)
+    LBC, LCOL = r("L16", 8, 16), r("L16", 16, 32)
+    cp(LBC, r("JF", 16, 136, 17))
+    cp(LCOL, r("JF", 0, 16))
+    aL, cL, mpL, hL, wL, dL, kL = r("L16", 32, 48), r("L16", 48, 64), 64, 80, r("L16", 96, 112), r("L16", 112, 128), 128
+    bL, LPR, aS = wL, r("L16", 152, 155), r("L16", 160, 176)
+
+    def start_mates():
+        cp(r("P16", 0, 256), r("IB", 0, 256))
+        ts(r("P16", 256, 384), mf, -2048.0, A.add)
+        iota(r("AV"), [[1, 16], [128, 16]])
+        dma("y", T.MT[2:128:16, 0:2048], mf[0], [mf], [r("MT", 0, 2048)], 2500)
+        for j in range(8):
+            ts(ind(r("MT", 2048, 4096), r("P16", 256 + 16 * j, 272 + 16 * j)), r("AV"), 1.0, A.mult, 16.0 * j, A.add)
+        dma("y", T.ST[2:128:16, 2048:4096], T.MT[2:128:16, 2048:4096], [r("MT", 2048, 4096)], [r("ST", 2048, 4096, row=2)], 2500)
+        for j in range(8):
+            act(r("MPP", 512 * j, 512 * j + 512), ind(r("MT"), r("P16", 32 * j, 32 * j + 32)), F.Copy)
+        for j in range(16):
+            act(r("MPU", 256 * j, 256 * j + 256), r("MPP", j, 4096, 16), F.Copy)
+        dma("y", T.ST[3:128:16, 0:4096], T.MPU[2:128:16, 0:4096], [r("MPU")], [r("ST", 0, 4096, row=3)], 2500)
+
+    def late_constants():
+        iota(r("K1", 0, 2176), [[0, 2176]], 5)
+        for o in (r("K1", 2176, WD), r("K2", 0, 2176), r("K2", 2176, WD)):
+            dma("y", o[0], T.K1[:, 0:2176], [r("K1", 0, 2176)], [o], 4000)
+        ts(r("NRB"), r("NRM"), -BIG, A.add)
+        ts(LPR, r("JF", 0, 3), 0.0, A.mult, PR, A.add)
+        ts(r("SELLO"), r("BLKb"), oh(5), A.mult)
+        mset(r3s("SBQ", 0, RO, 0, 96), -1.0)
+        mset(r("SG", 0, 96), 0.0)
+        ts(r("COL", 32, 44), r("COL", 16, 28), -2.0, A.mult, 1.0, A.add)
+        mset(r("BITS", 0, 1), 1.0)
+        for k in range(12):
+            ts(r("BITS", 1 << k, 2 << k), r("BITS", 0, 1 << k), col(32 + k), A.mult)
+        tt(col(44), oh(12), oh(13), A.add)
+        ts(col(45), col(44), 256.0, A.mult, oh(14), A.add)
+        ts(col(46), oh(15), TAG, A.mult, col(45), A.add)
+        ts(r("KSEL"), r("BLKb"), col(46), A.mult)
+        ts(col(47), PR, 12.0, A.is_lt, -B20 / 2, A.mult)
+        tt(col(48), col(47), col(45), A.add)
+        ts(r("PI", 3, 4), r("PI", 2, 3), 1, A.bitwise_and)
+        tt(col(50), col(48), r("PI", 3, 4), A.mult)
+        tt(col(49), col(48), col(50), A.subtract)
+        ts(r("TMP", 0, 128), r("MR", 0, 128), 4.0, A.is_equal, col(44), A.mult)
+        tt(r("DM"), r("TMP", 0, 128), r("BLKf"), A.mult)
+        tt(col(51), oh(0), oh(2), A.add)
+        tt(col(52), oh(1), oh(3), A.add)
+        ts(r("KEEP"), DJ, 0.0, A.is_equal, col(51), A.mult)
+        ts(r("SHIFT"), DJ, 1.0, A.is_equal, col(51), A.mult)
+        ts(r("TMP", 128, 256), DJ, -1.0, A.is_ge, col(52), A.mult)
+        tt(r("PO"), r("TMP", 128, 256), r("TRIx"), A.is_gt)
+        ts(r("MSW", 0, 128), DJ, 2.0, A.is_equal, oh(0), A.mult)
+        ts(r("MSW", 128, 256), DJ, 3.0, A.is_equal, oh(0), A.mult)
+        tt(r("TMP", 256, 384), r("KEEP"), r("SHIFT"), A.add)
+        ts(r("MSW", 256, 384), r("TMP", 256, 384), oh(2), A.mult)
+        ts(col(53), oh(4), 4096.0, A.mult)
+        tt(col(54), col(7), oh(5), A.add)
+        ts(col(55), oh(2), -1.0, A.mult, 1.0, A.add)
+        ts(col(56), oh(3), -1.0, A.mult, 1.0, A.add)
+        tt(col(57), col(55), oh(3), A.subtract)
+        ts(r("TMP", 384, 512), DJ, 0.0, A.is_lt, 128.0, A.mult)
+        tt(r("TMP", 0, 128), r("TMP", 384, 512), DJ, A.add)
+        for d in range(1, NR):
+            ts(r("ROT", 128 * d - 128, 128 * d), r("TMP", 0, 128), 16.0 * d, A.is_equal)
+        ts(r("UP"), r("IDb"), col(8), A.mult)
+        ts(r("nUP"), r("UP"), -1.0, A.mult)
+        tt(r("LOW"), r("IDb"), r("UP"), A.subtract)
+        mset(r("X2"), 1.0)
+        ts(sm(64), r("MG", 0, 128, 8), 0.0, A.mult, PF, A.add)
+        ts(sm(72, 8), sm(72, 8), 128.0, A.add)
+        cp(r("X2", 14, 256, 16), sm(64))
+        ts(sm(768), sm(64), 4096.0, A.add)
+        ts(sm(64), sm(64), -6 * B20, A.add)
+        ts(sm(80), LW, -3840.0, A.add)
+        ts(sm(96), LW, -3841.0, A.add)
+        ts(sm(112, 6), sm(0, 6), -4096.0, A.add)
+        ts(r("PI", 4, 5), r("PI", 0, 1), 1, A.bitwise_and)
+        ts(col(58), r("PI", 4, 5), -1.0, A.mult, 1.0, A.add)
+        ts(sm(118, 6), sm(112, 6), col(58), A.add)
+        ts(sm(124, 6), sm(112, 6), col(58), A.add)
+        for j in range(3):
+            cp(sm(130 + 6 * j, 6), sm(0, 6))
+        iota(r("KR", 0, 96), [[2, 48], [0, 2]], 1)
+
+    def r2w(b, lo, items, out, off="NRM"):
+        o = lo
+        for sel, src in items:
+            n = src[5]
+            mm([(ps(b, o, o + n), r("IDb"), r(off, 0, n), True, False)])
+            mm([(ps(b, o, o + n), sel, src, False, True)], acc=True)
+            o += n
+        scan(out, r("RESET", 0, o - lo), ps(b, lo, o), A.add, A.min)
+
+    def t2w(b, lo, win, lst, xe, mask=None, plus=None):
+        n = 16 * lst[5]
+        tt(r("XE", xe, xe + n), ind(win, lst), mask or r("RM", 0, n), A.mult)
+        if plus:
+            mm([(ps(b, lo, lo + n // 16), r("IDf"), plus, True, False)])
+        mm([(ps(b, lo + 8 * h, lo + 8 * h + 8), r("XE", xe + 128 * h, xe + 128 * h + 128), r("Q8"),
+             not plus, not plus or h == n // 128 - 1) for h in range(n // 128)], acc=bool(plus))
+
+    live, af = sm(160), sm(176)
+
+    def lanes(t):
+        s = (STEP * t) & 2047
+        cuts = sorted({0, 1024, 2048 - s, 2048})
+        for x, z in zip(cuts, cuts[1:]):
+            if t:
+                act(r("FL", x, z), r("ST", (x + s) & 2047, ((x + s) & 2047) + z - x), F.Copy)
+        for x in range(2):
+            mm([(ps(0, 64 * x, 64 * x + 64), r("B5", 15 - j, 143 - j), r("FL", 1024 * x + j, 1024 * x + 1024, 16), j == 0, j == 15)
+                for j in range(16)])
+        act(r("FW"), ps(0, 0, 128), F.Copy)
+        mm([(ps(1, 0, 128), r("FW"), r("BLKb"), True, True)])
+        act(r("CTX"), ps(1, 0, 128), F.Copy)
+        mm([(ps(1, 128, 136), r("TRI"), r("CTX", 0, 128, 16), True, True)] +
+           [(ps(1, 136 + 8 * j, 144 + 8 * j), r("ONES", 0, 128), r("CTX", 0, 128, 16), True, True) for j in range(2)])
+        mm([(ps(0, 128, 256), r("TRIB"), r("FW"), True, False), (ps(0, 128, 256), r("CTX"), r("TRIx"), False, True)])
+        ts(sm(192, 8), ps(1, 128, 136), -1.0, A.mult, 0.5, A.add)
+        for k in range(8):
+            o = (T.IND[:, :, 16 * k:16 * k + 16], "IND", k, k + 1, None, 256)
+            if k < 8 - S_IND:
+                ts(o, JB3, ps(1, 128 + k, 129 + k), A.is_ge, 2.0, A.mult)
+            else:
+                act(o, JB3, F.Sign, bias=sm(192 + k, 1))
+        act(r("PFW", 0, 128), ps(0, 128, 256), F.Copy)
+        ts(col(59), col(13), s / 8.0, A.add)
+        ts(sm(272), ps(1, 136, 152), -6 * B20, A.add)
+        mm([(ps(2, q, q + 1), (T.IND[:, q, :], "IND", 0, 8, None, 128), r("ONES", 0, 1), True, True) for q in range(16)])
+        ts(bL, ps(2, 0, 16), col(13), A.add, 0.5, A.mult)
+        ts(sm(224), ps(2, 0, 16), col(59), A.add, 8.0, A.mult)
+        tt(r("IND2"), ind(r("PFW"), bL), r("JF"), A.is_le)
+        mm([(ps(2, 16, 32), r("B2", 15 - j, 143 - j), r("IND2", j, 256, 16), j == 0, j == 15) for j in range(16)])
+        tt(r("BD", 16, 32), sm(224), ps(2, 16, 32), A.add)
+        ts(r("PI", 8, 24), r("BD", 16, 32), 2047, A.bitwise_and)
+        cp(aL, r("PI", 8, 24))
+        ts(live, r("BD", 16, 32), 2048.0 + s, A.is_lt)
+        tt(sm(240), r("PI", 8, 24), LW, A.subtract)
+        tt(sm(448), sm(240), live, A.mult)
+        tt(af, sm(448), LW, A.add)
+        cp(aS, af)
+
+    stage = [0]
+
+    def hop(h, f):
+        lo, hi = 128 * f, 128 * f + 128
+        c = lambda name: r(name, lo, hi)
+        y, e, wm = (c("Y2"), 2 * h + f, "WM") if h else (c("QA"), f, "WX")
+        raw, ku, key, ee = ps(f, 0, 128), ps(f, 128, 256), ps(2 + f, 0, 136), ps(2 + f, 136, 272)
+        mm([(raw, r("CST"), r("ONES", 0, 128), True, False)])
+        mm([(raw, r(wm, 0, 128), y, False, False), (raw, r(wm, 256, 384), y, False, True),
+            (ku, r(wm, 128, 256), y, True, False), (ku, r(wm, 384, 512), y, False, True)], acc=True)
+        ts(c("T1"), raw, M4096, A.add, M4096, A.subtract)
+        tt(c("UM"), raw, c("T1"), A.subtract)
+        act(c("SQ"), c("UM"), F.Square, bias=col(14))
+        ts(c("FLI"), c("SQ"), -12.0, A.add, 1.0 / 32, A.mult)
+        tt(c("SI"), c("FLI"), ku, A.add)
+        ts(c("CI"), c("SI"), 4095, A.bitwise_and)
+        cp(c("C16"), c("CI"))
+        cp(c("CF"), c("CI"))
+        tt(c("EQ"), c("CI"), ps(6, lo, hi), A.is_equal)
+        mm([(ee, c("CF"), r("DIFF"), True, True)])
+        mm([(key, c("EQ"), r("I65"), True, False), (key, r("IDb"), r("MRH", 136 * h, 136 * h + 136), False, False),
+            (key, c("QAM"), r("BL64"), False, False)])
+        x0 = 2048 * f
+        for j in range(4):
+            a, b = x0 + 512 * j, x0 + 512 * j + 512
+            got = ind(r("Q"), r("C16", lo + 32 * j, lo + 32 * j + 32))
+            if j < NS[f]:
+                bank = ps((4, 5, 7)[stage[0] % 3])
+                stage[0] += 1
+                act(r("XG", a, b), got, F.Copy)
+                mm([(bank, r("nIDb"), r("AREP", a, b), True, False)])
+                mm([(bank, r("IDb"), r("XG", a, b), False, True)], acc=True)
+                act(r("AB", a, b), bank, F.Relu)
+            else:
+                tt(r("XG", a, b), got, r("AREP", a, b), A.subtract)
+                if j < NS[f] + SR[f]:
+                    act(r("AB", a, b), r("XG", a, b), F.Relu)
+                else:
+                    ts(r("AB", a, b), r("XG", a, b), 0.0, A.max)
+        for src, bo in (("XG", r("BO", 8, 16)), ("AB", r("BO", 0, 8))):
+            mm([(ps(2 + f, i, 136, 17), r(src, x0 + i, x0 + 2048, 16), bo, False, i == 15 and src == "AB") for i in range(16)], acc=True)
+        stp = r("STP", 136 * f, 136 * f + 136)
+        scan(r3("PM", e, 1, 137), r("RS17"), key, A.add, A.min)
+        tt(stp, r3("PM", e, 1, 137), r3("PM", e, 0, 136), A.is_equal)
+        scan(r3("CS", e), ee, stp, A.add, A.mult)
+        if h + 1 < HO:
+            t2w(f, 256, r3("CS", e), LBC, lo)
+            l1, l2 = r("L16", hL + 8 * f, hL + 8 * f + 8), r("L16", mpL + 8 * f, mpL + 8 * f + 8)
+            cp(l1, ps(f, 256, 264))
+            act(c("GM"), ind(r("ST"), l1), F.Copy)
+            r2w(f, 272, [(SELMP, c("GM"))], c("SC"))
+            cp(l2, r("SC", lo + 15, hi, 16))
+            tt(c("YS"), ind(r("Q"), l2), c("A2"), A.add)
+            ts(c("Y2"), c("YS"), M2, A.add, M2, A.subtract)
+
+    def best(h, bk, bc, ok, oc):
+        for f in range(2):
+            k, c = r3s("PM", 2 * h + f, 2 * h + f + 1, 17, 137, 17), r3s("CS", 2 * h + f, 2 * h + f + 1, 16, 136, 17)
+            k = (T.PM[:, 2 * h + f, 17:137:17],) + k[1:]
+            c = (T.CS[:, 2 * h + f, 16:136:17],) + c[1:]
+            o = 8 * f
+            if bk is None:
+                cp(sm(ok + o, 8), k)
+                cp(sm(oc + o, 8), c)
+                continue
+            tt(sm(368 + o, 8), k, sm(bk + o, 8), A.is_lt)
+            tt(sm(384 + o, 8), c, sm(bc + o, 8), A.subtract)
+            tt(sm(ok + o, 8), k, sm(bk + o, 8), A.min)
+        if bk is not None:
+            tt(sm(400), sm(384), sm(368), A.mult)
+            tt(sm(oc), sm(400), sm(bc), A.add)
+
+    def swap(o, m, src, first=True):
+        b, lo = o
+        return [(ps(b, lo, lo + 96, 2), m, src(1), first, first), (ps(b, lo + 1, lo + 96, 2), m, src(0), first, True)]
+
+    later = [None]
+    lanes(0)
+    for t in range(RO):
+        last = t == RO - 1
+        act(r("QA"), ind(r("Q"), aL), F.Copy)
+        act(r("GSA"), ind(r("ST"), aL), F.Copy)
+        mm([(ps(7, 0, 256), r("XP"), r("QA"), True, True)])
+        mm([(ps(6, 0, 256), SELID, r("GSA"), True, True)])
+        act(r("AX_"), ps(7, 0, 256), F.Copy)
+        act(r("A2"), ps(7, 0, 256), F.Identity, bias=col(15))
+        for f in (1, 0):
+            act(r("QAM", 128 * f, 128 * f + 32 * NS[f]), r("QA", 128 * f, 128 * f + 32 * NS[f]), F.Copy)
+        for i in range(16):
+            cp((T.AREP[:, i:4096:16], "AREP", 0, 4096, i, 256), r("AX_"))
+        if t:
+            later[0]()
+        else:
+            start_mates()
+        for h in range(HO):
+            for f in (1, 0):
+                bonus[0] = SKEW * f
+                hop(h, f)
+            bonus[0] = 0.0
+            if t == 0 and h == 0:
+                late_constants()
+            best(h, None if h == 0 else 288 + 16 * (h % 2), 416 + 16 * (h % 2), 304 - 16 * (h % 2), 432 - 16 * (h % 2))
+        bk, bc, bd = sm(304), sm(432), r("BD", 0, 16)
+        tt(sm(352), sm(272), sm(64), A.is_le)
+        ts(sm(320), sm(352), 8192.0, A.mult)
+        t2w(0, 0, bc, LCOL, 0)
+        cp(cL, ps(0, 0, 16))
+        tt(sm(464), ps(0, 0, 16), LW, A.subtract)
+        act(r("GSC"), ind(r("ST"), cL), F.Copy)
+        act(r("GB"), ind(r("BITS"), cL), F.Copy)
+        act(r("QC"), ind(r("Q"), cL), F.Copy)
+        ts(bd, bk, -31.5, A.add, 1.0 / 64, A.mult)
+        ts(sm(512), bd, -4096.0, A.add)
+        ts(sm(784), sm(512), M64, A.add, M64, A.subtract)
+        tt(sm(800), sm(512), sm(784), A.subtract)
+        tt(sm(816), bd, sm(320), A.add)
+        tt(sm(336), bc, sm(768), A.subtract)
+        mset(r("X2", 15, 256, 16), float(RO - 1 - t))
+        mm([(ps(1, 8 * f, 8 * f + 8), r("GSC", 128 * f, 128 * f + 128), r("SELT"), True, True) for f in range(2)])
+        prop, dq, kb, kv = sm(544), sm(560), sm(592), sm(624)
+        tt(prop, sm(816), ps(1, 0, 16), A.is_lt)
+        tt(r("X2", 12, 256, 16), sm(784), prop, A.mult)
+        tt(r("X2", 13, 256, 16), sm(800), prop, A.mult)
+        tt(dq, sm(512), prop, A.mult)
+        mm([(ps(4, 128 * f, 128 * f + 128), r("X2", 128 * f, 128 * f + 128), r("IDb"), True, True) for f in range(2)])
+        ts(sm(576), dq, 256.0, A.mult)
+        tt(kb, sm(576), sm(64), A.add)
+        ts(r("U1", 0, 256), r("GB"), col(49), A.mult)
+        ts(r("U1", 256, 512), r("GB"), col(50), A.mult)
+        tt(r("U2"), r("GB"), ps(4, 0, 256), A.mult)
+        ts(sm(608), kb, 6 * B20 + (RO - 1 - t) * TAG - BIG, A.add)
+        tt(kv, sm(608), prop, A.mult)
+        tt(sm(528), sm(336), prop, A.mult)
+        tt(r("RP", 0, 256), ind(sm(528), LCOL), r("RM"), A.mult)
+        tt(r("RP", 256, 512), ind(kv, LCOL), r("RM"), A.mult)
+        nv = ns = 0
+        order = sorted(range(16), key=lambda j: (j * 16 // (16 - V_PAIR)) if j < 16 - V_PAIR else (j - 16 + V_PAIR) * 16 // V_PAIR + 2)
+        for j in order:
+            f, k = divmod(j, 8)
+            p = slice(32 * (k // 2), 32 * (k // 2) + 32)
+            u0 = 256 * (k % 2) + 128 * f
+            if j >= 16 - V_PAIR:
+                b, nv = 2 + nv % 2, nv + 1
+            else:
+                b, ns = ns % 2, ns + 1
+            mm([(ps(b, 256, 512), r("U1", u0, u0 + 128, p=p), r("U2", p=p), True, True)])
+            if j >= 16 - V_PAIR:
+                o, a = sm(640 + j, 1), ps(b, 256, 512)
+                add("v", [lambda o=o, a=a: g.vector.tensor_reduce(o[0], a[0], AX.X, A.min)], [a], [o], 280)
+            else:
+                act(r("JUNK", 256 * b, 256 * b + 256), ps(b, 256, 512), F.Relu, bias=sm(592 + j, 1), scale=-1.0,
+                    accum=r("LS", j, j + 1))
+        cp(ind(r("K1"), aS), r("U2"))
+        act(r("GK"), ind(r("K1"), cL), F.Copy)
+        r2w(4, 256, [(r("KSEL"), r("GK"))], r("SC", 0, 256), "NRB")
+        r2w(7, 0, [(SELP, r("GSC"))], r("SC", 256, 512))
+        tt(sm(480), r("SC", 271, 512, 16), LW, A.subtract)
+        tt(r("LS", 16 - V_PAIR, 16), sm(608 - V_PAIR, V_PAIR), sm(656 - V_PAIR, V_PAIR), A.subtract)
+        ts(sm(656), r("LS"), 0.0, A.is_equal)
+        t2w(2, 0, sm(656), LCOL, 0, r("RP", 0, 256), LW)
+        cp(wL, ps(2, 0, 16))
+        cp(ind(r("K2"), wL), r("U2"))
+        t2w(3, 0, sm(656), LCOL, 256, r("RP", 256, 512))
+        act(r("GK"), ind(r("K2"), aL), F.Copy)
+        r2w(4, 0, [(r("KSEL"), r("GK"))], r("SC", 512, 768), "NRB")
+        tt(sm(704), ps(3, 0, 16), r("SC", 15, 256, 16), A.is_lt)
+        tt(sm(720), ps(3, 0, 16), r("SC", 527, 768, 16), A.is_lt)
+        stand = r("TMP", 0, 16)
+        tt(stand, sm(704), sm(720), A.mult)
+        tt(r("TMP", 48, 96), ind(stand, LPR), sm(448, 48), A.mult)
+        tt(r("TMP", 96, 144), r("TMP", 48, 96), sm(0, 48), A.add)
+        cp(r("P16", 0, 48), r("TMP", 96, 144))
+        jA, jC, jO = r("P16", 0, 16), r("P16", 16, 32), r("P16", 32, 48)
+        tt(sm(752), live, stand, A.subtract)
+        mm([(ps(6, 256, 512), r("PO"), r("GSC"), True, True)])
+        act(r("YS"), ps(6, 256, 512), F.Identity, bias=col(54))
+        for j, (x, z) in enumerate((("GSC", "GSA"), ("GSA", "GSC"))):
+            o = ps(5, 256 * j, 256 * j + 256)
+            mm([(o, r("KEEP"), r(x), True, False)])
+            mm([(o, r("SHIFT"), r(z), False, False)], acc=True)
+            mm([(o, r("DM"), r("U2"), False, True)], acc=True)
+        act(r("VV"), ps(5), F.Identity, bias=col(53))
+        mm([(ps(7, 0, 256), r("XP"), r("QC"), True, False), (ps(7, 0, 256), r("nIDb"), r("QA"), False, True)])
+        mm([(ps(7, 256, 512), r("XP"), r("QA"), True, False), (ps(7, 256, 512), r("nIDb"), r("QC"), False, True)])
+        act(r("SGN"), ps(7), F.Sign)
+        cp(ind(r("ST"), jO), r("YS"))
+        cp(ind(r("ST"), jC), r("VV", 0, 256))
+        act(r("GS2"), ind(r("ST"), aL), F.Copy)
+        cp(ind(r("ST"), jA), r("VV", 256, 512))
+        if last:
+            dma("y", T.yp[:], T.ST[1:128:16, 0:4096], [r("ST", 0, 4096, row=1)], [], 2500)
+        r2w(7, 0, [(r("SELLO"), r("GS2"))], r("SC", 0, 256))
+        tt(r("RF"), r("SC", 15, 256, 16), sm(752), A.mult)
+        mm([(ps(7, 256, 272), r("BLKb"), r("RF"), True, True), (ps(7, 272, 288), r("TMB"), r("RF"), True, True)])
+        cc = sm(288)
+        scan(cc, r("ONES", 0, 16), ps(7, 256, 272), A.mult, A.add)
+        tt(sm(336), r("RF"), sm(80), A.mult)
+        tt(sm(352), sm(96), sm(336), A.subtract)
+        tt(sm(368), ps(7, 272, 288), sm(352), A.add)
+        tt(sm(384), sm(368), cc, A.add)
+        cp(dL, sm(384))
+        cp(ind(r3("SBQ", t), dL), r("QA"))
+        tr = []
+        for d in range(1, NR):
+            dst = T.cores[(rank + d) % NR]
+            rid, pid = topo.addr(dst)[:2]
+            mask = sum(1 << e for e in topo.engines(core, dst)[4 * (d - 1):4 * d])
+            tr.append(RemoteDMATransfer(dst_ids=[DstId(rid=rid, pnc=pid)], dma_engine_mask=mask, remote_sem=T.sem["arr%d" % t],
+                                        src=T.SBQ[:, t, 32 * (d - 1):32 * d], dst=T.LAND[:, t, 32 * (d - 1):32 * d]))
+        add("g", [lambda tr=tr: g.remote_dma_fused(tr, local_sem=T.sem.sent)], [r3("SBQ", t, 0, 96)], [r3("LAND", t)], 300.0,
+            sem="arr%d" % t, val=4 * (NR - 1), lat=2500.0, remote=True)
+        cp(ind(r("SG"), dL), r("GSA"))
+        tt(ind(r("Q"), jA), r("SGN", 0, 256), r("QA"), A.add)
+        tt(ind(r("Q"), jC), r("SGN", 256, 512), r("QC"), A.add)
+        if not last:
+            lanes(t + 1)
+        n = sm(303, 1)
+        r2w(3, 0, [(SELID, r("SG", 0, 96)), (SELM, r("SG", 0, 96))], r("SC", 256, 448))
+        ts(sm(512, 18), sm(112, 18), n, A.is_lt)
+        ts(r("KR", 96, 192), r("KR", 0, 96), n, A.is_lt)
+        tt(sm(544, 12), r("SC", 271, 448, 16), sm(130, 12), A.subtract)
+        tt(sm(560, 6), sm(544, 6), sm(512, 6), A.mult)
+        tt(sm(566, 12), sm(544, 12), sm(518, 12), A.mult)
+        tt(sm(592, 18), sm(560, 18), sm(130, 18), A.add)
+        cp(r("L16", kL, kL + 18), sm(592, 18))
+        sL, vsL, vmL, pmL = [r("L16", kL + 6 * j, kL + 6 * j + 6) for j in range(4)]
+        act(r("QM", 0, 96), ind(r("Q"), vmL), F.Copy)
+        act(r("SGK"), r("SG", 0, 96), F.Copy, scale=col(57))
+        sg = lambda j: r("SG", j, 96, 2)
+        for j in range(3):
+            mm(swap((5, 96 * j), r("MSW", 128 * j, 128 * j + 128), sg))
+        act(r("SW"), ps(5, 0, 288), F.Copy)
+        mm([(ps(4, 0, 96), r("LOW"), r("QM", 0, 96), True, False)] + swap((4, 0), r("UP"), lambda j: r("QM", j, 96, 2), False))
+        act(r("QM", 96, 192), ps(4, 0, 96), F.Copy)
+        cp(ind(r("Q"), vmL), r("QM", 96, 192))
+        own = r3("SBQ", t, 0, 96)
+        mm([(ps(7, 32 * j, 32 * j + 32), r("ROT", 128 * j, 128 * j + 128), r3("LAND", t, 32 * j, 32 * j + 32), True, True)
+            for j in range(NR - 1)])
+        ts(r("TQ"), ps(7, 0, 96), 0.0, A.is_ge)
+        tt(r("TMP", 160, 256), ps(7, 0, 96), own, A.subtract)
+        tt(r("TMP", 256, 352), r("TMP", 160, 256), r("TQ"), A.mult)
+        tt(r("R5"), r("TMP", 256, 352), own, A.add)
+        mm([(ps(7, 128, 224), r("nUP"), r("R5"), True, False)] + swap((7, 128), r("UP"), lambda j: r("R5", j, 96, 2), False))
+        tt(r("TQ"), ps(7, 128, 224), r("KR", 96, 192), A.mult)
+        tt(ind(r("Q"), sL), r("TQ"), r("R5"), A.add)
+        if last:
+            dma("y", T.yq[:, 0:2048], T.Q[:, 0:2048], [r("Q", 0, 2048)], [], 4000)
+            dma("s", T.yq[:, 2048:4096], T.Q[:, 2048:4096], [r("Q", 2048, 4096)], [], 4000)
+        tt(ind(r("ST"), vsL), r("SGK"), r("SW", 192, 288), A.add)
+        if last:
+            dma("y", T.ym[:], T.ST[2:128:16, 0:2048], [r("ST", 0, 2048, row=2)], [], 2500)
+        else:
+            def mend(vmL=vmL, pmL=pmL):
+                gm, gp = r("GMM", 0, 96), r("GMM", 96, 192)
+                act(gm, ind(r("ST"), vmL), F.Copy, scale=col(55))
+                tt(ind(r("ST"), vmL), gm, r("SW", 0, 96), A.add)
+                r2w(3, 256, [(SELP, gm)], r("SC", 512, 608))
+                tt(sm(624, 6), r("SC", 527, 608, 16), sm(130, 6), A.subtract)
+                tt(sm(632, 6), sm(624, 6), sm(518, 6), A.mult)
+                tt(sm(640, 6), sm(632, 6), sm(130, 6), A.add)
+                cp(pmL, sm(640, 6))
+                act(gp, ind(r("ST"), pmL), F.Copy, scale=col(56))
+                tt(ind(r("ST"), pmL), gp, r("SW", 96, 192), A.add)
+            later[0] = mend
+    return ops
+
+
+def depend(ops):
+    hist = {}
+    for i, o in enumerate(ops):
+        deps = {}
+        for kind, xs in (("r", o["reads"]), ("w", o["writes"])):
+            for x in xs:
+                name, lo, hi, row = x[1:5]
+                bank = name[:2] == "ps"
+                if bank:
+                    lo, hi = 0, 512
+                keep = []
+                for e in hist.get(name, []):
+                    j, k2, l2, h2, r2 = e
+                    meet = l2 < hi and lo < h2 and (row is None or r2 is None or row == r2)
+                    if meet and j != i:
+                        same = ops[j]["eng"] == o["eng"]
+                        if kind == "w" or k2 == "w" or (bank and not same):
+                            hard = not (bank and same and o["acc"])
+                            deps[j] = deps.get(j, False) or hard
+                    whole = x[5] >= hi - lo or bank
+                    if kind == "w" and whole and meet and lo <= l2 and h2 <= hi and (row is None or row == r2):
+                        continue
+                    keep.append(e)
+                keep.append((i, kind, lo, hi, row))
+                hist[name] = keep
+        o["deps"] = deps
+
+
+def schedule(ops):
+    n = len(ops)
+    succ = [[] for _ in ops]
+    for i, o in enumerate(ops):
+        for j in o["deps"]:
+            succ[j].append(i)
+
+    def gap(j, i):
+        if not ops[i]["deps"][j]:
+            return 0.0
+        return ops[j]["lat"] + (SAME if ops[j]["eng"] == ops[i]["eng"] else CROSS)
+    prio = [0.0] * n
+    for i in range(n - 1, -1, -1):
+        prio[i] = ops[i]["cost"] + max([ops[i]["lat"]] + [gap(i, s) + prio[s] for s in succ[i]])
+    left = [len(o["deps"]) for o in ops]
+    rdy = {i: 0.0 for i in range(n) if not left[i]}
+    free = {e: 0.0 for e in "vstgy"}
+    end = [0.0] * n
+    order = []
+    while rdy:
+        est = {i: max(rdy[i], free[ops[i]["eng"]]) for i in rdy}
+        first = min(est, key=lambda i: (est[i], -prio[i]))
+        e = ops[first]["eng"]
+        cand = [i for i in rdy if ops[i]["eng"] == e and est[i] <= est[first] + min(LOOK, 0.7 * ops[first]["cost"])]
+        i = max(cand, key=lambda i: prio[i] + ops[i]["bonus"])
+        end[i] = est[i] + ops[i]["cost"]
+        ops[i]["t0"] = est[i]
+        free[e] = end[i]
+        del rdy[i]
+        order.append(i)
+        for s in succ[i]:
+            left[s] -= 1
+            if not left[s]:
+                rdy[s] = max(end[j] + gap(j, s) for j in ops[s]["deps"])
+    return order
+
+
+def rank_program(g, core, T, topo):
+    if T.rank_of(core) is None:
+        return
+    ops = build(g, T, topo, core)
+    depend(ops)
+    order = schedule(ops)
+    queue = {"v": g.vector, "s": g.scalar, "t": g.tensor, "g": g, "y": g.sync}
+    count = {e: 0 for e in "vstg"}
+    seen = {e: {} for e in queue}
+    total = {}
+    for i in order:
+        o = ops[i]
+        q, need = queue[o["eng"]], {}
+        for j, hard in o["deps"].items():
+            if hard:
+                s, v = ops[j]["done"]
+                need[s] = max(need.get(s, 0), v)
+        for s, v in need.items():
+            if seen[o["eng"]].get(s, 0) < v:
+                q.wait_ge(T.sem[s], v)
+                seen[o["eng"]][s] = v
+        for fn in o["fns"]:
+            ins = fn()
+        if o["sem"] is None:
+            count[o["eng"]] += 1
+            o["done"] = ("e" + o["eng"], count[o["eng"]])
+            ins.then_inc(T.sem[o["done"][0]], 1)
+        else:
+            o["done"] = (o["sem"], o["val"])
+            if not o.get("remote"):
+                ins.then_inc(T.sem[o["sem"]], 16)
+        total[o["done"][0]] = o["done"][1]
+    total["sent"] = RO * 4 * (NR - 1)
+    for s, v in total.items():
+        g.wait_ge(T.sem[s], v)

@@ -6,8 +6,9 @@ WD = 4352
 NS = (2, 2)
 SR = (1, 1)
 S_IND = 4
+A_S = 4
 V_PAIR = 7
-LOOK, SKEW, SAME, CROSS, PE = 400.0, 0.0, 60.0, 120.0, 0.5
+LOOK, SKEW, SAME, CROSS, PE = 150.0, 800.0, 60.0, 120.0, 0.5
 B20 = float(1 << 20)
 TAG = float(1 << 21)
 BIG = 12582912.0
@@ -24,15 +25,15 @@ def _decl(dt_, spec):
         SCRATCH[name] = ("sbuf", [128] + [int(x) for x in n.split("x")], dt_)
 
 
-_decl("bfloat16", "Q:4352 K1:4352 K2:4352 BITS:4096 FL:2048 XG:4096 AB:4096 AREP:4096 SBQ:5x768 LAND:5x96 "
-      "WX:512 NRB:256 QAM:256 GS2:256 LOB:256 BL64:136 SELLO:128 "
-      "IDb:128 nIDb:128 I65:136 BLKb:128 XP:128 BO:24 MRH:408 NRM:256 KSEL:128 DM:128 ROT:384 "
+_decl("bfloat16", "Q:4352 K1:4352 GA:256 BITS:4096 FL:2048 XG:4096 AB:4096 AREP:4096 SBQ:5x768 LAND:5x96 "
+      "WX:512 NRB:256 QAM:256 GS2:256 LOB:256 BL64:144 SELLO:128 "
+      "IDb:128 nIDb:128 I65:144 BLKb:128 XP:128 BO:24 MRH:432 NRM:256 KSEL:128 DM:128 ROT:384 "
       "UP:128 nUP:128 LOW:128 TRI:128 TRIx:128 TRIB:128 TMB:128 B2:144 B5:144 WM:512 CST:128 ONES:256 "
-      "X2:256 QA:256 QC:256 AX_:256 Y2:256 EQ:256 GB:256 U1:512 U2:256 GK:256 SGN:512 JUNK:512 FW:128 CTX:128 "
+      "X2:256 QA:256 QC:256 AX_:256 Y2:256 EQ:256 GB:256 U1:1024 U2:256 GK:256 SGN:512 JUNK:1024 FW:128 CTX:128 "
       "IND:16x128 JB3:16x16 IND2:256 RF:16 R5:96 TQ:96 QM:192")
-_decl("float32", "ST:4352 MT:4096 MPP:4096 MPU:4096 AV:256 JF:256 MR:256 MG:256 DJ:128 COL:64 IDf:128 BLKf:128 DIFF:136 "
-      "M17:272 RS17:136 RESET:256 RM:256 Q8:8 SEL:512 SELT:8 KEEP:128 SHIFT:128 PO:128 MSW:384 TMP:512 BLD:1152 "
-      "A2:256 GSA:256 GSC:256 RP:512 T1:256 UM:256 SQ:256 CF:256 PM:6x144 STP:272 CS:6x136 XE:512 GM:256 "
+_decl("float32", "ST:4352 MT:4096 MPP:4096 AV:256 JF:256 MR:256 MG:256 DJ:128 COL:64 IDf:128 BLKf:128 DIFF:144 "
+      "M18:288 RS18:144 RESET:256 RM:256 Q8:8 SEL:512 SELT:8 KEEP:128 SHIFT:128 PO:128 MSW:384 TMP:512 BLD:1152 "
+      "A2:256 GSA:256 GSC:256 RP:256 T1:256 UM:256 SQ:256 CF:256 PM:6x152 STP:288 CS:6x144 XE:512 GM:256 "
       "SC:768 YS:256 SM:832 LS:16 VV:512 SG:768 SGK:96 GMM:192 SW:288 PFW:136 KR:192")
 _decl("int32", "FLI:256 SI:256 CI:256 IB:400 BD:32 PI:32")
 _decl("uint16", "C16:256 L16:176 P16:384")
@@ -55,15 +56,15 @@ def build(g, T, topo, core):
             ps_ = slice(row, 128, 16)
         return (T[name][ps_, lo:hi:step], name, lo, hi, row, (hi - lo + step - 1) // step)
 
-    def r3(name, i, lo=0, hi=None):
+    def r3(name, i, lo=0, hi=None, step=1):
         w = T[name].shape[2]
         if hi is None:
             hi = w
-        return (T[name][:, i, lo:hi], name, i * w + lo, i * w + hi, None, hi - lo)
+        return (T[name][:, i, lo:hi:step], name, i * w + lo, i * w + hi, None, (hi - lo + step - 1) // step)
 
-    def r3s(name, i0, i1, lo, hi, step=1):
+    def r3s(name, i0, i1, lo, hi):
         w = T[name].shape[2]
-        return (T[name][:, i0:i1, lo:hi:step], name, i0 * w, i1 * w, None, (i1 - i0) * ((hi - lo + step - 1) // step))
+        return (T[name][:, i0:i1, lo:hi], name, i0 * w, i1 * w, None, (i1 - i0) * (hi - lo))
 
     def ind(win, off):
         return (win[0].indirect(off[0]), win, off, 16 * off[5])
@@ -188,8 +189,8 @@ def build(g, T, topo, core):
     iota(r("MG"), [[1, 16], [0, 16]])
     iota(r("DJ"), [[1, 128]], 0, -1)
     iota(JB3, [[1, 256]])
-    iota(r("M17", 0, 136), [[0, 8], [1, 17]])
-    iota(r("M17", 136, 272), [[1, 8], [0, 17]])
+    iota(r("M18", 0, 144), [[0, 8], [1, 18]], -1)
+    iota(r("M18", 144, 288), [[1, 8], [0, 18]])
     bonus[0] = 0.0
     mset(r("FL"), 0.0)
     mset(r("AB", 0, 1088), 0.0)
@@ -241,8 +242,9 @@ def build(g, T, topo, core):
     ts(col(9), col(8), -16.0, A.mult, 8.0, A.add)
     ts(r("XP"), DJ, col(9), A.is_equal)
     ts(r("nIDb"), r("IDb"), -1.0, A.mult)
-    tt(col(12), PF, PG, A.add)
-    ts(r("I65"), r("JF", 0, 136), col(12), A.is_equal, 262144.0, A.mult)
+    ts(col(60), PG, 2.0, A.mult, 1.0, A.add)
+    tt(col(12), PF, col(60), A.add)
+    ts(r("I65"), r("JF", 0, 144), col(12), A.is_equal, 262144.0, A.mult)
     ts(r("TMP", 0, 128), r("IDf"), col(6), A.mult)
     mm([(ps(7, 0, 128), r("BLKf"), r("TMP", 0, 128), True, True)])
     ts(r("SI", 0, 128), ps(7, 0, 128), col(5), A.mult, 2048.0, A.add)
@@ -260,20 +262,23 @@ def build(g, T, topo, core):
     for j, v in enumerate((128.0, -64.0)):
         ts(r("BO", 8 * j, 8 * j + 8), r("Q8"), v, A.mult)
     for h in range(HO):
-        ts(r("MRH", 136 * h, 136 * h + 136), r("M17", 0, 136), 16.0 * h, A.add)
+        ts(r("MRH", 144 * h, 144 * h + 144), r("M18", 0, 144), 16.0 * h, A.add)
         for k in range(1, 8, 2):
-            ts(r("MRH", 136 * h + 17 * k, 136 * h + 17 * k + 17), r("M17", 0, 17), 16.0 * h + 0.5, A.add)
-    mset(r("MRH", 16, 408, 17), TAG)
-    ts(r("TMP", 256, 393), r("JF", 0, 137), -1.0, A.add, col(12), A.is_equal)
-    tt(r("DIFF"), r("TMP", 256, 392), r("TMP", 257, 393), A.subtract)
-    ts(r("RS17"), r("M17", 0, 136), 0.0, A.is_equal, 2.0 ** 26, A.mult)
+            ts(r("MRH", 144 * h + 18 * k, 144 * h + 18 * k + 18), r("M18", 0, 18), 16.0 * h + 0.5, A.add)
+    mset(r("MRH", 17, 432, 18), TAG)
+    mset(r("MRH", 0, 288, 18), TAG)
+    mset(r("MRH", 288, 432, 18), 0.0)
+    ts(r("TMP", 256, 401), r("JF", 0, 145), -1.0, A.add, col(12), A.is_equal)
+    tt(r("DIFF"), r("TMP", 256, 400), r("TMP", 257, 401), A.subtract)
+    ts(r("RS18"), r("M18", 0, 144), -1.0, A.is_equal, 2.0 ** 26, A.mult)
     ts(r("RESET"), r("MR"), 0.0, A.is_equal, 2.0 ** 26, A.mult)
     ts(r("RM"), r("MR"), PR, A.is_equal)
     ts(r("NRM"), r("MR"), PR, A.not_equal, 2.0 ** 25, A.mult)
     for j in range(4):
         ts(r("SEL", 128 * j, 128 * j + 128), r("BLKf"), oh(j), A.mult)
     SELID, SELP, SELM, SELMP = [r("SEL", 128 * j, 128 * j + 128) for j in range(4)]
-    ts(r("BL64"), r("M17", 136, 272), PG, A.is_equal, 64.0, A.mult)
+    ts(r("BL64"), r("M18", 144, 288), PG, A.is_equal, 64.0, A.mult)
+    mset(r("BL64", 0, 144, 18), 0.0)
     mset(r("QAM"), 0.0)
     ts(r("SELT"), r("Q8"), oh(4), A.mult)
     mset(r3s("PM", 0, 6, 0, 1), -2.0)
@@ -282,13 +287,16 @@ def build(g, T, topo, core):
     mset(r("PFW", 128, 136), 4096.0)
     ts(col(13), PG, 8.0 - S_IND, A.is_ge, 128.0, A.mult)
     LBC, LCOL = r("L16", 8, 16), r("L16", 16, 32)
-    cp(LBC, r("JF", 16, 136, 17))
+    cp(LBC, r("JF", 17, 144, 18))
     cp(LCOL, r("JF", 0, 16))
-    aL, cL, mpL, hL, wL, dL, kL = r("L16", 32, 48), r("L16", 48, 64), 64, 80, r("L16", 96, 112), r("L16", 112, 128), 128
-    bL, LPR, aS = wL, r("L16", 152, 155), r("L16", 160, 176)
+    aL, cL, mpL, hL, bL, dL, kL = r("L16", 32, 48), r("L16", 48, 64), 64, 80, r("L16", 96, 112), r("L16", 112, 128), 128
+    LPR, aS = r("L16", 152, 155), r("L16", 160, 176)
 
     def start_mates():
-        cp(r("P16", 0, 256), r("IB", 0, 256))
+        ts(r("RP", 0, 144), r("B2"), oh(1), A.mult)
+        for j in range(16):
+            mm([(ps(5, 0, 256), r("RP", 15 - j, 143 - j), r("ST", j, 4096, 16), j == 0, j == 15)], acc=j > 0)
+        cp(r("P16", 0, 256), ps(5, 0, 256))
         ts(r("P16", 256, 384), mf, -2048.0, A.add)
         iota(r("AV"), [[1, 16], [128, 16]])
         dma("y", T.MT[2:128:16, 0:2048], mf[0], [mf], [r("MT", 0, 2048)], 2500)
@@ -297,14 +305,11 @@ def build(g, T, topo, core):
         dma("y", T.ST[2:128:16, 2048:4096], T.MT[2:128:16, 2048:4096], [r("MT", 2048, 4096)], [r("ST", 2048, 4096, row=2)], 2500)
         for j in range(8):
             act(r("MPP", 512 * j, 512 * j + 512), ind(r("MT"), r("P16", 32 * j, 32 * j + 32)), F.Copy)
-        for j in range(16):
-            act(r("MPU", 256 * j, 256 * j + 256), r("MPP", j, 4096, 16), F.Copy)
-        dma("y", T.ST[3:128:16, 0:4096], T.MPU[2:128:16, 0:4096], [r("MPU")], [r("ST", 0, 4096, row=3)], 2500)
+        dma("y", T.ST[3:128:16, 0:4096], T.MPP[2:128:16, 0:4096], [r("MPP")], [r("ST", 0, 4096, row=3)], 2500)
 
     def late_constants():
         iota(r("K1", 0, 2176), [[0, 2176]], 5)
-        for o in (r("K1", 2176, WD), r("K2", 0, 2176), r("K2", 2176, WD)):
-            dma("y", o[0], T.K1[:, 0:2176], [r("K1", 0, 2176)], [o], 4000)
+        dma("y", T.K1[:, 2176:WD], T.K1[:, 0:2176], [r("K1", 0, 2176)], [r("K1", 2176, WD)], 4000)
         ts(r("NRB"), r("NRM"), -BIG, A.add)
         ts(LPR, r("JF", 0, 3), 0.0, A.mult, PR, A.add)
         ts(r("SELLO"), r("BLKb"), oh(5), A.mult)
@@ -351,7 +356,6 @@ def build(g, T, topo, core):
         ts(sm(64), r("MG", 0, 128, 8), 0.0, A.mult, PF, A.add)
         ts(sm(72, 8), sm(72, 8), 128.0, A.add)
         cp(r("X2", 14, 256, 16), sm(64))
-        ts(sm(768), sm(64), 4096.0, A.add)
         ts(sm(64), sm(64), -6 * B20, A.add)
         ts(sm(80), LW, -3840.0, A.add)
         ts(sm(96), LW, -3841.0, A.add)
@@ -373,13 +377,11 @@ def build(g, T, topo, core):
             o += n
         scan(out, r("RESET", 0, o - lo), ps(b, lo, o), A.add, A.min)
 
-    def t2w(b, lo, win, lst, xe, mask=None, plus=None):
+    def t2w(b, lo, win, lst, xe, mask=None):
         n = 16 * lst[5]
         tt(r("XE", xe, xe + n), ind(win, lst), mask or r("RM", 0, n), A.mult)
-        if plus:
-            mm([(ps(b, lo, lo + n // 16), r("IDf"), plus, True, False)])
-        mm([(ps(b, lo + 8 * h, lo + 8 * h + 8), r("XE", xe + 128 * h, xe + 128 * h + 128), r("Q8"),
-             not plus, not plus or h == n // 128 - 1) for h in range(n // 128)], acc=bool(plus))
+        mm([(ps(b, lo + 8 * h, lo + 8 * h + 8), r("XE", xe + 128 * h, xe + 128 * h + 128), r("Q8"), True, True)
+            for h in range(n // 128)])
 
     live, af = sm(160), sm(176)
 
@@ -428,7 +430,8 @@ def build(g, T, topo, core):
         lo, hi = 128 * f, 128 * f + 128
         c = lambda name: r(name, lo, hi)
         y, e, wm = (c("Y2"), 2 * h + f, "WM") if h else (c("QA"), f, "WX")
-        raw, ku, key, ee = ps(f, 0, 128), ps(f, 128, 256), ps(2 + f, 0, 136), ps(2 + f, 136, 272)
+        raw, ku, key, ee = ps(f, 0, 128), ps(f, 128, 256), ps(2 + f, 0, 144), ps(2 + f, 144, 288)
+        end, o = h == HO - 1, 8 * f
         mm([(raw, r("CST"), r("ONES", 0, 128), True, False)])
         mm([(raw, r(wm, 0, 128), y, False, False), (raw, r(wm, 256, 384), y, False, True),
             (ku, r(wm, 128, 256), y, True, False), (ku, r(wm, 384, 512), y, False, True)], acc=True)
@@ -441,9 +444,11 @@ def build(g, T, topo, core):
         cp(c("C16"), c("CI"))
         cp(c("CF"), c("CI"))
         tt(c("EQ"), c("CI"), ps(6, lo, hi), A.is_equal)
-        mm([(ee, c("CF"), r("DIFF"), True, True)])
-        mm([(key, c("EQ"), r("I65"), True, False), (key, r("IDb"), r("MRH", 136 * h, 136 * h + 136), False, False),
-            (key, c("QAM"), r("BL64"), False, False)])
+        mm([(ee, c("CF"), r("DIFF"), True, not end)] +
+           ([(ps(2 + f, 145, 288, 18), r("IDf"), sm(416 + o, 8), False, True)] if end else []))
+        mm([(key, c("EQ"), r("I65"), True, False), (key, r("IDb"), r("MRH", 144 * h, 144 * h + 144), False, False),
+            (key, c("QAM"), r("BL64"), False, False)] +
+           ([(ps(2 + f, 0, 144, 18), r("IDf"), sm(288 + o, 8), False, False)] if end else []))
         x0 = 2048 * f
         for j in range(4):
             a, b = x0 + 512 * j, x0 + 512 * j + 512
@@ -462,37 +467,37 @@ def build(g, T, topo, core):
                 else:
                     ts(r("AB", a, b), r("XG", a, b), 0.0, A.max)
         for src, bo in (("XG", r("BO", 8, 16)), ("AB", r("BO", 0, 8))):
-            mm([(ps(2 + f, i, 136, 17), r(src, x0 + i, x0 + 2048, 16), bo, False, i == 15 and src == "AB") for i in range(16)], acc=True)
-        stp = r("STP", 136 * f, 136 * f + 136)
-        scan(r3("PM", e, 1, 137), r("RS17"), key, A.add, A.min)
-        tt(stp, r3("PM", e, 1, 137), r3("PM", e, 0, 136), A.is_equal)
+            mm([(ps(2 + f, i + 1, 144, 18), r(src, x0 + i, x0 + 2048, 16), bo, False, i == 15 and src == "AB") for i in range(16)], acc=True)
+        stp = r("STP", 144 * f, 144 * f + 144)
+        scan(r3("PM", e, 1, 145), r("RS18"), key, A.add, A.min)
+        tt(stp, r3("PM", e, 1, 145), r3("PM", e, 0, 144), A.is_equal)
         scan(r3("CS", e), ee, stp, A.add, A.mult)
-        if h + 1 < HO:
-            t2w(f, 256, r3("CS", e), LBC, lo)
-            l1, l2 = r("L16", hL + 8 * f, hL + 8 * f + 8), r("L16", mpL + 8 * f, mpL + 8 * f + 8)
+        t2w(f, 256, r3("CS", e), LBC, lo)
+        key_end = lambda e: r3("PM", e, 18, 145, 18)
+        c_end = lambda e: r3("CS", e, 17, 144, 18)
+        if h == 1:
+            tt(sm(368 + o, 8), key_end(e), key_end(f), A.is_lt)
+            tt(sm(384 + o, 8), c_end(e), c_end(f), A.subtract)
+            tt(sm(288 + o, 8), key_end(e), key_end(f), A.min)
+            tt(sm(400 + o, 8), sm(384 + o, 8), sm(368 + o, 8), A.mult)
+            tt(sm(416 + o, 8), sm(400 + o, 8), c_end(f), A.add)
+        if end:
+            cl = r("L16", 48 + o, 56 + o)
+            cp(cl, ps(f, 256, 264))
+            tt(sm(464 + o, 8), ps(f, 256, 264), sm(o, 8), A.subtract)
+            ts(r("BD", o, o + 8), key_end(e), -31.5, A.add, 1.0 / 64, A.mult)
+            act(c("GSC"), ind(r("ST"), cl), F.Copy)
+            mm([(ps(f, 272, 280), c("GSC"), r("SELT"), True, True)])
+            tt(sm(816 + o, 8), r("BD", o, o + 8), sm(320 + o, 8), A.add)
+            tt(sm(544 + o, 8), sm(816 + o, 8), ps(f, 272, 280), A.is_lt)
+        else:
+            l1, l2 = r("L16", hL + o, hL + o + 8), r("L16", mpL + o, mpL + o + 8)
             cp(l1, ps(f, 256, 264))
             act(c("GM"), ind(r("ST"), l1), F.Copy)
-            r2w(f, 272, [(SELMP, c("GM"))], c("SC"))
+            r2w(f, 0, [(SELMP, c("GM"))], c("SC"))
             cp(l2, r("SC", lo + 15, hi, 16))
             tt(c("YS"), ind(r("Q"), l2), c("A2"), A.add)
             ts(c("Y2"), c("YS"), M2, A.add, M2, A.subtract)
-
-    def best(h, bk, bc, ok, oc):
-        for f in range(2):
-            k, c = r3s("PM", 2 * h + f, 2 * h + f + 1, 17, 137, 17), r3s("CS", 2 * h + f, 2 * h + f + 1, 16, 136, 17)
-            k = (T.PM[:, 2 * h + f, 17:137:17],) + k[1:]
-            c = (T.CS[:, 2 * h + f, 16:136:17],) + c[1:]
-            o = 8 * f
-            if bk is None:
-                cp(sm(ok + o, 8), k)
-                cp(sm(oc + o, 8), c)
-                continue
-            tt(sm(368 + o, 8), k, sm(bk + o, 8), A.is_lt)
-            tt(sm(384 + o, 8), c, sm(bc + o, 8), A.subtract)
-            tt(sm(ok + o, 8), k, sm(bk + o, 8), A.min)
-        if bk is not None:
-            tt(sm(400), sm(384), sm(368), A.mult)
-            tt(sm(oc), sm(400), sm(bc), A.add)
 
     def swap(o, m, src, first=True):
         b, lo = o
@@ -511,7 +516,11 @@ def build(g, T, topo, core):
         for f in (1, 0):
             act(r("QAM", 128 * f, 128 * f + 32 * NS[f]), r("QA", 128 * f, 128 * f + 32 * NS[f]), F.Copy)
         for i in range(16):
-            cp((T.AREP[:, i:4096:16], "AREP", 0, 4096, i, 256), r("AX_"))
+            o = (T.AREP[:, i:4096:16], "AREP", 0, 4096, i, 256)
+            if i < A_S:
+                act(o, r("AX_"), F.Copy)
+            else:
+                cp(o, r("AX_"))
         if t:
             later[0]()
         else:
@@ -521,28 +530,22 @@ def build(g, T, topo, core):
                 bonus[0] = SKEW * f
                 hop(h, f)
             bonus[0] = 0.0
-            if t == 0 and h == 0:
-                late_constants()
-            best(h, None if h == 0 else 288 + 16 * (h % 2), 416 + 16 * (h % 2), 304 - 16 * (h % 2), 432 - 16 * (h % 2))
-        bk, bc, bd = sm(304), sm(432), r("BD", 0, 16)
-        tt(sm(352), sm(272), sm(64), A.is_le)
-        ts(sm(320), sm(352), 8192.0, A.mult)
-        t2w(0, 0, bc, LCOL, 0)
-        cp(cL, ps(0, 0, 16))
-        tt(sm(464), ps(0, 0, 16), LW, A.subtract)
-        act(r("GSC"), ind(r("ST"), cL), F.Copy)
+            if h == 0:
+                if t == 0:
+                    late_constants()
+                tt(sm(352), sm(272), sm(64), A.is_le)
+                ts(sm(320), sm(352), 8192.0, A.mult)
+                act(r("GA"), ind(r("BITS"), aL), F.Copy)
+                ts(r("U1", 512, 768), r("GA"), col(49), A.mult)
+                ts(r("U1", 768, 1024), r("GA"), col(50), A.mult)
+        bd = r("BD", 0, 16)
         act(r("GB"), ind(r("BITS"), cL), F.Copy)
         act(r("QC"), ind(r("Q"), cL), F.Copy)
-        ts(bd, bk, -31.5, A.add, 1.0 / 64, A.mult)
         ts(sm(512), bd, -4096.0, A.add)
         ts(sm(784), sm(512), M64, A.add, M64, A.subtract)
         tt(sm(800), sm(512), sm(784), A.subtract)
-        tt(sm(816), bd, sm(320), A.add)
-        tt(sm(336), bc, sm(768), A.subtract)
         mset(r("X2", 15, 256, 16), float(RO - 1 - t))
-        mm([(ps(1, 8 * f, 8 * f + 8), r("GSC", 128 * f, 128 * f + 128), r("SELT"), True, True) for f in range(2)])
         prop, dq, kb, kv = sm(544), sm(560), sm(592), sm(624)
-        tt(prop, sm(816), ps(1, 0, 16), A.is_lt)
         tt(r("X2", 12, 256, 16), sm(784), prop, A.mult)
         tt(r("X2", 13, 256, 16), sm(800), prop, A.mult)
         tt(dq, sm(512), prop, A.mult)
@@ -554,9 +557,7 @@ def build(g, T, topo, core):
         tt(r("U2"), r("GB"), ps(4, 0, 256), A.mult)
         ts(sm(608), kb, 6 * B20 + (RO - 1 - t) * TAG - BIG, A.add)
         tt(kv, sm(608), prop, A.mult)
-        tt(sm(528), sm(336), prop, A.mult)
-        tt(r("RP", 0, 256), ind(sm(528), LCOL), r("RM"), A.mult)
-        tt(r("RP", 256, 512), ind(kv, LCOL), r("RM"), A.mult)
+        tt(r("RP"), ind(kv, LCOL), r("RM"), A.mult)
         nv = ns = 0
         order = sorted(range(16), key=lambda j: (j * 16 // (16 - V_PAIR)) if j < 16 - V_PAIR else (j - 16 + V_PAIR) * 16 // V_PAIR + 2)
         for j in order:
@@ -567,13 +568,12 @@ def build(g, T, topo, core):
                 b, nv = 2 + nv % 2, nv + 1
             else:
                 b, ns = ns % 2, ns + 1
-            mm([(ps(b, 256, 512), r("U1", u0, u0 + 128, p=p), r("U2", p=p), True, True)])
+            mm([(ps(b, 256 * x, 256 * x + 256), r("U1", u0 + 512 * x, u0 + 512 * x + 128, p=p), r("U2", p=p), True, True) for x in range(2)])
             if j >= 16 - V_PAIR:
-                o, a = sm(640 + j, 1), ps(b, 256, 512)
-                add("v", [lambda o=o, a=a: g.vector.tensor_reduce(o[0], a[0], AX.X, A.min)], [a], [o], 280)
+                o, a = sm(640 + j, 1), ps(b)
+                add("v", [lambda o=o, a=a: g.vector.tensor_reduce(o[0], a[0], AX.X, A.min)], [a], [o], 536)
             else:
-                act(r("JUNK", 256 * b, 256 * b + 256), ps(b, 256, 512), F.Relu, bias=sm(592 + j, 1), scale=-1.0,
-                    accum=r("LS", j, j + 1))
+                act(r("JUNK", 512 * b, 512 * b + 512), ps(b), F.Relu, bias=sm(592 + j, 1), scale=-1.0, accum=r("LS", j, j + 1))
         cp(ind(r("K1"), aS), r("U2"))
         act(r("GK"), ind(r("K1"), cL), F.Copy)
         r2w(4, 256, [(r("KSEL"), r("GK"))], r("SC", 0, 256), "NRB")
@@ -581,16 +581,9 @@ def build(g, T, topo, core):
         tt(sm(480), r("SC", 271, 512, 16), LW, A.subtract)
         tt(r("LS", 16 - V_PAIR, 16), sm(608 - V_PAIR, V_PAIR), sm(656 - V_PAIR, V_PAIR), A.subtract)
         ts(sm(656), r("LS"), 0.0, A.is_equal)
-        t2w(2, 0, sm(656), LCOL, 0, r("RP", 0, 256), LW)
-        cp(wL, ps(2, 0, 16))
-        cp(ind(r("K2"), wL), r("U2"))
-        t2w(3, 0, sm(656), LCOL, 256, r("RP", 256, 512))
-        act(r("GK"), ind(r("K2"), aL), F.Copy)
-        r2w(4, 0, [(r("KSEL"), r("GK"))], r("SC", 512, 768), "NRB")
-        tt(sm(704), ps(3, 0, 16), r("SC", 15, 256, 16), A.is_lt)
-        tt(sm(720), ps(3, 0, 16), r("SC", 527, 768, 16), A.is_lt)
+        t2w(3, 0, sm(656), LCOL, 256, r("RP"))
         stand = r("TMP", 0, 16)
-        tt(stand, sm(704), sm(720), A.mult)
+        tt(stand, ps(3, 0, 16), r("SC", 15, 256, 16), A.is_lt)
         tt(r("TMP", 48, 96), ind(stand, LPR), sm(448, 48), A.mult)
         tt(r("TMP", 96, 144), r("TMP", 48, 96), sm(0, 48), A.add)
         cp(r("P16", 0, 48), r("TMP", 96, 144))

@@ -3,18 +3,18 @@ from concourse.mybir import AluOpType as A, AxisListType as AX, ActivationFuncti
 
 RO, HO, STEP, NR = 5, 3, 341, 4
 WD = 4352
-NS = (2, 2)
-SR = (1, 1)
-S_IND = 4
-A_S = 4
-V_PAIR = 7
+MODES = ("SVMS", "SVMS")
+PARTS = ((0, 3), (3, 4))
+S_IND = 3
+V_PAIR = (4, 3)
+A_S = 3
+FIRST = (0, 1)
 LOOK, SKEW, SAME, CROSS, PE = 150.0, 800.0, 60.0, 120.0, 0.5
-B20 = float(1 << 20)
 TAG = float(1 << 21)
-BIG = 12582912.0
+BETA = 1024.0
 M64 = 1.5 * 2.0 ** 29
 M4096 = 1.5 * 2.0 ** 35
-M2 = 1.5 * 2.0 ** 24
+KW = 19
 
 SCRATCH = {}
 
@@ -25,21 +25,21 @@ def _decl(dt_, spec):
         SCRATCH[name] = ("sbuf", [128] + [int(x) for x in n.split("x")], dt_)
 
 
-_decl("bfloat16", "Q:4352 K1:4352 GA:256 BITS:4096 FL:2048 XG:4096 AB:4096 AREP:4096 SBQ:5x768 LAND:5x96 "
-      "WX:512 NRB:256 QAM:256 GS2:256 LOB:256 BL64:144 SELLO:128 "
-      "IDb:128 nIDb:128 I65:144 BLKb:128 XP:128 BO:24 MRH:432 NRM:256 KSEL:128 DM:128 ROT:384 "
-      "UP:128 nUP:128 LOW:128 TRI:128 TRIx:128 TRIB:128 TMB:128 B2:144 B5:144 WM:512 CST:128 ONES:256 "
-      "X2:256 QA:256 QC:256 AX_:256 Y2:256 EQ:256 GB:256 U1:1024 U2:256 GK:256 SGN:512 JUNK:1024 FW:128 CTX:128 "
-      "IND:16x128 JB3:16x16 IND2:256 RF:16 R5:96 TQ:96 QM:192")
-_decl("float32", "ST:4352 MT:4096 MPP:4096 AV:256 JF:256 MR:256 MG:256 DJ:128 COL:64 IDf:128 BLKf:128 DIFF:144 "
-      "M18:288 RS18:144 RESET:256 RM:256 Q8:8 SEL:512 SELT:8 KEEP:128 SHIFT:128 PO:128 MSW:384 TMP:512 BLD:1152 "
-      "A2:256 GSA:256 GSC:256 RP:256 T1:256 UM:256 SQ:256 CF:256 PM:6x152 STP:288 CS:6x144 XE:512 GM:256 "
-      "SC:768 YS:256 SM:832 LS:16 VV:512 SG:768 SGK:96 GMM:192 SW:288 PFW:136 KR:192")
-_decl("int32", "FLI:256 SI:256 CI:256 IB:400 BD:32 PI:32")
-_decl("uint16", "C16:256 L16:176 P16:384")
+_decl("bfloat16", "Q:4352 ST:4352 K1:4352 BITS:4096 XG:4096 AB:4096 AREP:4096 MT:4096 MPP:4096 AV:2048 SBQ:5x768 "
+      "LAND:5x96 SG:768 P0:512 BH:1024 IDb:128 nIDb:128 BLKb:128 XP:128 I65:152 DIFF:152 MRH:456 RS:152 RESET:256 "
+      "NRM:256 RM:256 RMH:128 NM:128 MC:384 ONES:512 Q8:16 BO:16 B2:144 B0:144 B10:144 B23:144 B45:144 TRI:128 TRIx:128 "
+      "TRIB:128 NTM:128 SEL:640 SELJ:128 KSEL:128 DM:128 KEEP:128 SHIFT:128 PO:128 MSW:512 ROT:1536 "
+      "UP:128 nUP:128 LOW:128 STP:304 X3:256 QA:256 QC:256 GSA:256 GSC:256 GM:256 GS2:256 EQ:256 GA:512 "
+      "GB:512 U2:256 GK:256 SGN:512 JUNK:1024 YS:256 VV:512 FW:128 CTX:128 IND:16x128 JB3:16x16 IND2:256 XS:256 "
+      "RF:16 RR:96 RA:96 TQ:96 QM:192 SW:288 GMM:192 KR:192 C16B:16")
+_decl("float16", "RW:4096 W16:512 Y:256 CF:256 XH:256 KM:128 H16:768 T16:32")
+_decl("float32", "CT:4112 JF:256 MR:256 MG:256 DJ:128 COL:96 IDf:128 BLKf:128 Q8f:8 TMP:512 BLD:768 A2:256 PM:6x152 "
+      "CS:6x152 XE:256 X2:256 SC:1024 SM:832 LS:16 PFW:136")
+_decl("int32", "IB:400 SI:512 BD:32 PI:32")
+_decl("uint16", "C16:256 L16:192 P16:384")
 for _b in range(8):
     SCRATCH["ps%d" % _b] = ("psum", [128, 512], "float32")
-NDMA = 32
+NDMA = 36
 SEMAPHORES = ["ev", "es", "et", "eg", "sent"] + ["arr%d" % t for t in range(RO)] + ["d%d" % i for i in range(NDMA)]
 
 
@@ -66,6 +66,10 @@ def build(g, T, topo, core):
         w = T[name].shape[2]
         return (T[name][:, i0:i1, lo:hi], name, i0 * w, i1 * w, None, (i1 - i0) * (hi - lo))
 
+    def r3c(name, i0, i1, c):
+        w = T[name].shape[2]
+        return (T[name][:, i0:i1, c], name, i0 * w, i1 * w, None, i1 - i0)
+
     def ind(win, off):
         return (win[0].indirect(off[0]), win, off, 16 * off[5])
 
@@ -83,7 +87,7 @@ def build(g, T, topo, core):
         return x[0] if isinstance(x, tuple) else x
 
     def two(x):
-        return not isind(x) and x[1][:2] != "ps" and SCRATCH[x[1]][2] in ("bfloat16", "uint16")
+        return not isind(x) and x[1][:2] != "ps" and SCRATCH[x[1]][2] in ("bfloat16", "uint16", "float16")
 
     def add(eng, fns, reads, writes, cost, **kw):
         o = dict(eng=eng, fns=fns, reads=reads, writes=writes, cost=cost, acc=False, sem=None, lat=0.0, bonus=bonus[0])
@@ -115,8 +119,11 @@ def build(g, T, topo, core):
         else:
             vop(lambda: g.vector.tensor_scalar(out[0], a[0], ap(s1), ap(s2), op0, op1), out, [a, s1, s2], f)
 
-    def scan(out, d0, d1, op0, op1):
-        vop(lambda: g.vector.tensor_tensor_scan(out[0], d0[0], d1[0], 0.0, op0, op1), out, [d0, d1], 1)
+    def scan(out, d0, d1, op0, op1, init=0.0):
+        vop(lambda: g.vector.tensor_tensor_scan(out[0], d0[0], d1[0], ap(init), op0, op1), out, [d0, d1, init], 1)
+
+    def red(out, a, op):
+        add("v", [lambda: g.vector.tensor_reduce(out[0], a[0], AX.X, op)], [a], [out], 20 + max(64, a[5]))
 
     def mset(out, v):
         add("v", [lambda: g.vector.memset(out[0], v)], [], [out], 20 + max(64, out[5] * (0.5 if two(out) else 1)))
@@ -134,12 +141,12 @@ def build(g, T, topo, core):
             [out] + ([accum] if accum else []), c + (20 if accum else 0))
 
     def mm(items, acc=False):
-        fns, rd, wr, c = [], [], [], 30.0
+        fns, rd, wr, c = [], [], [], 20.0
         for (o, l, rr, st, sp) in items:
             fns.append(lambda o=o, l=l, rr=rr, st=st, sp=sp: g.tensor.matmul(o[0], l[0], rr[0], st, sp))
             rd += [l, rr]
             wr.append(o)
-            c += PE * max(64, rr[5]) * (1 if two(l) else 4)
+            c += 10 + PE * max(min(64, l[5]), rr[5]) * (1 if two(l) else 4)
         add("t", fns, rd, wr, c, acc=acc)
 
     def iota(out, pat, base=0, cm=0):
@@ -160,11 +167,14 @@ def build(g, T, topo, core):
             fn = lambda: {"g": g, "y": g.sync, "s": g.scalar}[q].dma_start(out, a)
         add(q, [fn], rd, wr, 100.0, sem=sem, val=16, lat=lat)
 
-    def ps(b, lo=0, hi=512, step=1):
-        return r("ps%d" % b, lo, hi, step)
+    def rows(out, a, q="y"):
+        dma(q, out[0], a[0], [a], [out], 2500)
 
-    def col(i):
-        return r("COL", i, i + 1)
+    def ps(b, lo=0, hi=512, step=1, p=None):
+        return r("ps%d" % b, lo, hi, step, p=p)
+
+    def col(i, n=1):
+        return r("COL", i, i + n)
 
     def sm(lo, n=16):
         return r("SM", lo, lo + n)
@@ -172,450 +182,541 @@ def build(g, T, topo, core):
     def oh(f):
         return col(16 + f)
 
+    one = slice(0, 1)
+    Mp, Mn, ZERO = (r("MC", 128 * j, 128 * j + 128, p=one) for j in range(3))
+
+    def ones(n):
+        return r("ONES", 0, n, p=one)
+
     bonus[0] = 20000.0
     dma("y", T.IB[:, 0:256], T.pr[:], [], [r("IB", 0, 256)], 2000)
     dma("g", T.IB[:, 384:385], T.w[:], [], [r("IB", 384, 388)], 2000, True)
     dma("g", T.IB[:, 388:389], T.kk[:], [], [r("IB", 388, 392)], 2000, True)
     mset(r("IB", 392, 396), 0)
-    dma("g", T.IB[4:128:16, 392:393], T.th[:], [], [r("IB", 392, 396)], 2000, True)
+    dma("g", T.IB[8:128:16, 392:393], T.th[:], [], [r("IB", 392, 396)], 2000, True)
     dma("y", T.IB[:, 256:384], T.mt[:], [], [r("IB", 256, 384)], 2000)
     dma("s", T.Q[:, 0:2048], T.rec[:, 0:2048], [], [r("Q", 0, 2048)], 4500)
     dma("y", T.Q[:, 2048:4096], T.rec[:, 2048:4096], [], [r("Q", 2048, 4096)], 4500)
-    JB3 = (T.JB3[:], "JB3", 0, 256, None, 256)
+    JB3 = lambda f: r3s("JB3", 8 * f, 8 * f + 8, 0, 16)
     bonus[0] = 9000.0
-    iota(r("JF"), [[1, 256]])
     iota(r("PI", 0, 1), [[0, 1]], 0, 1)
-    iota(r("MR"), [[0, 16], [1, 16]])
-    iota(r("MG"), [[1, 16], [0, 16]])
+    iota(r("JF"), [[1, 256]])
     iota(r("DJ"), [[1, 128]], 0, -1)
-    iota(JB3, [[1, 256]])
-    iota(r("M18", 0, 144), [[0, 8], [1, 18]], -1)
-    iota(r("M18", 144, 288), [[1, 8], [0, 18]])
+    iota(r("MG"), [[1, 16], [0, 16]])
+    iota(r("MR"), [[0, 16], [1, 16]])
+    iota(r("BH", 0, 512), [[64, 8], [0, 64]])
+    iota(r("BH", 512, 1024), [[0, 8], [1, 64]])
+    iota(r3s("JB3", 0, 16, 0, 16), [[1, 256]])
     bonus[0] = 0.0
-    mset(r("FL"), 0.0)
-    mset(r("AB", 0, 1088), 0.0)
-    for j in range(4):
-        act(r("ST", 1088 * j, 1088 * j + 1088), r("AB", 0, 1088), F.Copy)
-    for j in range(2):
-        act(r("MT", 1024 * j, 1024 * j + 1024), r("AB", 0, 1024), F.Copy)
-    PF, PR, PG, PG16 = col(0), col(1), col(2), col(3)
+    for h in range(HO):
+        iota(r("MRH", 152 * h, 152 * h + 152), [[0, 8], [1, KW]], 16 * h - 2)
+    PF, PR, PG = col(0), col(1), col(2)
+    DJ = r("DJ")
     ts(r("PI", 1, 2), r("PI", 0, 1), 15, A.bitwise_and)
     ts(r("PI", 2, 3), r("PI", 0, 1), 4, A.logical_shift_right)
-    cp(r("COL", 0, 3), r("PI", 0, 3))
-    ts(PG16, PG, 16.0, A.mult, 15.0, A.add)
-    ts(r("COL", 16, 32), r("JF", 0, 16), PR, A.is_equal)
-    DJ = r("DJ")
-    pf, idb, lob, jb, mf = (r("BLD", 0, 256), r("BLD", 256, 512), r("BLD", 512, 768), r("BLD", 768, 1024),
-                            r("BLD", 1024, 1152))
-    cp(pf, r("IB", 0, 256))
+    ts(r("PI", 3, 4), r("PI", 0, 1), 7, A.bitwise_and)
+    cp(col(0, 4), r("PI", 0, 4))
+    ts(col(16, 16), r("JF", 0, 16), PR, A.is_equal)
+    mset(r("ONES"), 1.0)
+    mset(r("MC", 0, 128), M4096)
+    mset(r("MC", 128, 256), -M4096)
+    mset(r("MC", 256, 384), 0.0)
+    for i, v in ((10, 2047.5), (11, -2048.0), (12, 2048.0)):
+        mset(col(i), v)
+    ids, xs = r("BLD", 0, 256), r("BLD", 256, 640)
     ts(col(4), PR, 256.0, A.mult)
-    ts(idb, r("JF"), col(4), A.add)
-    tt(r("LOB"), pf, idb, A.is_equal)
-    for j in range(8):
-        dma("ys"[j % 2], T.FL[16 * j + 5:16 * j + 6, :], T.LOB[16 * j:16 * j + 8, :], [r("LOB")], [r("FL", row=j)], 2000)
-    cp(lob, r("LOB"))
-    dma("y", T.ST[5:128:16, 0:4096], lob[0], [lob], [r("ST", 0, 4096, row=5)], 2500)
-    dma("s", T.ST[0:128:16, 0:4096], idb[0], [idb], [r("ST", 0, 4096, row=0)], 2500)
-    cp(mf, r("IB", 256, 384))
-    dma("y", T.ST[2:128:16, 0:2048], mf[0], [mf], [r("ST", 0, 2048, row=2)], 2500)
-    dma("y", T.ST[1:128:16, 0:4096], pf[0], [pf], [r("ST", 0, 4096, row=1)], 2500)
+    ts(ids, r("JF"), col(4), A.add)
+    bonus[0] = 9000.0
+    lob = r("XS")
+    tt(lob, r("IB", 0, 256), ids, A.is_equal)
+    flc = r("MPP", p=slice(0, 8))
+    rows(flc, lob)
+    bonus[0] = 0.0
     ts(r("IDb"), DJ, 0.0, A.is_equal)
     ts(r("IDf"), DJ, 0.0, A.is_equal)
     ts(r("BLKb"), r("MG", 0, 128), PG, A.is_equal)
     ts(r("BLKf"), r("MG", 0, 128), PG, A.is_equal)
-    cp(r("COL", 5, 8), r("IB", 384, 396, 4))
-    mm([(ps(7, 0, 1), r("BLKf"), col(7), True, True)])
-    ts(jb, r("JF"), 0.0, A.mult, ps(7, 0, 1), A.add)
-    dma("y", T.ST[4:128:16, 0:4096], jb[0], [jb], [r("ST", 0, 4096, row=4)], 2500)
-    ts(r("B2"), r("JF", 0, 144), PG16, A.is_equal)
-    ts(r("B5"), r("B2"), oh(5), A.mult)
+    ts(r("Q8f"), r("JF", 0, 8), PG, A.is_equal)
+    Q8, nQ8 = r("Q8", 0, 8), r("Q8", 8, 16)
+    cp(Q8, r("Q8f"))
+    ts(nQ8, r("Q8f"), -1.0, A.mult)
+    ts(col(8), PR, 8.0, A.is_ge)
+    ts(col(9), col(8), -16.0, A.mult, 8.0, A.add)
+    ts(r("XP"), DJ, col(9), A.is_equal)
+    OFF, OFFX, OFFA = col(13), col(14), col(15)
+    ts(OFF, col(8), -4608.0, A.mult, 2048.0, A.add)
+    ts(OFFX, col(8), 4608.0, A.mult, -2560.0, A.add)
+    ts(OFFA, OFF, -0.5, A.add)
+    cp(col(5, 3), r("IB", 384, 396, 4))
+    ts(r("TMP", 0, 1), col(5), 0.5, A.mult, OFF, A.mult)
+    cp(r("TMP", 1, 2), col(7))
+    mm([(ps(7, 0, 2), r("BLKf"), r("TMP", 0, 2), True, True)])
+    cp(r("T16", 0, 1), col(5))
+    mm([(ps(7, 2, 3), r("XP"), r("T16", 0, 1), True, True)])
+    ts(col(32), ps(7, 0, 1), -1.0, A.mult, -2048.0, A.add)
+    cp(r("C16B", 0, 1), ps(7, 1, 2))
+    tt(col(33), ps(7, 1, 2), r("C16B", 0, 1), A.subtract)
+    ts(col(34), oh(8), r("C16B", 0, 1), A.mult)
+    THC = col(35)
+    ts(THC, oh(9), col(33), A.mult, col(34), A.add)
+    ts(col(36), col(5), 0.5, A.mult)
+    ts(col(37), col(5), -0.5, A.mult)
+    ts(col(38), ps(7, 2, 3), 0.5, A.mult)
+    ts(col(39), ps(7, 2, 3), -0.5, A.mult)
+    for j in range(4):
+        ts(r("W16", 128 * j, 128 * j + 128), r("BLKb"), col(36 + j), A.mult)
+    bonus[0] = 5000.0
+    ts(r("SI", 0, 256), ids, col(32), A.add)
+    ts(r("SI", 256, 512), r("SI", 0, 256), 4095, A.bitwise_and)
+    cp(r("TMP", 0, 256), r("SI", 256, 512))
+    ts(r("H16", 0, 256), r("SI", 256, 512), -2048.0, A.add)
+    act(r("TMP", 256, 512), r("TMP", 0, 256), F.Square)
+    ts(r("SI", 0, 256), r("TMP", 256, 512), -12.0, A.add, 1.0 / 32, A.mult)
+    ts(r("SI", 256, 512), r("SI", 0, 256), 4095, A.bitwise_and)
+    ts(r("H16", 256, 512), r("SI", 256, 512), -2048.0, A.add)
+    ts(r("H16", 512, 768), r("ONES", 0, 256), 0.5, A.mult)
+    for j in (2, 0, 1):
+        dma("y", T.RW[8 * j:8 * j + 8, :], T.H16[:, 256 * j:256 * j + 256], [r("H16", 256 * j, 256 * j + 256)],
+            [(None, "RW", 0, 4096, j, 4096)], 2500)
+    km = r("T16", 8, 32)
+    ts(r("T16", 24, 32), r("JF", 0, 8), 0.0, A.is_equal)
+    ts(r("T16", 8, 16), r("Q8f"), col(6), A.mult)
+    cp(r("T16", 16, 24), r("Q8f"))
+    ts(r("PI", 4, 5), r("IB", 388, 389), 1, A.bitwise_and)
+    ts(r("T16", 25, 26), r("PI", 4, 5), 4096.0, A.mult)
+    k24 = slice(0, 24)
+    mm([(ps(6, 0, 128, p=k24), km, r("IDb"), True, True)])
+    cp(r("KM", p=k24), ps(6, 0, 128, p=k24))
+    ts(r("H16", 0, 128, p=k24), ps(6, 0, 128, p=k24), -1.0, A.mult)
+    for j in range(8):
+        b, x = ps(3 + j % 2), r("RW", 512 * j, 512 * j + 512, p=k24)
+        mm([(b, Mp, ones(512), True, False), (b, r("H16", 0, 128, p=k24), x, False, False),
+            (b, Mn, ones(512), False, False), (b, r("KM", p=k24), x, False, True)])
+        act(r("CT", 512 * j, 512 * j + 512), b, bias=col(10))
+    cp(r("CT", 4096, 4097), r("CT", 0, 1))
+    bonus[0] = 0.0
+    ts(xs, r("IB", 0, 384), -2048.0, A.add)
+    hi_, lo_ = r("JUNK", 0, 384), r("JUNK", 384, 768)
+    act(hi_, xs, F.Copy)
+    tt(lo_, xs, hi_, A.subtract)
+    ts(r("BH", 0, 512), r("BH", 0, 512), oh(0), A.mult)
+    ts(r("BH", 512, 1024), r("BH", 512, 1024), oh(1), A.mult)
+    tt(r("P0"), r("BH", 0, 512), r("BH", 512, 1024), A.add)
+    ts(r("TMP", 0, 9), r("JF", 0, 9), 512.0, A.mult, -2048.0, A.add)
+    ts(col(40, 9), r("TMP", 0, 9), oh(0), A.mult, THC, A.add)
+    for j in range(9):
+        n = min(512, WD - 512 * j)
+        act(r("ST", 512 * j, 512 * j + n), r("P0", 0, n), bias=col(40 + j))
+    rows(r("ST", 0, 4096, row=10), lob)
+    mset(r("MT", 0, 2048), 0.0)
+    for j, x in enumerate((hi_, lo_)):
+        o = x[2]
+        dma("y", T.AB[8 * j:8 * j + 8, :], T.JUNK[:, o:o + 256], [x], [(None, "AB", 0, 4096, j, 4096)], 2500)
+        rows(r("ST", 0, 4096, row=2 + j), r("JUNK", o, o + 256))
+        rows(r("ST", 0, 2048, row=4 + j), r("JUNK", o + 256, o + 384))
+        rows(r("MT", 0, 2048, row=4 + j), r("JUNK", o + 256, o + 384))
+    ts(col(50), col(3), 16.0, A.mult, 15.0, A.add)
+    ts(r("B0"), r("JF", 0, 144), col(50), A.is_equal)
+    ts(col(51), PG, 16.0, A.mult, 15.0, A.add)
+    ts(r("B2"), r("JF", 0, 144), col(51), A.is_equal)
     ts(r("TRI"), DJ, 0.0, A.is_ge)
     ts(r("TRIx"), DJ, 0.0, A.is_gt)
     tt(r("TRIB"), r("TRI"), r("BLKb"), A.mult)
-    tt(r("TMB"), r("TRIB"), r("BLKb"), A.subtract)
-    mset(r("ONES"), 1.0)
     mset(r("Q", 4096, WD), 0.0)
     LW = sm(0)
     for j in range(3):
         ts(sm(16 * j), r("JF", 0, 256, 16), PR, A.add, 4096.0, A.add)
-    ts(col(8), PR, 8.0, A.is_ge)
-    ts(col(9), col(8), -16.0, A.mult, 8.0, A.add)
-    ts(r("XP"), DJ, col(9), A.is_equal)
+    LWm = sm(48)
+    ts(LWm, LW, -2048.0, A.add)
     ts(r("nIDb"), r("IDb"), -1.0, A.mult)
-    ts(col(60), PG, 2.0, A.mult, 1.0, A.add)
-    tt(col(12), PF, col(60), A.add)
-    ts(r("I65"), r("JF", 0, 144), col(12), A.is_equal, 262144.0, A.mult)
-    ts(r("TMP", 0, 128), r("IDf"), col(6), A.mult)
-    mm([(ps(7, 0, 128), r("BLKf"), r("TMP", 0, 128), True, True)])
-    ts(r("SI", 0, 128), ps(7, 0, 128), col(5), A.mult, 2048.0, A.add)
-    ts(r("SI", 128, 256), r("SI", 0, 128), 4095, A.bitwise_and)
-    ts(r("TMP", 128, 256), r("SI", 128, 256), -2048.0, A.add, 0.5, A.mult)
-    ts(r("TMP", 0, 128), r("BLKf"), col(5), A.mult, 0.5, A.mult)
-    ts(r("WM", 0, 256), r("TMP", 0, 256), M64 / 2, A.add, M64 / 2, A.subtract)
-    tt(r("WM", 256, 512), r("TMP", 0, 256), r("WM", 0, 256), A.subtract)
-    mm([(ps(7), r("XP"), r("WM"), True, True)])
-    act(r("WX"), ps(7), F.Copy, scale=2.0)
-    ts(col(10), PF, 0.0, A.is_equal, -2048.0, A.mult)
-    ts(col(11), PF, 1.0, A.is_equal, 0.5, A.mult)
-    ts(r("CST"), r("ONES", 0, 128), col(10), A.mult, col(11), A.add)
-    ts(r("Q8"), r("JF", 0, 8), PG, A.is_equal)
-    for j, v in enumerate((128.0, -64.0)):
-        ts(r("BO", 8 * j, 8 * j + 8), r("Q8"), v, A.mult)
-    for h in range(HO):
-        ts(r("MRH", 144 * h, 144 * h + 144), r("M18", 0, 144), 16.0 * h, A.add)
-        for k in range(1, 8, 2):
-            ts(r("MRH", 144 * h + 18 * k, 144 * h + 18 * k + 18), r("M18", 0, 18), 16.0 * h + 0.5, A.add)
-    mset(r("MRH", 17, 432, 18), TAG)
-    mset(r("MRH", 0, 288, 18), TAG)
-    mset(r("MRH", 288, 432, 18), 0.0)
-    ts(r("TMP", 256, 401), r("JF", 0, 145), -1.0, A.add, col(12), A.is_equal)
-    tt(r("DIFF"), r("TMP", 256, 400), r("TMP", 257, 401), A.subtract)
-    ts(r("RS18"), r("M18", 0, 144), -1.0, A.is_equal, 2.0 ** 26, A.mult)
-    ts(r("RESET"), r("MR"), 0.0, A.is_equal, 2.0 ** 26, A.mult)
+    ts(col(52), PG, KW - 16.0, A.mult, 2.0, A.add)
+    tt(col(53), PF, col(52), A.add)
+    ts(r("I65"), r("JF", 0, 152), col(53), A.is_equal, 262144.0, A.mult)
+    ts(r("EQ", 0, 153), r("JF", 0, 153), -1.0, A.add, col(53), A.is_equal)
+    tt(r("DIFF"), r("EQ", 0, 152), r("EQ", 1, 153), A.subtract)
+    for j, v in enumerate((64.0, -64.0)):
+        ts(r("BO", 8 * j, 8 * j + 8), r("Q8f"), v, A.mult)
+    mset(r("MRH", KW - 1, 456, KW), TAG)
+    for j in range(2):
+        mset(r("MRH", j, 304, KW), TAG)
+        mset(r("MRH", 304 + j, 456, KW), 0.0)
+    mset(r("RS"), 0.0)
+    mset(r("RS", 0, 152, KW), 2.0 ** 26)
+    ts(r("RESET"), r("MR"), 0.0, A.is_equal, 2.0 ** 31, A.mult)
     ts(r("RM"), r("MR"), PR, A.is_equal)
+    ts(r("RMH"), r("RM", 0, 128), 0.5, A.mult, 0.5, A.add)
     ts(r("NRM"), r("MR"), PR, A.not_equal, 2.0 ** 25, A.mult)
+    ts(r("NM"), r("NRM", 0, 128), 32.0, A.mult, -M4096, A.add)
     for j in range(4):
-        ts(r("SEL", 128 * j, 128 * j + 128), r("BLKf"), oh(j), A.mult)
-    SELID, SELP, SELM, SELMP = [r("SEL", 128 * j, 128 * j + 128) for j in range(4)]
-    ts(r("BL64"), r("M18", 144, 288), PG, A.is_equal, 64.0, A.mult)
-    mset(r("BL64", 0, 144, 18), 0.0)
-    mset(r("QAM"), 0.0)
-    ts(r("SELT"), r("Q8"), oh(4), A.mult)
-    mset(r3s("PM", 0, 6, 0, 1), -2.0)
-    mset(col(14), 2047.5)
-    mset(col(15), -0.5)
+        tt(col(56 + j), oh(2 * j), oh(2 * j + 1), A.add)
+        act(r("SEL", 128 * j, 128 * j + 128), r("BLKb"), F.Copy, scale=col(56 + j))
+    act(r("SEL", 512, 640), r("BLKb"), F.Copy, scale=oh(10))
+    SELID, SELP, SELM, SELMP, SELLO = [r("SEL", 128 * j, 128 * j + 128) for j in range(5)]
     mset(r("PFW", 128, 136), 4096.0)
-    ts(col(13), PG, 8.0 - S_IND, A.is_ge, 128.0, A.mult)
-    LBC, LCOL = r("L16", 8, 16), r("L16", 16, 32)
-    cp(LBC, r("JF", 17, 144, 18))
-    cp(LCOL, r("JF", 0, 16))
-    aL, cL, mpL, hL, bL, dL, kL = r("L16", 32, 48), r("L16", 48, 64), 64, 80, r("L16", 96, 112), r("L16", 112, 128), 128
-    LPR, aS = r("L16", 152, 155), r("L16", 160, 176)
+    ts(col(60), PG, 8.0 - S_IND, A.is_ge, 128.0, A.mult)
+    ts(col(61), PF, 128.0, A.add)
+    lane = (PF, col(61))
+    mset(r("X3"), 0.0)
+    LCOL = r("L16", 16, 24)
+    cp(LCOL, r("JF", 0, 8))
+    LBC = r("L16", 8, 16)
+    cp(LBC, r("JF", KW - 1, 152, KW))
+    aL, cL, mpL, hL, bL, dL, kL, uL = 32, 48, 64, 80, 96, r("L16", 112, 128), 128, 176
+    LPR, aS = r("L16", 152, 155), 160
+
+    def lst(base, f=None):
+        return r("L16", base, base + 16) if f is None else r("L16", base + 8 * f, base + 8 * f + 8)
 
     def start_mates():
-        ts(r("RP", 0, 144), r("B2"), oh(1), A.mult)
-        for j in range(16):
-            mm([(ps(5, 0, 256), r("RP", 15 - j, 143 - j), r("ST", j, 4096, 16), j == 0, j == 15)], acc=j > 0)
-        cp(r("P16", 0, 256), ps(5, 0, 256))
-        ts(r("P16", 256, 384), mf, -2048.0, A.add)
-        iota(r("AV"), [[1, 16], [128, 16]])
-        dma("y", T.MT[2:128:16, 0:2048], mf[0], [mf], [r("MT", 0, 2048)], 2500)
+        k16 = slice(0, 16)
+        mm([(ps(5, 0, 256), r("B0", 15 - j, 143 - j, p=k16), r("AB", j, 4096, 16, p=k16), j == 0, j == 15) for j in range(16)])
+        ts(r("P16", 0, 256), ps(5, 0, 256), 2048.0, A.add)
+        ts(r("P16", 256, 384), r("IB", 256, 384), -2048.0, A.add)
+        ts(r("GM"), r("MR"), 128.0, A.mult, oh(4), A.mult)
+        ts(r("GK"), r("MG"), oh(5), A.mult)
+        tt(r("EQ"), r("GM"), r("GK"), A.add)
+        iota(sm(64, 8), [[64, 2], [0, 4]], -2048)
+        iota(sm(72, 8), [[0, 2], [16, 4]])
+        ts(sm(80, 8), sm(64, 8), oh(4), A.mult)
+        ts(sm(88, 8), sm(72, 8), oh(5), A.mult)
+        tt(sm(64, 8), sm(80, 8), sm(88, 8), A.add)
         for j in range(8):
-            ts(ind(r("MT", 2048, 4096), r("P16", 256 + 16 * j, 272 + 16 * j)), r("AV"), 1.0, A.mult, 16.0 * j, A.add)
-        dma("y", T.ST[2:128:16, 2048:4096], T.MT[2:128:16, 2048:4096], [r("MT", 2048, 4096)], [r("ST", 2048, 4096, row=2)], 2500)
+            av = r("AV", 256 * j, 256 * j + 256)
+            act(av, r("EQ"), bias=sm(64 + j, 1))
+            cp(ind(r("MT", 2048, 4096), r("P16", 256 + 16 * j, 272 + 16 * j)), av)
         for j in range(8):
             act(r("MPP", 512 * j, 512 * j + 512), ind(r("MT"), r("P16", 32 * j, 32 * j + 32)), F.Copy)
-        dma("y", T.ST[3:128:16, 0:4096], T.MPP[2:128:16, 0:4096], [r("MPP")], [r("ST", 0, 4096, row=3)], 2500)
+        for j in range(2):
+            rows(r("ST", 0, 4096, row=6 + j), r("MPP", 0, 4096, row=4 + j))
+            rows(r("ST", 2048, 4096, row=4 + j), r("MT", 2048, 4096, row=4 + j))
 
     def late_constants():
         iota(r("K1", 0, 2176), [[0, 2176]], 5)
         dma("y", T.K1[:, 2176:WD], T.K1[:, 0:2176], [r("K1", 0, 2176)], [r("K1", 2176, WD)], 4000)
-        ts(r("NRB"), r("NRM"), -BIG, A.add)
         ts(LPR, r("JF", 0, 3), 0.0, A.mult, PR, A.add)
-        ts(r("SELLO"), r("BLKb"), oh(5), A.mult)
+        act(r("B10"), r("B2"), F.Copy, scale=oh(10))
+        act(r("B23"), r("B2"), F.Copy, scale=col(57))
+        act(r("B45"), r("B2"), F.Copy, scale=col(58))
+        tt(r("NTM"), r("BLKb"), r("TRIB"), A.subtract)
         mset(r3s("SBQ", 0, RO, 0, 96), -1.0)
         mset(r("SG", 0, 96), 0.0)
-        ts(r("COL", 32, 44), r("COL", 16, 28), -2.0, A.mult, 1.0, A.add)
-        mset(r("BITS", 0, 1), 1.0)
+        ts(col(64, 12), col(16, 12), -2.0, A.mult, 1.0, A.add)
+        tt(col(76), oh(12), oh(13), A.add)
+        ts(col(77), col(76), 256.0, A.mult, oh(14), A.add)
+        ts(col(78), PR, 12.0, A.is_lt, BETA, A.mult)
+        tt(col(79), col(78), col(77), A.subtract)
+        cp(r("BITS", 0, 1), col(79))
         for k in range(12):
-            ts(r("BITS", 1 << k, 2 << k), r("BITS", 0, 1 << k), col(32 + k), A.mult)
-        tt(col(44), oh(12), oh(13), A.add)
-        ts(col(45), col(44), 256.0, A.mult, oh(14), A.add)
-        ts(col(46), oh(15), TAG, A.mult, col(45), A.add)
-        ts(r("KSEL"), r("BLKb"), col(46), A.mult)
-        ts(col(47), PR, 12.0, A.is_lt, -B20 / 2, A.mult)
-        tt(col(48), col(47), col(45), A.add)
-        ts(r("PI", 3, 4), r("PI", 2, 3), 1, A.bitwise_and)
-        tt(col(50), col(48), r("PI", 3, 4), A.mult)
-        tt(col(49), col(48), col(50), A.subtract)
-        ts(r("TMP", 0, 128), r("MR", 0, 128), 4.0, A.is_equal, col(44), A.mult)
-        tt(r("DM"), r("TMP", 0, 128), r("BLKf"), A.mult)
-        tt(col(51), oh(0), oh(2), A.add)
-        tt(col(52), oh(1), oh(3), A.add)
-        ts(r("KEEP"), DJ, 0.0, A.is_equal, col(51), A.mult)
-        ts(r("SHIFT"), DJ, 1.0, A.is_equal, col(51), A.mult)
-        ts(r("TMP", 128, 256), DJ, -1.0, A.is_ge, col(52), A.mult)
-        tt(r("PO"), r("TMP", 128, 256), r("TRIx"), A.is_gt)
-        ts(r("MSW", 0, 128), DJ, 2.0, A.is_equal, oh(0), A.mult)
-        ts(r("MSW", 128, 256), DJ, 3.0, A.is_equal, oh(0), A.mult)
-        tt(r("TMP", 256, 384), r("KEEP"), r("SHIFT"), A.add)
-        ts(r("MSW", 256, 384), r("TMP", 256, 384), oh(2), A.mult)
-        ts(col(53), oh(4), 4096.0, A.mult)
-        tt(col(54), col(7), oh(5), A.add)
-        ts(col(55), oh(2), -1.0, A.mult, 1.0, A.add)
-        ts(col(56), oh(3), -1.0, A.mult, 1.0, A.add)
-        tt(col(57), col(55), oh(3), A.subtract)
+            if k < 10:
+                ts(r("BITS", 1 << k, 2 << k), r("BITS", 0, 1 << k), col(64 + k), A.mult)
+            else:
+                act(r("BITS", 1 << k, 2 << k), r("BITS", 0, 1 << k), F.Copy, scale=col(64 + k))
+        ts(col(80), oh(15), TAG, A.mult, col(77), A.add)
+        act(r("KSEL"), r("BLKb"), F.Copy, scale=col(80))
+        ts(r("PI", 5, 6), r("PI", 2, 3), 1, A.bitwise_and)
+        cp(col(81), r("PI", 5, 6))
+        ts(col(82, RO), r("JF", 0, RO), 1.0, A.add, oh(15), A.mult)
+        ts(col(82, RO), col(82, RO), -1.0, A.mult)
+        tt(col(87), oh(8), oh(9), A.add)
+        ts(r("TMP", 0, 128), r("MR", 0, 128), 15.0, A.is_equal, col(87), A.mult)
+        ts(r("TMP", 128, 256), r("TMP", 0, 128), -2.0 ** 25, A.mult)
+        tt(r("SELJ"), r("TMP", 128, 256), r("BLKf"), A.mult)
+        ts(r("DM"), DJ, -4.0, A.is_equal, col(76), A.mult)
+        tt(col(88), col(56), col(58), A.add)
+        tt(col(89), col(57), col(59), A.add)
+        ts(r("KEEP"), DJ, 0.0, A.is_equal, col(88), A.mult)
+        ts(r("SHIFT"), DJ, 2.0, A.is_equal, col(88), A.mult)
+        ts(r("TMP", 256, 384), DJ, 0.0, A.is_equal, col(89), A.mult)
+        ts(r("TMP", 384, 512), DJ, -2.0, A.is_equal, col(89), A.mult)
+        tt(r("PO"), r("TMP", 256, 384), r("TMP", 384, 512), A.add)
+        ts(r("MSW", 0, 128), DJ, 4.0, A.is_equal, col(56), A.mult)
+        ts(r("MSW", 128, 256), DJ, 6.0, A.is_equal, col(56), A.mult)
+        tt(r("TMP", 0, 128), r("KEEP"), r("SHIFT"), A.add)
+        ts(r("MSW", 256, 384), r("TMP", 0, 128), col(58), A.mult)
+        tt(col(90), THC, oh(10), A.add)
+        ts(col(91), col(58), -1.0, A.mult, 1.0, A.add)
+        ts(col(92), col(59), -1.0, A.mult, 1.0, A.add)
+        tt(col(93), col(91), col(59), A.subtract)
+        act(r("MSW", 384, 512), r("IDb"), F.Copy, scale=col(93))
         ts(r("TMP", 384, 512), DJ, 0.0, A.is_lt, 128.0, A.mult)
-        tt(r("TMP", 0, 128), r("TMP", 384, 512), DJ, A.add)
+        tt(r("TMP", 128, 256), r("TMP", 384, 512), DJ, A.add)
         for d in range(1, NR):
-            ts(r("ROT", 128 * d - 128, 128 * d), r("TMP", 0, 128), 16.0 * d, A.is_equal)
+            ts(r("ROT", 128 * d - 128, 128 * d), r("TMP", 128, 256), 16.0 * d, A.is_equal)
+        act(r("ROT", 384, 768), r("ROT", 0, 384), F.Copy, scale=-256.0)
+        act(r("ROT", 768, 1152), r("ROT", 0, 384), F.Copy, scale=col(8))
+        act(r("ROT", 1152, 1536), r("ROT", 768, 1152), F.Copy, scale=-1.0)
         ts(r("UP"), r("IDb"), col(8), A.mult)
         ts(r("nUP"), r("UP"), -1.0, A.mult)
         tt(r("LOW"), r("IDb"), r("UP"), A.subtract)
-        mset(r("X2"), 1.0)
-        ts(sm(64), r("MG", 0, 128, 8), 0.0, A.mult, PF, A.add)
-        ts(sm(72, 8), sm(72, 8), 128.0, A.add)
-        cp(r("X2", 14, 256, 16), sm(64))
-        ts(sm(64), sm(64), -6 * B20, A.add)
+        mset(r("X2"), -2.0 ** 30)
+        for f in range(2):
+            ts(r("X2", 128 * f + 14, 128 * f + 128, 16), r("JF", 0, 8), 0.0, A.mult, lane[f], A.add)
+            ts(sm(96 + 8 * f, RO), r("JF", 0, RO), 1.0, A.add)
+            tt(sm(112 + 8 * f, RO), sm(96 + 8 * f, RO), sm(96 + 8 * f, RO), A.mult)
+            ts(sm(96 + 8 * f, RO), sm(112 + 8 * f, RO), -1.0, A.mult, lane[f], A.add)
+            ts(sm(96 + 8 * f, RO), sm(96 + 8 * f, RO), 1.0 - 12 * BETA * BETA, A.add)
         ts(sm(80), LW, -3840.0, A.add)
-        ts(sm(96), LW, -3841.0, A.add)
+        ts(col(94), PR, 239.0, A.add)
+        mset(r("C16B"), 16.0)
         ts(sm(112, 6), sm(0, 6), -4096.0, A.add)
-        ts(r("PI", 4, 5), r("PI", 0, 1), 1, A.bitwise_and)
-        ts(col(58), r("PI", 4, 5), -1.0, A.mult, 1.0, A.add)
-        ts(sm(118, 6), sm(112, 6), col(58), A.add)
-        ts(sm(124, 6), sm(112, 6), col(58), A.add)
+        ts(r("PI", 6, 7), r("PI", 0, 1), 1, A.bitwise_and)
+        ts(col(95), r("PI", 6, 7), -1.0, A.mult, 1.0, A.add)
+        ts(sm(118, 6), sm(112, 6), col(95), A.add)
+        ts(sm(124, 6), sm(112, 6), col(95), A.add)
         for j in range(3):
             cp(sm(130 + 6 * j, 6), sm(0, 6))
+        ts(sm(148, 12), sm(130, 12), -2048.0, A.add)
         iota(r("KR", 0, 96), [[2, 48], [0, 2]], 1)
 
-    def r2w(b, lo, items, out, off="NRM"):
+    def r2w(b, lo, items, out):
         o = lo
         for sel, src in items:
             n = src[5]
-            mm([(ps(b, o, o + n), r("IDb"), r(off, 0, n), True, False)])
+            mm([(ps(b, o, o + n), r("IDb"), r("NRM", 0, n), True, False)])
             mm([(ps(b, o, o + n), sel, src, False, True)], acc=True)
             o += n
         scan(out, r("RESET", 0, o - lo), ps(b, lo, o), A.add, A.min)
 
-    def t2w(b, lo, win, lst, xe, mask=None):
-        n = 16 * lst[5]
-        tt(r("XE", xe, xe + n), ind(win, lst), mask or r("RM", 0, n), A.mult)
-        mm([(ps(b, lo + 8 * h, lo + 8 * h + 8), r("XE", xe + 128 * h, xe + 128 * h + 128), r("Q8"), True, True)
-            for h in range(n // 128)])
-
-    live, af = sm(160), sm(176)
+    live = sm(160)
 
     def lanes(t):
         s = (STEP * t) & 2047
-        cuts = sorted({0, 1024, 2048 - s, 2048})
-        for x, z in zip(cuts, cuts[1:]):
-            if t:
-                act(r("FL", x, z), r("ST", (x + s) & 2047, ((x + s) & 2047) + z - x), F.Copy)
-        for x in range(2):
-            mm([(ps(0, 64 * x, 64 * x + 64), r("B5", 15 - j, 143 - j), r("FL", 1024 * x + j, 1024 * x + 1024, 16), j == 0, j == 15)
-                for j in range(16)])
+        if t == 0:
+            k8 = slice(0, 8)
+            mm([(ps(0, 0, 128), r("B0", 15 - j, 143 - j, p=k8), r("MPP", j, 2048, 16, p=k8), j == 0, j == 15) for j in range(16)])
+        else:
+            mm([(ps(0, 0, 128), ZERO, ones(128), True, False)])
+            items = []
+            for j in range(16):
+                nb = (2048 - s - j + 15) // 16
+                x = s + j + 16 * nb - 2048
+                sel = r("B10", 15 - j, 143 - j)
+                items += [(ps(0, 0, nb), sel, r("ST", s + j, 2048, 16), False, False),
+                          (ps(0, nb, 128), sel, r("ST", x, x + 16 * (128 - nb), 16), False, j == 15)]
+            mm(items, acc=True)
         act(r("FW"), ps(0, 0, 128), F.Copy)
         mm([(ps(1, 0, 128), r("FW"), r("BLKb"), True, True)])
         act(r("CTX"), ps(1, 0, 128), F.Copy)
-        mm([(ps(1, 128, 136), r("TRI"), r("CTX", 0, 128, 16), True, True)] +
-           [(ps(1, 136 + 8 * j, 144 + 8 * j), r("ONES", 0, 128), r("CTX", 0, 128, 16), True, True) for j in range(2)])
+        mm([(ps(1, 128, 136), r("TRI"), r("CTX", 0, 128, 16), True, True),
+            (ps(1, 136, 144), r("ONES", 0, 128), r("CTX", 0, 128, 16), True, True)])
         mm([(ps(0, 128, 256), r("TRIB"), r("FW"), True, False), (ps(0, 128, 256), r("CTX"), r("TRIx"), False, True)])
         ts(sm(192, 8), ps(1, 128, 136), -1.0, A.mult, 0.5, A.add)
-        for k in range(8):
-            o = (T.IND[:, :, 16 * k:16 * k + 16], "IND", k, k + 1, None, 256)
-            if k < 8 - S_IND:
-                ts(o, JB3, ps(1, 128 + k, 129 + k), A.is_ge, 2.0, A.mult)
-            else:
-                act(o, JB3, F.Sign, bias=sm(192 + k, 1))
         act(r("PFW", 0, 128), ps(0, 128, 256), F.Copy)
-        ts(col(59), col(13), s / 8.0, A.add)
-        ts(sm(272), ps(1, 136, 152), -6 * B20, A.add)
-        mm([(ps(2, q, q + 1), (T.IND[:, q, :], "IND", 0, 8, None, 128), r("ONES", 0, 1), True, True) for q in range(16)])
-        ts(bL, ps(2, 0, 16), col(13), A.add, 0.5, A.mult)
-        ts(sm(224), ps(2, 0, 16), col(59), A.add, 8.0, A.mult)
-        tt(r("IND2"), ind(r("PFW"), bL), r("JF"), A.is_le)
-        mm([(ps(2, 16, 32), r("B2", 15 - j, 143 - j), r("IND2", j, 256, 16), j == 0, j == 15) for j in range(16)])
-        tt(r("BD", 16, 32), sm(224), ps(2, 16, 32), A.add)
-        ts(r("PI", 8, 24), r("BD", 16, 32), 2047, A.bitwise_and)
-        cp(aL, r("PI", 8, 24))
+        ts(col(62), col(60), s / 8.0, A.add)
+        for f in FIRST:
+            o = 8 * f
+            part = lambda a, b, n: (a, "IND", o + b, o + b + n, None, 128)
+            for k in range(8):
+                x = part(T.IND[:, o:o + 8, 16 * k:16 * k + 16], k, 1)
+                if k < 8 - S_IND:
+                    ts(x, JB3(f), ps(1, 128 + k, 129 + k), A.is_ge, 2.0, A.mult)
+                else:
+                    act(x, JB3(f), F.Sign, bias=sm(192 + k, 1))
+            mm([(ps(2 + f, q, q + 1), part(T.IND[:, o + q, :], 0, 8), r("ONES", 0, 1), True, True) for q in range(8)])
+            ts(lst(bL, f), ps(2 + f, 0, 8), col(60), A.add, 0.5, A.mult)
+            ts(sm(224 + o, 8), ps(2 + f, 0, 8), col(62), A.add, 8.0, A.mult)
+            i2 = r("IND2", 128 * f, 128 * f + 128)
+            tt(i2, ind(r("PFW"), lst(bL, f)), r("JF", 128 * f, 128 * f + 128), A.is_le)
+            mm([(ps(2 + f, 16, 24), r("B2", 15 - j, 143 - j), r("IND2", 128 * f + j, 128 * f + 128, 16), j == 0, j == 15)
+                for j in range(16)])
+            tt(r("BD", 16 + o, 24 + o), sm(224 + o, 8), ps(2 + f, 16, 24), A.add)
+            ts(r("PI", 8 + o, 16 + o), r("BD", 16 + o, 24 + o), 2047, A.bitwise_and)
+            cp(lst(aL, f), r("PI", 8 + o, 16 + o))
+        for f in range(2):
+            ts(r("X3", 128 * f + 15, 128 * f + 128, 16), ps(1, 136, 144), lane[f], A.is_le, 2.0 ** 40, A.mult)
         ts(live, r("BD", 16, 32), 2048.0 + s, A.is_lt)
         tt(sm(240), r("PI", 8, 24), LW, A.subtract)
         tt(sm(448), sm(240), live, A.mult)
-        tt(af, sm(448), LW, A.add)
-        cp(aS, af)
+        tt(sm(176), sm(448), LW, A.add)
+        cp(lst(aS), sm(176))
 
     stage = [0]
 
-    def hop(h, f):
+    def hop(t, h, f):
         lo, hi = 128 * f, 128 * f + 128
         c = lambda name: r(name, lo, hi)
-        y, e, wm = (c("Y2"), 2 * h + f, "WM") if h else (c("QA"), f, "WX")
-        raw, ku, key, ee = ps(f, 0, 128), ps(f, 128, 256), ps(2 + f, 0, 144), ps(2 + f, 144, 288)
-        end, o = h == HO - 1, 8 * f
-        mm([(raw, r("CST"), r("ONES", 0, 128), True, False)])
-        mm([(raw, r(wm, 0, 128), y, False, False), (raw, r(wm, 256, 384), y, False, True),
-            (ku, r(wm, 128, 256), y, True, False), (ku, r(wm, 384, 512), y, False, True)], acc=True)
-        ts(c("T1"), raw, M4096, A.add, M4096, A.subtract)
-        tt(c("UM"), raw, c("T1"), A.subtract)
-        act(c("SQ"), c("UM"), F.Square, bias=col(14))
-        ts(c("FLI"), c("SQ"), -12.0, A.add, 1.0 / 32, A.mult)
-        tt(c("SI"), c("FLI"), ku, A.add)
-        ts(c("CI"), c("SI"), 4095, A.bitwise_and)
-        cp(c("C16"), c("CI"))
-        cp(c("CF"), c("CI"))
-        tt(c("EQ"), c("CI"), ps(6, lo, hi), A.is_equal)
+        e, o, end = 2 * h + f, 8 * f, h == HO - 1
+        raw, kb = ps(f, 0, 128), 2 + f
+        key, ee = ps(kb, 0, 152), ps(kb, 152, 304)
+        w0 = 0 if h else 256
+        mm([(raw, Mp, ones(128), True, False)])
+        mm([(raw, r("W16", w0 + 128, w0 + 256), c("Y"), False, False), (raw, r("IDb"), r("NM"), False, False),
+            (raw, r("W16", w0, w0 + 128), c("Y"), False, True)], acc=True)
+        scan(r("SC", 768 + lo, 768 + hi), r("RESET", 0, 128), raw, A.add, A.min)
+        ts(lst(uL, f), r("SC", 768 + lo + 15, 768 + hi, 16), 2048.0, A.add)
+        cp(c("C16"), ind(r("CT"), lst(uL, f)))
+        ts(c("CF"), c("C16"), -2048.0, A.add)
+        tt(c("EQ"), c("CF"), ps(6, lo, hi), A.is_equal)
+        key_end = lambda e: r3("PM", e, KW - 1, 152, KW)
+        c_end = lambda e: r3("CS", e, KW - 1, 152, KW)
+        slot = lambda j: ps(kb, 152 + j, 304, KW)
+        if end:
+            tt(sm(368 + o, 8), c_end(f), c_end(2 + f), A.subtract)
         mm([(ee, c("CF"), r("DIFF"), True, not end)] +
-           ([(ps(2 + f, 145, 288, 18), r("IDf"), sm(416 + o, 8), False, True)] if end else []))
-        mm([(key, c("EQ"), r("I65"), True, False), (key, r("IDb"), r("MRH", 144 * h, 144 * h + 144), False, False),
-            (key, c("QAM"), r("BL64"), False, False)] +
-           ([(ps(2 + f, 0, 144, 18), r("IDf"), sm(288 + o, 8), False, False)] if end else []))
-        x0 = 2048 * f
-        for j in range(4):
-            a, b = x0 + 512 * j, x0 + 512 * j + 512
+           ([(slot(1), r("IDf"), sm(368 + o, 8), False, False), (slot(2), r("IDf"), c_end(2 + f), False, True)] if end else []))
+        mm([(key, r("IDb"), r("MRH", 152 * h, 152 * h + 152), True, False), (key, c("EQ"), r("I65"), False, False)] +
+           ([(ps(kb, j, 152, KW), r("IDf"), key_end(2 * j + f), False, False) for j in range(2)] if end else []))
+
+        def sums(src, j0, j1, bo, stop):
+            x, z, p = 2048 * f + 512 * j0, 2048 * f + 512 * j1, slice(32 * j0, 32 * j1)
+            mm([(ps(kb, i + 2, 152, KW, p=p), r(src, x + i, z, 16), bo, False, stop and i == 15) for i in range(16)], acc=True)
+        for j, mode in enumerate(MODES[f]):
+            a, b = 2048 * f + 512 * j, 2048 * f + 512 * j + 512
             got = ind(r("Q"), r("C16", lo + 32 * j, lo + 32 * j + 32))
-            if j < NS[f]:
+            arep = r("AREP", a, b)
+            if mode == "S":
                 bank = ps((4, 5, 7)[stage[0] % 3])
                 stage[0] += 1
                 act(r("XG", a, b), got, F.Copy)
-                mm([(bank, r("nIDb"), r("AREP", a, b), True, False)])
+                mm([(bank, r("nIDb"), arep, True, False)])
                 mm([(bank, r("IDb"), r("XG", a, b), False, True)], acc=True)
-                act(r("AB", a, b), bank, F.Relu)
+                act(r("AB", a, b), bank, F.Abs)
             else:
-                tt(r("XG", a, b), got, r("AREP", a, b), A.subtract)
-                if j < NS[f] + SR[f]:
-                    act(r("AB", a, b), r("XG", a, b), F.Relu)
+                tt(r("XG", a, b), got, arep, A.subtract)
+                if mode == "M":
+                    act(r("AB", a, b), r("XG", a, b), F.Abs)
                 else:
-                    ts(r("AB", a, b), r("XG", a, b), 0.0, A.max)
-        for src, bo in (("XG", r("BO", 8, 16)), ("AB", r("BO", 0, 8))):
-            mm([(ps(2 + f, i + 1, 144, 18), r(src, x0 + i, x0 + 2048, 16), bo, False, i == 15 and src == "AB") for i in range(16)], acc=True)
-        stp = r("STP", 144 * f, 144 * f + 144)
-        scan(r3("PM", e, 1, 145), r("RS18"), key, A.add, A.min)
-        tt(stp, r3("PM", e, 1, 145), r3("PM", e, 0, 144), A.is_equal)
+                    ts(r("AB", a, b), r("XG", a, b), 0.0, A.max, 2.0, A.mult)
+                    sums("XG", j, j + 1, r("BO", 8, 16), False)
+            for j0, j1 in PARTS:
+                if j1 == j + 1:
+                    sums("AB", j0, j1, r("BO", 0, 8), True)
+        scan(r3("PM", e), r("RS"), key, A.add, A.min)
+        stp, wr = r("STP", 152 * f, 152 * f + 152), ps(f, 128, 136)
+        tt(stp, key, r3("PM", e), A.not_equal)
         scan(r3("CS", e), ee, stp, A.add, A.mult)
-        t2w(f, 256, r3("CS", e), LBC, lo)
-        key_end = lambda e: r3("PM", e, 18, 145, 18)
-        c_end = lambda e: r3("CS", e, 17, 144, 18)
-        if h == 1:
-            tt(sm(368 + o, 8), key_end(e), key_end(f), A.is_lt)
-            tt(sm(384 + o, 8), c_end(e), c_end(f), A.subtract)
-            tt(sm(288 + o, 8), key_end(e), key_end(f), A.min)
-            tt(sm(400 + o, 8), sm(384 + o, 8), sm(368 + o, 8), A.mult)
-            tt(sm(416 + o, 8), sm(400 + o, 8), c_end(f), A.add)
-        if end:
-            cl = r("L16", 48 + o, 56 + o)
-            cp(cl, ps(f, 256, 264))
-            tt(sm(464 + o, 8), ps(f, 256, 264), sm(o, 8), A.subtract)
-            ts(r("BD", o, o + 8), key_end(e), -31.5, A.add, 1.0 / 64, A.mult)
-            act(c("GSC"), ind(r("ST"), cl), F.Copy)
-            mm([(ps(f, 272, 280), c("GSC"), r("SELT"), True, True)])
-            tt(sm(816 + o, 8), r("BD", o, o + 8), sm(320 + o, 8), A.add)
-            tt(sm(544 + o, 8), sm(816 + o, 8), ps(f, 272, 280), A.is_lt)
-        else:
-            l1, l2 = r("L16", hL + o, hL + o + 8), r("L16", mpL + o, mpL + o + 8)
-            cp(l1, ps(f, 256, 264))
-            act(c("GM"), ind(r("ST"), l1), F.Copy)
-            r2w(f, 0, [(SELMP, c("GM"))], c("SC"))
-            cp(l2, r("SC", lo + 15, hi, 16))
-            tt(c("YS"), ind(r("Q"), l2), c("A2"), A.add)
-            ts(c("Y2"), c("YS"), M2, A.add, M2, A.subtract)
+        tt(c("XH"), ind(r3("CS", e), LBC), r("RM", 0, 128), A.mult)
+        mm([(wr, c("XH"), Q8, True, True)])
+        if not end:
+            ts(lst(hL, f), wr, 2048.0, A.add)
+            act(c("GM"), ind(r("ST"), lst(hL, f)), F.Copy)
+            r2w(f, 256, [(SELMP, c("GM"))], c("SC"))
+            ts(lst(mpL, f), r("SC", lo + 15, hi, 16), 2048.0, A.add)
+            tt(c("Y"), ind(r("Q"), lst(mpL, f)), c("A2"), A.add)
+            return
+        cl = lst(cL, f)
+        ts(cl, wr, 2048.0, A.add)
+        tt(sm(464 + o, 8), wr, sm(48 + o, 8), A.subtract)
+        bd, nk, z = r("BD", o, o + 8), sm(592 + o, 8), ps(f, 256, 384)
+        x2 = lambda j: r("X2", lo + j, hi, 16)
+        ts(bd, key_end(e), -31.5, A.add, 1.0 / 64, A.mult)
+        ts(x2(15), key_end(e), 8.0, A.add, 2.0 ** 19, A.mult)
+        ts(x2(12), bd, M64, A.add, M64, A.subtract)
+        tt(x2(13), bd, x2(12), A.subtract)
+        act(c("GSC"), ind(r("ST"), cl), F.Copy)
+        ts(c("GB"), ind(r("BITS"), cl), col(82 + t), A.add)
+        mm([(z, c("X2"), r("IDf"), True, False), (z, c("X3"), r("IDb"), False, False)])
+        mm([(z, r("SELJ"), c("GSC"), False, True)], acc=True)
+        tt(c("U2"), c("GB"), z, A.max)
+        ts(r("GB", 256 + lo, 256 + hi), c("GB"), col(81), A.mult)
+        cp(ind(r("K1"), lst(aS, f)), c("U2"))
+        ts(nk, bd, 256.0, A.mult, sm(96 + o + t, 1), A.add)
+        ts(sm(608 + o, 8), nk, 12 * BETA * BETA + (t + 1) ** 2 - 1.0 - (t + 1) * TAG, A.add)
+        tt(c("XE"), ind(sm(608 + o, 8), LCOL), r("RM", 0, 128), A.mult)
+        mm([(ps(6, 256 + o, 264 + o), c("XE"), r("Q8f"), True, True)])
 
-    def swap(o, m, src, first=True):
-        b, lo = o
-        return [(ps(b, lo, lo + 96, 2), m, src(1), first, first), (ps(b, lo + 1, lo + 96, 2), m, src(0), first, True)]
+    def swap(b, lo, n, m, src, first, last):
+        return [(ps(b, lo, lo + n, 2), m, src(1), first, first), (ps(b, lo + 1, lo + n, 2), m, src(0), first, last)]
+
+    def put_out(out, b, n, sel, o):
+        mm([(ps(b, 0, n), r(sel, 15 - j, 143 - j), r("ST", n * j, n * j + n), j == 0, j == 15) for j in range(16)])
+        act(r("BLD", o, o + n), ps(b, 0, n), bias=col(12))
+        dma("y", out, T.BLD[:, o:o + n], [r("BLD", o, o + n)], [], 2500)
 
     later = [None]
     lanes(0)
+    start_mates()
     for t in range(RO):
         last = t == RO - 1
-        act(r("QA"), ind(r("Q"), aL), F.Copy)
-        act(r("GSA"), ind(r("ST"), aL), F.Copy)
-        mm([(ps(7, 0, 256), r("XP"), r("QA"), True, True)])
-        mm([(ps(6, 0, 256), SELID, r("GSA"), True, True)])
-        act(r("AX_"), ps(7, 0, 256), F.Copy)
-        act(r("A2"), ps(7, 0, 256), F.Identity, bias=col(15))
-        for f in (1, 0):
-            act(r("QAM", 128 * f, 128 * f + 32 * NS[f]), r("QA", 128 * f, 128 * f + 32 * NS[f]), F.Copy)
-        for i in range(16):
-            o = (T.AREP[:, i:4096:16], "AREP", 0, 4096, i, 256)
-            if i < A_S:
-                act(o, r("AX_"), F.Copy)
-            else:
-                cp(o, r("AX_"))
+        for f in FIRST:
+            lo, hi = 128 * f, 128 * f + 128
+            bonus[0] = SKEW * (f == FIRST[0])
+            al, ax = lst(aL, f), ps(7, 256 + lo, 256 + hi)
+            ts(r("Y", lo, hi), ind(r("Q"), al), 2.0, A.mult, OFFX, A.add)
+            act(r("QA", lo, hi), ind(r("Q"), al), F.Copy)
+            mm([(ax, r("XP"), r("QA", lo, hi), True, True)])
+            rep = lambda i: (T.AREP[:, 16 * lo + i:16 * hi:16], "AREP", 16 * lo, 16 * hi, i, 128)
+            for i in range(16):
+                if i < A_S:
+                    act(rep(i), ax, F.Copy)
+                else:
+                    cp(rep(i), rep(0))
+            act(r("A2", lo, hi), ax, bias=OFFA)
+            act(r("GSA", lo, hi), ind(r("ST", 0, 2048), al), F.Copy)
+            mm([(ps(6, lo, hi), SELID, r("GSA", lo, hi), True, True)])
+        bonus[0] = 0.0
         if t:
             later[0]()
-        else:
-            start_mates()
         for h in range(HO):
-            for f in (1, 0):
-                bonus[0] = SKEW * f
-                hop(h, f)
+            for f in FIRST:
+                bonus[0] = SKEW * (f == FIRST[0])
+                hop(t, h, f)
             bonus[0] = 0.0
             if h == 0:
                 if t == 0:
                     late_constants()
-                tt(sm(352), sm(272), sm(64), A.is_le)
-                ts(sm(320), sm(352), 8192.0, A.mult)
-                act(r("GA"), ind(r("BITS"), aL), F.Copy)
-                ts(r("U1", 512, 768), r("GA"), col(49), A.mult)
-                ts(r("U1", 768, 1024), r("GA"), col(50), A.mult)
-        bd = r("BD", 0, 16)
-        act(r("GB"), ind(r("BITS"), cL), F.Copy)
-        act(r("QC"), ind(r("Q"), cL), F.Copy)
-        ts(sm(512), bd, -4096.0, A.add)
-        ts(sm(784), sm(512), M64, A.add, M64, A.subtract)
-        tt(sm(800), sm(512), sm(784), A.subtract)
-        mset(r("X2", 15, 256, 16), float(RO - 1 - t))
-        prop, dq, kb, kv = sm(544), sm(560), sm(592), sm(624)
-        tt(r("X2", 12, 256, 16), sm(784), prop, A.mult)
-        tt(r("X2", 13, 256, 16), sm(800), prop, A.mult)
-        tt(dq, sm(512), prop, A.mult)
-        mm([(ps(4, 128 * f, 128 * f + 128), r("X2", 128 * f, 128 * f + 128), r("IDb"), True, True) for f in range(2)])
-        ts(sm(576), dq, 256.0, A.mult)
-        tt(kb, sm(576), sm(64), A.add)
-        ts(r("U1", 0, 256), r("GB"), col(49), A.mult)
-        ts(r("U1", 256, 512), r("GB"), col(50), A.mult)
-        tt(r("U2"), r("GB"), ps(4, 0, 256), A.mult)
-        ts(sm(608), kb, 6 * B20 + (RO - 1 - t) * TAG - BIG, A.add)
-        tt(kv, sm(608), prop, A.mult)
-        tt(r("RP"), ind(kv, LCOL), r("RM"), A.mult)
-        nv = ns = 0
-        order = sorted(range(16), key=lambda j: (j * 16 // (16 - V_PAIR)) if j < 16 - V_PAIR else (j - 16 + V_PAIR) * 16 // V_PAIR + 2)
-        for j in order:
-            f, k = divmod(j, 8)
-            p = slice(32 * (k // 2), 32 * (k // 2) + 32)
-            u0 = 256 * (k % 2) + 128 * f
-            if j >= 16 - V_PAIR:
-                b, nv = 2 + nv % 2, nv + 1
-            else:
-                b, ns = ns % 2, ns + 1
-            mm([(ps(b, 256 * x, 256 * x + 256), r("U1", u0 + 512 * x, u0 + 512 * x + 128, p=p), r("U2", p=p), True, True) for x in range(2)])
-            if j >= 16 - V_PAIR:
-                o, a = sm(640 + j, 1), ps(b)
-                add("v", [lambda o=o, a=a: g.vector.tensor_reduce(o[0], a[0], AX.X, A.min)], [a], [o], 536)
-            else:
-                act(r("JUNK", 512 * b, 512 * b + 512), ps(b), F.Relu, bias=sm(592 + j, 1), scale=-1.0, accum=r("LS", j, j + 1))
-        cp(ind(r("K1"), aS), r("U2"))
-        act(r("GK"), ind(r("K1"), cL), F.Copy)
-        r2w(4, 256, [(r("KSEL"), r("GK"))], r("SC", 0, 256), "NRB")
+                act(r("GA", 0, 256), ind(r("BITS"), lst(aL)), bias=col(82 + t))
+                ts(r("GA", 256, 512), r("GA", 0, 256), col(81), A.mult)
+        act(r("GK"), ind(r("K1"), lst(cL)), F.Copy)
+        r2w(4, 256, [(r("KSEL"), r("GK"))], r("SC", 0, 256))
         r2w(7, 0, [(SELP, r("GSC"))], r("SC", 256, 512))
-        tt(sm(480), r("SC", 271, 512, 16), LW, A.subtract)
-        tt(r("LS", 16 - V_PAIR, 16), sm(608 - V_PAIR, V_PAIR), sm(656 - V_PAIR, V_PAIR), A.subtract)
-        ts(sm(656), r("LS"), 0.0, A.is_equal)
-        t2w(3, 0, sm(656), LCOL, 256, r("RP"))
-        stand = r("TMP", 0, 16)
-        tt(stand, ps(3, 0, 16), r("SC", 15, 256, 16), A.is_lt)
-        tt(r("TMP", 48, 96), ind(stand, LPR), sm(448, 48), A.mult)
+        tt(sm(480), r("SC", 271, 512, 16), LWm, A.subtract)
+        w2 = sm(544)
+        tt(w2, ps(6, 256, 272), r("SC", 15, 256, 16), A.is_lt)
+        tt(sm(688, 48), ind(w2, LPR), sm(448, 48), A.mult)
+        nv = ns = 0
+        for f in FIRST:
+            o, v = 8 * f, V_PAIR[f]
+            for k in sorted(range(8), key=lambda k: k * 8 / (8 - v) if k < 8 - v else (k - 8 + v) * 8 / v + 0.5):
+                p = slice(16 * k, 16 * k + 16) if k % 2 == 0 else slice(16 * k - 16, 16 * k + 16)
+                u0 = 256 * (k % 2) + 128 * f
+                if k >= 8 - v:
+                    b, nv = 2 + nv % 2, nv + 1
+                else:
+                    b, ns = ns % 2, ns + 1
+                mm([(ps(b, 256 * x, 256 * x + 256), r(("GB", "GA")[x], u0, u0 + 128, p=p), r("U2", p=p), True, True) for x in range(2)])
+                if k >= 8 - v:
+                    red(sm(640 + o + k, 1), ps(b), A.max)
+                else:
+                    act(r("JUNK", 512 * b, 512 * b + 512), ps(b), F.Relu, bias=sm(592 + o + k, 1), accum=r("LS", o + k, o + k + 1))
+            tt(r("LS", o + 8 - v, o + 8), sm(648 + o - v, v), sm(600 + o - v, v), A.add)
+            xs_ = r("XS", 128 * f, 128 * f + 128)
+            tt(xs_, ind(r("LS", o, o + 8), LCOL), r("RMH"), A.is_equal)
+            mm([(ps(6, 272 + 16 * j + o, 280 + 16 * j + o), xs_, Q8, True, True) for j in range(3)])
+        act(r("QC"), ind(r("Q"), lst(cL)), F.Copy)
+        tt(r("TMP", 48, 96), ps(6, 272, 320), sm(688, 48), A.mult)
         tt(r("TMP", 96, 144), r("TMP", 48, 96), sm(0, 48), A.add)
         cp(r("P16", 0, 48), r("TMP", 96, 144))
         jA, jC, jO = r("P16", 0, 16), r("P16", 16, 32), r("P16", 32, 48)
-        tt(sm(752), live, stand, A.subtract)
-        mm([(ps(6, 256, 512), r("PO"), r("GSC"), True, True)])
-        act(r("YS"), ps(6, 256, 512), F.Identity, bias=col(54))
+        tt(sm(736), ps(6, 272, 288), w2, A.mult)
+        tt(sm(752), live, sm(736), A.subtract)
+        tt(sm(768), sm(752), sm(80), A.mult)
+        mm([(ps(4, 0, 256), r("PO"), r("GSC"), True, True)])
+        act(r("YS"), ps(4, 0, 256), bias=col(90))
         for j, (x, z) in enumerate((("GSC", "GSA"), ("GSA", "GSC"))):
             o = ps(5, 256 * j, 256 * j + 256)
-            mm([(o, r("KEEP"), r(x), True, False)])
-            mm([(o, r("SHIFT"), r(z), False, False)], acc=True)
-            mm([(o, r("DM"), r("U2"), False, True)], acc=True)
-        act(r("VV"), ps(5), F.Identity, bias=col(53))
+            mm([(o, r("KEEP"), r(x), True, False), (o, r("SHIFT"), r(z), False, False), (o, r("DM"), r("U2"), False, True)])
+        act(r("VV"), ps(5), F.Copy)
         mm([(ps(7, 0, 256), r("XP"), r("QC"), True, False), (ps(7, 0, 256), r("nIDb"), r("QA"), False, True)])
         mm([(ps(7, 256, 512), r("XP"), r("QA"), True, False), (ps(7, 256, 512), r("nIDb"), r("QC"), False, True)])
         act(r("SGN"), ps(7), F.Sign)
         cp(ind(r("ST"), jO), r("YS"))
         cp(ind(r("ST"), jC), r("VV", 0, 256))
-        act(r("GS2"), ind(r("ST"), aL), F.Copy)
+        act(r("GS2"), ind(r("ST"), lst(aL)), F.Copy)
         cp(ind(r("ST"), jA), r("VV", 256, 512))
         if last:
-            dma("y", T.yp[:], T.ST[1:128:16, 0:4096], [r("ST", 0, 4096, row=1)], [], 2500)
-        r2w(7, 0, [(r("SELLO"), r("GS2"))], r("SC", 0, 256))
+            put_out(T.yp[:], 0, 256, "B23", 0)
+        r2w(4, 0, [(SELLO, r("GS2"))], r("SC", 0, 256))
+        t1 = r("T16", 0, 16)
         tt(r("RF"), r("SC", 15, 256, 16), sm(752), A.mult)
-        mm([(ps(7, 256, 272), r("BLKb"), r("RF"), True, True), (ps(7, 272, 288), r("TMB"), r("RF"), True, True)])
-        cc = sm(288)
-        scan(cc, r("ONES", 0, 16), ps(7, 256, 272), A.mult, A.add)
-        tt(sm(336), r("RF"), sm(80), A.mult)
-        tt(sm(352), sm(96), sm(336), A.subtract)
-        tt(sm(368), ps(7, 272, 288), sm(352), A.add)
-        tt(sm(384), sm(368), cc, A.add)
+        tt(t1, r("SC", 15, 256, 16), sm(768), A.mult)
+        mm([(ps(4, 256, 272), r("TRIB"), r("RF"), True, False), (ps(4, 257, 272), r("NTM"), r("RF", 0, 15), False, False),
+            (ps(4, 256, 272), r("nIDb"), t1, False, False), (ps(4, 257, 272), r("IDb"), r("T16", 0, 15), False, True),
+            (ps(4, 272, 288), r("BLKb"), r("RF"), True, True)])
+        scan(sm(384), r("C16B"), ps(4, 256, 272), A.add, A.add, col(94))
         cp(dL, sm(384))
+        n = sm(303, 1)
+        red(n, ps(4, 272, 288), A.add)
         cp(ind(r3("SBQ", t), dL), r("QA"))
         tr = []
         for d in range(1, NR):
@@ -631,52 +732,58 @@ def build(g, T, topo, core):
         tt(ind(r("Q"), jC), r("SGN", 256, 512), r("QC"), A.add)
         if not last:
             lanes(t + 1)
-        n = sm(303, 1)
-        r2w(3, 0, [(SELID, r("SG", 0, 96)), (SELM, r("SG", 0, 96))], r("SC", 256, 448))
+        r2w(5, 288, [(SELID, r("SG", 0, 96)), (SELM, r("SG", 0, 96))], r("SC", 256, 448))
         ts(sm(512, 18), sm(112, 18), n, A.is_lt)
         ts(r("KR", 96, 192), r("KR", 0, 96), n, A.is_lt)
-        tt(sm(544, 12), r("SC", 271, 448, 16), sm(130, 12), A.subtract)
+        tt(sm(544, 12), r("SC", 271, 448, 16), sm(148, 12), A.subtract)
         tt(sm(560, 6), sm(544, 6), sm(512, 6), A.mult)
         tt(sm(566, 12), sm(544, 12), sm(518, 12), A.mult)
         tt(sm(592, 18), sm(560, 18), sm(130, 18), A.add)
         cp(r("L16", kL, kL + 18), sm(592, 18))
         sL, vsL, vmL, pmL = [r("L16", kL + 6 * j, kL + 6 * j + 6) for j in range(4)]
         act(r("QM", 0, 96), ind(r("Q"), vmL), F.Copy)
-        act(r("SGK"), r("SG", 0, 96), F.Copy, scale=col(57))
         sg = lambda j: r("SG", j, 96, 2)
-        for j in range(3):
-            mm(swap((5, 96 * j), r("MSW", 128 * j, 128 * j + 128), sg))
+        mm(swap(5, 0, 96, r("MSW", 0, 128), sg, True, True) + swap(5, 96, 96, r("MSW", 128, 256), sg, True, True) +
+           [(ps(5, 192, 288), r("MSW", 384, 512), r("SG", 0, 96), True, False)] +
+           swap(5, 192, 96, r("MSW", 256, 384), sg, False, True))
         act(r("SW"), ps(5, 0, 288), F.Copy)
-        mm([(ps(4, 0, 96), r("LOW"), r("QM", 0, 96), True, False)] + swap((4, 0), r("UP"), lambda j: r("QM", j, 96, 2), False))
+        mm([(ps(4, 0, 96), r("LOW"), r("QM", 0, 96), True, False)] + swap(4, 0, 96, r("UP"), lambda j: r("QM", j, 96, 2), False, True))
         act(r("QM", 96, 192), ps(4, 0, 96), F.Copy)
         cp(ind(r("Q"), vmL), r("QM", 96, 192))
-        own = r3("SBQ", t, 0, 96)
-        mm([(ps(7, 32 * j, 32 * j + 32), r("ROT", 128 * j, 128 * j + 128), r3("LAND", t, 32 * j, 32 * j + 32), True, True)
-            for j in range(NR - 1)])
-        ts(r("TQ"), ps(7, 0, 96), 0.0, A.is_ge)
-        tt(r("TMP", 160, 256), ps(7, 0, 96), own, A.subtract)
-        tt(r("TMP", 256, 352), r("TMP", 160, 256), r("TQ"), A.mult)
-        tt(r("R5"), r("TMP", 256, 352), own, A.add)
-        mm([(ps(7, 128, 224), r("nUP"), r("R5"), True, False)] + swap((7, 128), r("UP"), lambda j: r("R5", j, 96, 2), False))
-        tt(r("TQ"), ps(7, 128, 224), r("KR", 96, 192), A.mult)
-        tt(ind(r("Q"), sL), r("TQ"), r("R5"), A.add)
+        m3 = lambda name, j: r("ROT", 384 * ("ROT", "RN", "RU", "nRU").index(name) + 128 * j,
+                               384 * ("ROT", "RN", "RU", "nRU").index(name) + 128 * j + 128)
+        land = lambda j, x=0, s=1: r3("LAND", t, 32 * j + x, 32 * j + 32, s)
+        mm([(ps(7, 0, 96), r("IDb"), r3("SBQ", t, 0, 96), True, False)])
+        mm([(ps(7, 32 * j, 32 * j + 32), m3("RN", j), land(j), False, j == 2) for j in range(3)], acc=True)
+        ts(r("RR"), ps(7, 0, 96), -255.0, A.add, 0.0, A.max)
+        mm([(ps(6, 320, 416), ZERO, ones(96), True, False)])
+        mm([(ps(6, 320 + 32 * j, 352 + 32 * j), m3("ROT", j), land(j), False, False) for j in range(3)], acc=True)
+        mm([(ps(6, 320, 416), r("IDb"), r("RR"), False, True)], acc=True)
+        act(r("RA"), ps(6, 320, 416), F.Copy)
+        mm([(ps(4, 384, 480), ZERO, ones(96), True, False)])
+        mm([x for j in range(3) for x in [(ps(4, 384 + 32 * j, 416 + 32 * j), m3("nRU", j), land(j), False, False)] +
+            swap(4, 384 + 32 * j, 32, m3("RU", j), lambda x, j=j: land(j, x, 2), False, False)], acc=True)
+        mm([(ps(4, 384, 480), r("nUP"), r("RR"), False, False)] +
+           swap(4, 384, 96, r("UP"), lambda j: r("RR", j, 96, 2), False, True), acc=True)
+        tt(r("TQ"), ps(4, 384, 480), r("KR", 96, 192), A.mult)
+        tt(ind(r("Q"), sL), r("TQ"), r("RA"), A.add)
         if last:
             dma("y", T.yq[:, 0:2048], T.Q[:, 0:2048], [r("Q", 0, 2048)], [], 4000)
             dma("s", T.yq[:, 2048:4096], T.Q[:, 2048:4096], [r("Q", 2048, 4096)], [], 4000)
-        tt(ind(r("ST"), vsL), r("SGK"), r("SW", 192, 288), A.add)
+        cp(ind(r("ST"), vsL), r("SW", 192, 288))
         if last:
-            dma("y", T.ym[:], T.ST[2:128:16, 0:2048], [r("ST", 0, 2048, row=2)], [], 2500)
+            put_out(T.ym[:], 1, 128, "B45", 256)
         else:
             def mend(vmL=vmL, pmL=pmL):
                 gm, gp = r("GMM", 0, 96), r("GMM", 96, 192)
-                act(gm, ind(r("ST"), vmL), F.Copy, scale=col(55))
+                act(gm, ind(r("ST"), vmL), F.Copy, scale=col(91))
                 tt(ind(r("ST"), vmL), gm, r("SW", 0, 96), A.add)
-                r2w(3, 256, [(SELP, gm)], r("SC", 512, 608))
-                tt(sm(624, 6), r("SC", 527, 608, 16), sm(130, 6), A.subtract)
+                r2w(4, 0, [(SELP, gm)], r("SC", 512, 608))
+                tt(sm(624, 6), r("SC", 527, 608, 16), sm(148, 6), A.subtract)
                 tt(sm(632, 6), sm(624, 6), sm(518, 6), A.mult)
                 tt(sm(640, 6), sm(632, 6), sm(130, 6), A.add)
                 cp(pmL, sm(640, 6))
-                act(gp, ind(r("ST"), pmL), F.Copy, scale=col(56))
+                act(gp, ind(r("ST"), pmL), F.Copy, scale=col(92))
                 tt(ind(r("ST"), pmL), gp, r("SW", 96, 192), A.add)
             later[0] = mend
     return ops

@@ -1,15 +1,27 @@
+import math
 from concourse.bass import DstId, RemoteDMATransfer
 from concourse.mybir import AluOpType as A, AxisListType as AX, ActivationFunctionType as F
 
 RO, HO, STEP, NR = 5, 3, 341, 4
 WD = 4352
-MODES = ("SVMS", "SVMS")
+STREAMS = ((0, 128), (128, 256))
+CUTS = ((0, 32, 64, 96, 128),) * 2
+STEPS = "g0 s2 g3 s1 a0 r1 a2 a3"
+LAST_STEPS = "g0 s2 g3 s1 a0 r2 r1 a3"
+STAGE = (4, 5, 7)
+GM_V = False
+EARLY = 9000.0
+TEMPLATE = {"v": "s2a' tH'' s1a' s1b' sM'' tM'' Y'' r1' sU tU C s2b PM' CF NE' EQ CS' XH'", "s": "a3' g3 g0 GM' a0 a2"}
+PAIRS = ([("s", (3,), (0, 1, 2, 3, 4, 5)), ("v", (2, 0), (6, 7))], [("v", (2, 0), (0, 1, 2, 3, 4, 5, 6, 7))],
+         [("s", (3, 1, 5), (0, 1, 2, 3)), ("v", (2, 0, 4), (4, 5, 6, 7))],
+         [("s", (3, 1, 5), (0, 2, 4, 6)), ("v", (2, 0, 4), (1, 3, 5, 7))])
 PARTS = ((0, 3), (3, 4))
-S_IND = 3
-V_PAIR = (4, 3)
-A_S = 3
-FIRST = (0, 1)
-LOOK, SKEW, SAME, CROSS, PE = 150.0, 800.0, 60.0, 120.0, 0.5
+S_IND = (5, 8, 8)
+A_RUNS = STREAMS
+A_S = (5, 6)
+V_CUT = 256
+LOOK, SKEW, SAME, CROSS, PE = 250.0, 800.0, 100.0, 180.0, 0.5
+WINDOW, TRIES, SWEEPS, HEAT = 140, 6000, 2, 60.0
 TAG = float(1 << 21)
 BETA = 1024.0
 M64 = 1.5 * 2.0 ** 29
@@ -26,15 +38,15 @@ def _decl(dt_, spec):
 
 
 _decl("bfloat16", "Q:4352 ST:4352 K1:4352 BITS:4096 XG:4096 AB:4096 AREP:4096 MT:4096 MPP:4096 AV:2048 SBQ:5x768 "
-      "LAND:5x96 SG:768 P0:512 BH:1024 IDb:128 nIDb:128 BLKb:128 XP:128 I65:152 DIFF:152 MRH:456 RS:152 RESET:256 "
-      "NRM:256 RM:256 RMH:128 NM:128 MC:384 ONES:512 Q8:16 BO:16 B2:144 B0:144 B10:144 B23:144 B45:144 TRI:128 TRIx:128 "
-      "TRIB:128 NTM:128 SEL:640 SELJ:128 KSEL:128 DM:128 KEEP:128 SHIFT:128 PO:128 MSW:512 ROT:1536 "
-      "UP:128 nUP:128 LOW:128 STP:304 X3:256 QA:256 QC:256 GSA:256 GSC:256 GM:256 GS2:256 EQ:256 GA:512 "
+      "LAND:5x96 SG:768 BH:1024 IDb:128 nIDb:128 BLKb:128 XP:128 I65:152 DIFF:152 MRH:456 RS:152 RESET:256 "
+      "NRM:256 RM:256 RMH:128 NM:128 MC:512 ONES:512 Q8:24 BO:16 B2:144 B0:144 B10:144 B23:144 B45:144 TRI:128 TRIx:128 "
+      "TRIB:128 NTM:128 SEL:640 SELJ:128 DG:640 DM:128 KEEP:128 SHIFT:128 PO:256 MSW:640 ROT:1536 "
+      "UP:384 STP:456 X3:384 QA:256 QC:256 GSA:256 GSC:256 GM:256 GS2:256 EQ:256 GA:512 MR:256 MG:256 DJ:128 "
       "GB:512 U2:256 GK:256 SGN:512 JUNK:1024 YS:256 VV:512 FW:128 CTX:128 IND:16x128 JB3:16x16 IND2:256 XS:256 "
-      "RF:16 RR:96 RA:96 TQ:96 QM:192 SW:288 GMM:192 KR:192 C16B:16")
-_decl("float16", "RW:4096 W16:512 Y:256 CF:256 XH:256 KM:128 H16:768 T16:32")
-_decl("float32", "CT:4112 JF:256 MR:256 MG:256 DJ:128 COL:96 IDf:128 BLKf:128 Q8f:8 TMP:512 BLD:768 A2:256 PM:6x152 "
-      "CS:6x152 XE:256 X2:256 SC:1024 SM:832 LS:16 PFW:136")
+      "RF:16 RR:96 RA:96 TQ:96 QM:192 SW:288 GMM:192 KR:192 C16B:32")
+_decl("float16", "RW:4096 W16:512 Y:256 CF:256 XH:384 KM:128 H16:768 T16:32 T80:64")
+_decl("float32", "CT:4112 JF:256 COL:128 IDf:256 BLKf:128 CN:128 Q8f:8 TMP:512 BLD:768 A2:256 PM:9x152 "
+      "CS:9x152 X2:384 SC:1024 SM:832 LS:96 LW2:96 LO:96 PFW:136")
 _decl("int32", "IB:400 SI:512 BD:32 PI:32")
 _decl("uint16", "C16:256 L16:192 P16:384")
 for _b in range(8):
@@ -66,9 +78,8 @@ def build(g, T, topo, core):
         w = T[name].shape[2]
         return (T[name][:, i0:i1, lo:hi], name, i0 * w, i1 * w, None, (i1 - i0) * (hi - lo))
 
-    def r3c(name, i0, i1, c):
-        w = T[name].shape[2]
-        return (T[name][:, i0:i1, c], name, i0 * w, i1 * w, None, i1 - i0)
+    def blk(name, j, n=128):
+        return r(name, n * j, n * j + n)
 
     def ind(win, off):
         return (win[0].indirect(off[0]), win, off, 16 * off[5])
@@ -149,12 +160,22 @@ def build(g, T, topo, core):
             c += 10 + PE * max(min(64, l[5]), rr[5]) * (1 if two(l) else 4)
         add("t", fns, rd, wr, c, acc=acc)
 
+    def mms(items, n=4):
+        for j in range(0, len(items), n):
+            mm(items[j:j + n], acc=j > 0 or not items[0][3])
+
     def iota(out, pat, base=0, cm=0):
         if SCRATCH[out[1]][2] == "int32":
             fn = lambda: g.iota(out[0], pat, base, cm)
         else:
             fn = lambda: g.iota(out[0], pat, base, cm, allow_small_or_imprecise_dtypes=True)
         add("g", [fn], [], [out], 130 + 2 * out[5])
+
+    def fill(out, v):
+        iota(out, [[0, out[5]]], v)
+
+    def select(out, a, k, op=A.is_equal, other=0.0, sign=1):
+        add("g", [lambda: g.affine_select(out[0], a[0], [[sign, out[5]]], op, other, -sign * k, -sign)], [a], [out], 170 + 2 * out[5])
 
     nd = [0]
 
@@ -176,14 +197,17 @@ def build(g, T, topo, core):
     def col(i, n=1):
         return r("COL", i, i + n)
 
-    def sm(lo, n=16):
-        return r("SM", lo, lo + n)
+    def sm(lo, n=16, step=1):
+        return r("SM", lo, lo + n * step, step)
 
     def oh(f):
         return col(16 + f)
 
+    def scaled(out, a, s):
+        act(out, a, F.Copy, scale=s)
+
     one = slice(0, 1)
-    Mp, Mn, ZERO = (r("MC", 128 * j, 128 * j + 128, p=one) for j in range(3))
+    Mp, Mn, ZERO, M4K = (r("MC", 128 * j, 128 * j + 128, p=one) for j in range(4))
 
     def ones(n):
         return r("ONES", 0, n, p=one)
@@ -191,299 +215,290 @@ def build(g, T, topo, core):
     bonus[0] = 20000.0
     dma("y", T.IB[:, 0:256], T.pr[:], [], [r("IB", 0, 256)], 2000)
     dma("g", T.IB[:, 384:385], T.w[:], [], [r("IB", 384, 388)], 2000, True)
+    dma("y", T.IB[:, 256:384], T.mt[:], [], [r("IB", 256, 384)], 2000)
     dma("g", T.IB[:, 388:389], T.kk[:], [], [r("IB", 388, 392)], 2000, True)
     mset(r("IB", 392, 396), 0)
     dma("g", T.IB[8:128:16, 392:393], T.th[:], [], [r("IB", 392, 396)], 2000, True)
-    dma("y", T.IB[:, 256:384], T.mt[:], [], [r("IB", 256, 384)], 2000)
     dma("s", T.Q[:, 0:2048], T.rec[:, 0:2048], [], [r("Q", 0, 2048)], 4500)
     dma("y", T.Q[:, 2048:4096], T.rec[:, 2048:4096], [], [r("Q", 2048, 4096)], 4500)
-    JB3 = lambda f: r3s("JB3", 8 * f, 8 * f + 8, 0, 16)
+    NS = len(STREAMS)
     bonus[0] = 9000.0
     iota(r("PI", 0, 1), [[0, 1]], 0, 1)
     iota(r("JF"), [[1, 256]])
-    iota(r("DJ"), [[1, 128]], 0, -1)
     iota(r("MG"), [[1, 16], [0, 16]])
     iota(r("MR"), [[0, 16], [1, 16]])
-    iota(r("BH", 0, 512), [[64, 8], [0, 64]])
-    iota(r("BH", 512, 1024), [[0, 8], [1, 64]])
+    iota(r("DJ"), [[1, 128]], 0, -1)
+    bonus[0] = EARLY
     iota(r3s("JB3", 0, 16, 0, 16), [[1, 256]])
-    bonus[0] = 0.0
-    for h in range(HO):
-        iota(r("MRH", 152 * h, 152 * h + 152), [[0, 8], [1, KW]], 16 * h - 2)
     PF, PR, PG = col(0), col(1), col(2)
-    DJ = r("DJ")
+    DJ, ID = r("DJ"), r("IDb")
+    mset(r("ST"), 0.0)
+    dma("y", T.MT[:, 0:2048], T.rec[:, 0:2048], [], [r("MT", 0, 2048)], 4500)
     ts(r("PI", 1, 2), r("PI", 0, 1), 15, A.bitwise_and)
     ts(r("PI", 2, 3), r("PI", 0, 1), 4, A.logical_shift_right)
     ts(r("PI", 3, 4), r("PI", 0, 1), 7, A.bitwise_and)
     cp(col(0, 4), r("PI", 0, 4))
     ts(col(16, 16), r("JF", 0, 16), PR, A.is_equal)
     mset(r("ONES"), 1.0)
-    mset(r("MC", 0, 128), M4096)
-    mset(r("MC", 128, 256), -M4096)
-    mset(r("MC", 256, 384), 0.0)
-    for i, v in ((10, 2047.5), (11, -2048.0), (12, 2048.0)):
-        mset(col(i), v)
+    for j, v in enumerate((M4096, -M4096, 0.0, 4096.0)):
+        mset(r("MC", 128 * j, 128 * j + 128, p=one), v)
     ids, xs = r("BLD", 0, 256), r("BLD", 256, 640)
-    ts(col(4), PR, 256.0, A.mult)
-    ts(ids, r("JF"), col(4), A.add)
-    bonus[0] = 9000.0
+    scaled(col(4), PR, 256.0)
+    act(ids, r("JF"), bias=col(4))
     lob = r("XS")
     tt(lob, r("IB", 0, 256), ids, A.is_equal)
-    flc = r("MPP", p=slice(0, 8))
-    rows(flc, lob)
-    bonus[0] = 0.0
-    ts(r("IDb"), DJ, 0.0, A.is_equal)
-    ts(r("IDf"), DJ, 0.0, A.is_equal)
+    rows(r("MPP", p=slice(0, 8)), lob)
+    ts(ID, DJ, 0.0, A.is_equal)
+    scaled(blk("IDf", 0), ID, 1.0)
+    scaled(blk("IDf", 1), ID, -1.0)
+    scaled(r("nIDb"), ID, -1.0)
+    IDf, nIDf = blk("IDf", 0), blk("IDf", 1)
     ts(r("BLKb"), r("MG", 0, 128), PG, A.is_equal)
-    ts(r("BLKf"), r("MG", 0, 128), PG, A.is_equal)
+    scaled(r("BLKf"), r("BLKb"), 1.0)
+    Q8, Q8n, KS8 = r("Q8", 0, 8), r("Q8", 8, 16), r("Q8", 16, 24)
     ts(r("Q8f"), r("JF", 0, 8), PG, A.is_equal)
-    Q8, nQ8 = r("Q8", 0, 8), r("Q8", 8, 16)
-    cp(Q8, r("Q8f"))
-    ts(nQ8, r("Q8f"), -1.0, A.mult)
+    scaled(Q8, r("Q8f"), 1.0)
+    scaled(Q8n, r("Q8f"), -8192.0)
     ts(col(8), PR, 8.0, A.is_ge)
-    ts(col(9), col(8), -16.0, A.mult, 8.0, A.add)
+    act(col(9), col(8), bias=8.0, scale=-16.0)
     ts(r("XP"), DJ, col(9), A.is_equal)
-    OFF, OFFX, OFFA = col(13), col(14), col(15)
-    ts(OFF, col(8), -4608.0, A.mult, 2048.0, A.add)
-    ts(OFFX, col(8), 4608.0, A.mult, -2560.0, A.add)
-    ts(OFFA, OFF, -0.5, A.add)
+    OFF, OFFA = col(13), col(15)
+    act(OFF, col(8), bias=2048.0, scale=-4608.0)
+    act(OFFA, col(8), bias=2047.5, scale=-4608.0)
     cp(col(5, 3), r("IB", 384, 396, 4))
     ts(r("TMP", 0, 1), col(5), 0.5, A.mult, OFF, A.mult)
-    cp(r("TMP", 1, 2), col(7))
+    scaled(r("TMP", 1, 2), col(7), 1.0)
     mm([(ps(7, 0, 2), r("BLKf"), r("TMP", 0, 2), True, True)])
     cp(r("T16", 0, 1), col(5))
-    mm([(ps(7, 2, 3), r("XP"), r("T16", 0, 1), True, True)])
-    ts(col(32), ps(7, 0, 1), -1.0, A.mult, -2048.0, A.add)
-    cp(r("C16B", 0, 1), ps(7, 1, 2))
-    tt(col(33), ps(7, 1, 2), r("C16B", 0, 1), A.subtract)
-    ts(col(34), oh(8), r("C16B", 0, 1), A.mult)
-    THC = col(35)
-    ts(THC, oh(9), col(33), A.mult, col(34), A.add)
-    ts(col(36), col(5), 0.5, A.mult)
-    ts(col(37), col(5), -0.5, A.mult)
-    ts(col(38), ps(7, 2, 3), 0.5, A.mult)
-    ts(col(39), ps(7, 2, 3), -0.5, A.mult)
-    for j in range(4):
-        ts(r("W16", 128 * j, 128 * j + 128), r("BLKb"), col(36 + j), A.mult)
-    bonus[0] = 5000.0
+    mm([(ps(3, 0, 1), r("XP"), r("T16", 0, 1), True, True)])
+    act(col(32), ps(7, 0, 1), bias=-2048.0, scale=-1.0)
+    act(col(14), ps(7, 0, 1), bias=2048.0)
+    scaled(r("C16B", 16, 17), ps(7, 1, 2), 1.0)
+    scaled(col(33), r("C16B", 16, 17), 1.0)
+    tt(col(34), ps(7, 1, 2), col(33), A.subtract)
+    scaled(col(38), ps(3, 0, 1), 1.0)
+    ts(r("CN"), r("ONES", 0, 128), r("TMP", 0, 1), A.mult, -1.0, A.mult)
+    for j, (x, v) in enumerate(((5, 0.5), (5, -0.5), (38, 1.0), (38, -1.0))):
+        ts(blk("W16", j), r("BLKb"), col(x), A.mult, v, A.mult)
     ts(r("SI", 0, 256), ids, col(32), A.add)
     ts(r("SI", 256, 512), r("SI", 0, 256), 4095, A.bitwise_and)
-    cp(r("TMP", 0, 256), r("SI", 256, 512))
+    cp(r("TMP", 256, 512), r("SI", 256, 512))
     ts(r("H16", 0, 256), r("SI", 256, 512), -2048.0, A.add)
-    act(r("TMP", 256, 512), r("TMP", 0, 256), F.Square)
-    ts(r("SI", 0, 256), r("TMP", 256, 512), -12.0, A.add, 1.0 / 32, A.mult)
+    act(r("SC", 0, 256), r("TMP", 256, 512), F.Square)
+    ts(r("SI", 0, 256), r("SC", 0, 256), -12.0, A.add, 1.0 / 32, A.mult)
     ts(r("SI", 256, 512), r("SI", 0, 256), 4095, A.bitwise_and)
     ts(r("H16", 256, 512), r("SI", 256, 512), -2048.0, A.add)
     ts(r("H16", 512, 768), r("ONES", 0, 256), 0.5, A.mult)
     for j in (2, 0, 1):
-        dma("y", T.RW[8 * j:8 * j + 8, :], T.H16[:, 256 * j:256 * j + 256], [r("H16", 256 * j, 256 * j + 256)],
-            [(None, "RW", 0, 4096, j, 4096)], 2500)
-    km = r("T16", 8, 32)
+        dma("y", T.RW[8 * j:8 * j + 8, :], T.H16[:, 256 * j:256 * j + 256], [blk("H16", j, 256)], [(None, "RW", 0, 4096, j, 4096)], 2500)
     ts(r("T16", 24, 32), r("JF", 0, 8), 0.0, A.is_equal)
     ts(r("T16", 8, 16), r("Q8f"), col(6), A.mult)
     cp(r("T16", 16, 24), r("Q8f"))
     ts(r("PI", 4, 5), r("IB", 388, 389), 1, A.bitwise_and)
     ts(r("T16", 25, 26), r("PI", 4, 5), 4096.0, A.mult)
     k24 = slice(0, 24)
-    mm([(ps(6, 0, 128, p=k24), km, r("IDb"), True, True)])
+    mm([(ps(6, 0, 128, p=k24), r("T16", 8, 32), ID, True, True)])
     cp(r("KM", p=k24), ps(6, 0, 128, p=k24))
-    ts(r("H16", 0, 128, p=k24), ps(6, 0, 128, p=k24), -1.0, A.mult)
+    ts(r("Y", 0, 128, p=k24), ps(6, 0, 128, p=k24), -1.0, A.mult)
     for j in range(8):
-        b, x = ps(3 + j % 2), r("RW", 512 * j, 512 * j + 512, p=k24)
-        mm([(b, Mp, ones(512), True, False), (b, r("H16", 0, 128, p=k24), x, False, False),
-            (b, Mn, ones(512), False, False), (b, r("KM", p=k24), x, False, True)])
-        act(r("CT", 512 * j, 512 * j + 512), b, bias=col(10))
-    cp(r("CT", 4096, 4097), r("CT", 0, 1))
-    bonus[0] = 0.0
+        b, x = ps((4, 5, 7)[j % 3]), r("RW", 512 * j, 512 * j + 512, p=k24)
+        mms([(b, Mp, ones(512), True, False), (b, r("Y", 0, 128, p=k24), x, False, False),
+             (b, Mn, ones(512), False, False), (b, r("KM", p=k24), x, False, True)], 1)
+        act(blk("CT", j, 512), b, bias=2047.5)
+    scaled(r("CT", 4096, 4097), r("CT", 0, 1), 1.0)
     ts(xs, r("IB", 0, 384), -2048.0, A.add)
     hi_, lo_ = r("JUNK", 0, 384), r("JUNK", 384, 768)
-    act(hi_, xs, F.Copy)
+    scaled(hi_, xs, 1.0)
     tt(lo_, xs, hi_, A.subtract)
-    ts(r("BH", 0, 512), r("BH", 0, 512), oh(0), A.mult)
-    ts(r("BH", 512, 1024), r("BH", 512, 1024), oh(1), A.mult)
-    tt(r("P0"), r("BH", 0, 512), r("BH", 512, 1024), A.add)
-    ts(r("TMP", 0, 9), r("JF", 0, 9), 512.0, A.mult, -2048.0, A.add)
-    ts(col(40, 9), r("TMP", 0, 9), oh(0), A.mult, THC, A.add)
-    for j in range(9):
-        n = min(512, WD - 512 * j)
-        act(r("ST", 512 * j, 512 * j + n), r("P0", 0, n), bias=col(40 + j))
+    iota(r("GA", 0, 256), [[64, 4], [0, 64]], -2048)
+    act(blk("BH", 0, 256), r("GA", 0, 256), bias=col(4))
+    iota(blk("BH", 1, 256), [[0, 4], [1, 64]])
+    scaled(blk("BH", 2, 256), r("ONES", 0, 256), col(33))
+    scaled(blk("BH", 3, 256), r("ONES", 0, 256), col(34))
+    for j, row in enumerate((0, 1, 8, 9)):
+        rows(r("ST", 0, 4096, row=row), blk("BH", j, 256))
     rows(r("ST", 0, 4096, row=10), lob)
-    mset(r("MT", 0, 2048), 0.0)
     for j, x in enumerate((hi_, lo_)):
         o = x[2]
         dma("y", T.AB[8 * j:8 * j + 8, :], T.JUNK[:, o:o + 256], [x], [(None, "AB", 0, 4096, j, 4096)], 2500)
         rows(r("ST", 0, 4096, row=2 + j), r("JUNK", o, o + 256))
         rows(r("ST", 0, 2048, row=4 + j), r("JUNK", o + 256, o + 384))
         rows(r("MT", 0, 2048, row=4 + j), r("JUNK", o + 256, o + 384))
-    ts(col(50), col(3), 16.0, A.mult, 15.0, A.add)
+    act(col(50), col(3), bias=15.0, scale=16.0)
     ts(r("B0"), r("JF", 0, 144), col(50), A.is_equal)
-    ts(col(51), PG, 16.0, A.mult, 15.0, A.add)
+    act(col(51), PG, bias=15.0, scale=16.0)
     ts(r("B2"), r("JF", 0, 144), col(51), A.is_equal)
-    ts(r("TRI"), DJ, 0.0, A.is_ge)
-    ts(r("TRIx"), DJ, 0.0, A.is_gt)
-    tt(r("TRIB"), r("TRI"), r("BLKb"), A.mult)
-    mset(r("Q", 4096, WD), 0.0)
+    select(r("TRI"), r("ONES", 0, 128), 0, A.is_ge)
+    select(r("TRIx"), r("ONES", 0, 128), 0, A.is_gt)
+    select(r("TRIB"), r("BLKb"), 0, A.is_ge)
+    fill(r("Q", 4096, WD), 0)
     LW = sm(0)
-    for j in range(3):
-        ts(sm(16 * j), r("JF", 0, 256, 16), PR, A.add, 4096.0, A.add)
-    LWm = sm(48)
-    ts(LWm, LW, -2048.0, A.add)
-    ts(r("nIDb"), r("IDb"), -1.0, A.mult)
-    ts(col(52), PG, KW - 16.0, A.mult, 2.0, A.add)
-    tt(col(53), PF, col(52), A.add)
+    ts(LW, r("JF", 0, 256, 16), PR, A.add, 4096.0, A.add)
+    act(col(52), PG, bias=2.0, scale=KW - 16.0)
+    act(col(53), PF, bias=col(52))
     ts(r("I65"), r("JF", 0, 152), col(53), A.is_equal, 262144.0, A.mult)
-    ts(r("EQ", 0, 153), r("JF", 0, 153), -1.0, A.add, col(53), A.is_equal)
+    fill(r("EQ", 0, 1), 0)
+    scaled(r("EQ", 1, 153), r("I65"), 1.0 / 262144)
     tt(r("DIFF"), r("EQ", 0, 152), r("EQ", 1, 153), A.subtract)
     for j, v in enumerate((64.0, -64.0)):
-        ts(r("BO", 8 * j, 8 * j + 8), r("Q8f"), v, A.mult)
-    mset(r("MRH", KW - 1, 456, KW), TAG)
+        scaled(blk("BO", j, 8), r("Q8f"), v)
+    for h in range(HO):
+        iota(blk("MRH", h, 152), [[0, 8], [1, KW]], 16 * h - 26)
+    fill(r("MRH", KW - 1, 456, KW), int(TAG))
     for j in range(2):
-        mset(r("MRH", j, 304, KW), TAG)
-        mset(r("MRH", 304 + j, 456, KW), 0.0)
-    mset(r("RS"), 0.0)
-    mset(r("RS", 0, 152, KW), 2.0 ** 26)
-    ts(r("RESET"), r("MR"), 0.0, A.is_equal, 2.0 ** 31, A.mult)
+        fill(r("MRH", j, 304, KW), int(TAG))
+        fill(r("MRH", 304 + j, 456, KW), 0)
+    fill(r("RS"), 0)
+    fill(r("RS", 0, 152, KW), 1 << 23)
+    act(r("RESET"), r("MR"), F.Relu, bias=2.0 ** 31, scale=-2.0 ** 31)
     ts(r("RM"), r("MR"), PR, A.is_equal)
-    ts(r("RMH"), r("RM", 0, 128), 0.5, A.mult, 0.5, A.add)
-    ts(r("NRM"), r("MR"), PR, A.not_equal, 2.0 ** 25, A.mult)
-    ts(r("NM"), r("NRM", 0, 128), 32.0, A.mult, -M4096, A.add)
+    act(r("RMH"), r("RM", 0, 128), bias=0.5, scale=0.5)
+    act(r("NRM"), r("RM"), bias=2.0 ** 25, scale=-2.0 ** 25)
+    act(r("NM"), r("RM", 0, 128), bias=2.0 ** 30 - M4096, scale=-2.0 ** 30)
+    tt(col(56, 5), r("COL", 16, 26, 2), r("COL", 17, 26, 2), A.add)
     for j in range(4):
-        tt(col(56 + j), oh(2 * j), oh(2 * j + 1), A.add)
-        act(r("SEL", 128 * j, 128 * j + 128), r("BLKb"), F.Copy, scale=col(56 + j))
-    act(r("SEL", 512, 640), r("BLKb"), F.Copy, scale=oh(10))
-    SELID, SELP, SELM, SELMP, SELLO = [r("SEL", 128 * j, 128 * j + 128) for j in range(5)]
-    mset(r("PFW", 128, 136), 4096.0)
-    ts(col(60), PG, 8.0 - S_IND, A.is_ge, 128.0, A.mult)
-    ts(col(61), PF, 128.0, A.add)
-    lane = (PF, col(61))
-    mset(r("X3"), 0.0)
-    LCOL = r("L16", 16, 24)
-    cp(LCOL, r("JF", 0, 8))
-    LBC = r("L16", 8, 16)
+        scaled(blk("SEL", j), r("BLKb"), col(56 + j))
+    SELID, SELP, SELM, SELMP, SELLO = [blk("SEL", j) for j in range(5)]
+    fill(r("PFW", 128, 136), 4096)
+    for f in range(NS):
+        ts(col(104 + f), PG, 8.0 - S_IND[f], A.is_ge, 128.0, A.mult)
+        act(col(108 + f), col(104 + f), bias=1.0, scale=-1.0 / 256)
+        act(col(112 + f), col(108 + f), scale=16.0)
+        act(col(120 + f), PF, bias=(STREAMS[f][0] + 1.0) * 2.0 ** 40, scale=2.0 ** 40)
+        iota(r3s("CS", HO * f, HO * f + HO, 0, 152), [[0, HO * 152]])
+    fill(r("X3"), 0)
+    fill(r("X3", 13, 128 * NS, 16), 2048)
+    L3, LBC = r("L16", 16, 24), r("L16", 8, 16)
     cp(LBC, r("JF", KW - 1, 152, KW))
-    aL, cL, mpL, hL, bL, dL, kL, uL = 32, 48, 64, 80, 96, r("L16", 112, 128), 128, 176
-    LPR, aS = r("L16", 152, 155), 160
+    aL, cL, mpL, hL, bL, dL, kL, uL, aS = 32, 48, 64, 80, 96, r("L16", 112, 128), 128, 176, 160
 
     def lst(base, f=None):
-        return r("L16", base, base + 16) if f is None else r("L16", base + 8 * f, base + 8 * f + 8)
+        lo, hi = (0, 256) if f is None else STREAMS[f]
+        return r("L16", base + lo // 16, base + hi // 16)
 
     def start_mates():
         k16 = slice(0, 16)
-        mm([(ps(5, 0, 256), r("B0", 15 - j, 143 - j, p=k16), r("AB", j, 4096, 16, p=k16), j == 0, j == 15) for j in range(16)])
-        ts(r("P16", 0, 256), ps(5, 0, 256), 2048.0, A.add)
-        ts(r("P16", 256, 384), r("IB", 256, 384), -2048.0, A.add)
-        ts(r("GM"), r("MR"), 128.0, A.mult, oh(4), A.mult)
-        ts(r("GK"), r("MG"), oh(5), A.mult)
-        tt(r("EQ"), r("GM"), r("GK"), A.add)
-        iota(sm(64, 8), [[64, 2], [0, 4]], -2048)
-        iota(sm(72, 8), [[0, 2], [16, 4]])
-        ts(sm(80, 8), sm(64, 8), oh(4), A.mult)
-        ts(sm(88, 8), sm(72, 8), oh(5), A.mult)
-        tt(sm(64, 8), sm(80, 8), sm(88, 8), A.add)
+        mms([(ps(6, 256, 512), r("B0", 15 - j, 143 - j, p=k16), r("AB", j, 4096, 16, p=k16), j == 0, j == 15) for j in range(16)], 2)
+        ts(r("P16", 0, 256), ps(6, 256, 512), 2048.0, A.add)
         for j in range(8):
-            av = r("AV", 256 * j, 256 * j + 256)
-            act(av, r("EQ"), bias=sm(64 + j, 1))
-            cp(ind(r("MT", 2048, 4096), r("P16", 256 + 16 * j, 272 + 16 * j)), av)
+            ts(r("P16", 256 + 16 * j, 272 + 16 * j), r("IB", 256 + j, 384, 8), -2048.0, A.add)
+        iota(r("GM"), [[8, 16], [128, 16]], -2048)
+        scaled(r("GK"), r("GM"), oh(4))
+        ts(sm(64, 8), r("JF", 0, 8), oh(5), A.mult)
         for j in range(8):
-            act(r("MPP", 512 * j, 512 * j + 512), ind(r("MT"), r("P16", 32 * j, 32 * j + 32)), F.Copy)
+            act(blk("AV", j, 256), r("GK"), bias=sm(64 + j, 1))
+            cp(ind(r("MT", 2048, 4096), r("P16", 256 + 16 * j, 272 + 16 * j)), blk("AV", j, 256))
+        bonus[0] = 0.0
+        for j in range(16):
+            if j % 3 == 2:
+                cp(blk("MPP", j, 256), ind(r("MT"), blk("P16", j, 16)))
+            else:
+                act(blk("MPP", j, 256), ind(r("MT"), blk("P16", j, 16)), F.Copy)
         for j in range(2):
             rows(r("ST", 0, 4096, row=6 + j), r("MPP", 0, 4096, row=4 + j))
             rows(r("ST", 2048, 4096, row=4 + j), r("MT", 2048, 4096, row=4 + j))
 
     def late_constants():
-        iota(r("K1", 0, 2176), [[0, 2176]], 5)
+        fill(r("K1", 0, 2176), 5)
         dma("y", T.K1[:, 2176:WD], T.K1[:, 0:2176], [r("K1", 0, 2176)], [r("K1", 2176, WD)], 4000)
-        ts(LPR, r("JF", 0, 3), 0.0, A.mult, PR, A.add)
-        act(r("B10"), r("B2"), F.Copy, scale=oh(10))
-        act(r("B23"), r("B2"), F.Copy, scale=col(57))
-        act(r("B45"), r("B2"), F.Copy, scale=col(58))
-        tt(r("NTM"), r("BLKb"), r("TRIB"), A.subtract)
-        mset(r3s("SBQ", 0, RO, 0, 96), -1.0)
-        mset(r("SG", 0, 96), 0.0)
-        ts(col(64, 12), col(16, 12), -2.0, A.mult, 1.0, A.add)
-        tt(col(76), oh(12), oh(13), A.add)
-        ts(col(77), col(76), 256.0, A.mult, oh(14), A.add)
+        cp(L3, r("JF", 5, 48, 6))
+        act(col(61), oh(10), scale=1.0 / 8192)
+        scaled(SELLO, r("BLKb"), col(61))
+        scaled(r("B10"), r("B2"), oh(10))
+        scaled(r("B23"), r("B2"), col(57))
+        scaled(r("B45"), r("B2"), col(58))
+        select(r("NTM"), r("BLKb"), 0, A.is_gt, sign=-1)
+        iota(r3s("SBQ", 0, RO, 0, 96), [[0, RO * 96]], -1)
+        fill(r("SG", 0, 96), 0)
+        act(col(64, 12), col(16, 12), bias=1.0, scale=-2.0)
+        act(col(76), oh(12), bias=oh(13))
+        act(col(77), col(76), bias=oh(14), scale=4.0)
         ts(col(78), PR, 12.0, A.is_lt, BETA, A.mult)
-        tt(col(79), col(78), col(77), A.subtract)
-        cp(r("BITS", 0, 1), col(79))
+        act(r("BITS", 0, 1), col(77), bias=col(78), scale=-1.0)
         for k in range(12):
-            if k < 10:
-                ts(r("BITS", 1 << k, 2 << k), r("BITS", 0, 1 << k), col(64 + k), A.mult)
-            else:
-                act(r("BITS", 1 << k, 2 << k), r("BITS", 0, 1 << k), F.Copy, scale=col(64 + k))
-        ts(col(80), oh(15), TAG, A.mult, col(77), A.add)
-        act(r("KSEL"), r("BLKb"), F.Copy, scale=col(80))
-        ts(r("PI", 5, 6), r("PI", 2, 3), 1, A.bitwise_and)
-        cp(col(81), r("PI", 5, 6))
-        ts(col(82, RO), r("JF", 0, RO), 1.0, A.add, oh(15), A.mult)
-        ts(col(82, RO), col(82, RO), -1.0, A.mult)
-        tt(col(87), oh(8), oh(9), A.add)
-        ts(r("TMP", 0, 128), r("MR", 0, 128), 15.0, A.is_equal, col(87), A.mult)
-        ts(r("TMP", 128, 256), r("TMP", 0, 128), -2.0 ** 25, A.mult)
-        tt(r("SELJ"), r("TMP", 128, 256), r("BLKf"), A.mult)
-        ts(r("DM"), DJ, -4.0, A.is_equal, col(76), A.mult)
-        tt(col(88), col(56), col(58), A.add)
-        tt(col(89), col(57), col(59), A.add)
-        ts(r("KEEP"), DJ, 0.0, A.is_equal, col(88), A.mult)
-        ts(r("SHIFT"), DJ, 2.0, A.is_equal, col(88), A.mult)
-        ts(r("TMP", 256, 384), DJ, 0.0, A.is_equal, col(89), A.mult)
-        ts(r("TMP", 384, 512), DJ, -2.0, A.is_equal, col(89), A.mult)
-        tt(r("PO"), r("TMP", 256, 384), r("TMP", 384, 512), A.add)
-        ts(r("MSW", 0, 128), DJ, 4.0, A.is_equal, col(56), A.mult)
-        ts(r("MSW", 128, 256), DJ, 6.0, A.is_equal, col(56), A.mult)
-        tt(r("TMP", 0, 128), r("KEEP"), r("SHIFT"), A.add)
-        ts(r("MSW", 256, 384), r("TMP", 0, 128), col(58), A.mult)
-        tt(col(90), THC, oh(10), A.add)
-        ts(col(91), col(58), -1.0, A.mult, 1.0, A.add)
-        ts(col(92), col(59), -1.0, A.mult, 1.0, A.add)
-        tt(col(93), col(91), col(59), A.subtract)
-        act(r("MSW", 384, 512), r("IDb"), F.Copy, scale=col(93))
-        ts(r("TMP", 384, 512), DJ, 0.0, A.is_lt, 128.0, A.mult)
-        tt(r("TMP", 128, 256), r("TMP", 384, 512), DJ, A.add)
+            for x in range(0, 1 << k, 512):
+                ts(r("BITS", (1 << k) + x, (1 << k) + min(1 << k, x + 512)), r("BITS", x, min(1 << k, x + 512)), col(64 + k), A.mult)
+        act(col(80), oh(15), bias=col(77), scale=TAG)
+        scaled(KS8, r("Q8f"), col(80))
+        ts(r("PI", 5, 7), r("PI", 1, 3), 1, A.bitwise_and)
+        cp(col(98, 2), r("PI", 5, 7))
+        act(col(79), oh(15), scale=-1.0)
+        scaled(col(82, RO), r("JF", 1, RO + 1), col(79))
+        fill(r("SELJ"), 0)
+        act(col(87), col(60), scale=-2.0 ** 25)
+        scaled(r("SELJ", 15, 128, 16), r("Q8f"), col(87))
+        for j, k in enumerate((-4, 2, -2, 4, 6)):
+            select(blk("DG", j), r("ONES", 0, 128), k)
+        act(col(81), col(76), scale=1.0 / 64)
+        scaled(r("DM"), blk("DG", 0), col(81))
+        act(col(88), col(56), bias=col(58))
+        act(col(89), col(57), bias=col(59))
+        scaled(r("KEEP"), ID, col(88))
+        scaled(r("SHIFT"), blk("DG", 1), col(88))
+        scaled(blk("PO", 0), ID, col(89))
+        scaled(blk("PO", 1), blk("DG", 2), col(89))
+        scaled(blk("MSW", 0), blk("DG", 3), col(56))
+        scaled(blk("MSW", 1), blk("DG", 4), col(56))
+        scaled(blk("MSW", 2), ID, col(58))
+        scaled(blk("MSW", 3), blk("DG", 1), col(58))
+        act(col(35), oh(8), bias=oh(10), scale=col(33))
+        act(col(90), oh(9), bias=col(35), scale=col(34))
+        act(col(91), col(58), bias=1.0, scale=-1.0)
+        act(col(92), col(59), bias=1.0, scale=-1.0)
+        act(col(93), col(59), bias=col(91), scale=-1.0)
+        act(col(100), oh(9), scale=-32.0)
+        scaled(blk("MSW", 4), ID, col(93))
         for d in range(1, NR):
-            ts(r("ROT", 128 * d - 128, 128 * d), r("TMP", 128, 256), 16.0 * d, A.is_equal)
-        act(r("ROT", 384, 768), r("ROT", 0, 384), F.Copy, scale=-256.0)
-        act(r("ROT", 768, 1152), r("ROT", 0, 384), F.Copy, scale=col(8))
-        act(r("ROT", 1152, 1536), r("ROT", 768, 1152), F.Copy, scale=-1.0)
-        ts(r("UP"), r("IDb"), col(8), A.mult)
-        ts(r("nUP"), r("UP"), -1.0, A.mult)
-        tt(r("LOW"), r("IDb"), r("UP"), A.subtract)
-        mset(r("X2"), -2.0 ** 30)
-        for f in range(2):
-            ts(r("X2", 128 * f + 14, 128 * f + 128, 16), r("JF", 0, 8), 0.0, A.mult, lane[f], A.add)
-            ts(sm(96 + 8 * f, RO), r("JF", 0, RO), 1.0, A.add)
-            tt(sm(112 + 8 * f, RO), sm(96 + 8 * f, RO), sm(96 + 8 * f, RO), A.mult)
-            ts(sm(96 + 8 * f, RO), sm(112 + 8 * f, RO), -1.0, A.mult, lane[f], A.add)
-            ts(sm(96 + 8 * f, RO), sm(96 + 8 * f, RO), 1.0 - 12 * BETA * BETA, A.add)
-        ts(sm(80), LW, -3840.0, A.add)
-        ts(col(94), PR, 239.0, A.add)
-        mset(r("C16B"), 16.0)
-        ts(sm(112, 6), sm(0, 6), -4096.0, A.add)
-        ts(r("PI", 6, 7), r("PI", 0, 1), 1, A.bitwise_and)
-        ts(col(95), r("PI", 6, 7), -1.0, A.mult, 1.0, A.add)
-        ts(sm(118, 6), sm(112, 6), col(95), A.add)
-        ts(sm(124, 6), sm(112, 6), col(95), A.add)
+            select(blk("ROT", 2 + d), r("ONES", 0, 128), 16 * d)
+            select(blk("ROT", d - 1), blk("ROT", 2 + d), 16 * d - 128, A.not_equal, 1.0)
+        scaled(blk("ROT", 1, 384), blk("ROT", 0, 384), -256.0)
+        scaled(blk("ROT", 2, 384), blk("ROT", 0, 384), col(8))
+        scaled(blk("ROT", 3, 384), blk("ROT", 2, 384), -1.0)
+        scaled(blk("UP", 0), ID, col(8))
+        scaled(blk("UP", 1), blk("UP", 0), -1.0)
+        act(col(101), col(8), bias=1.0, scale=-1.0)
+        scaled(blk("UP", 2), ID, col(101))
+        fill(r("X2"), -(1 << 20))
+        for f in range(NS):
+            iota(r("X2", 128 * f + 14, 128 * f + 128, 16), [[0, 8]], STREAMS[f][0], 1)
+        for t in range(RO):
+            iota(sm(96 + t, 2, 8), [[128, 2]], 8193 - int(12 * BETA * BETA) - (t + 1) ** 2, 1)
+            iota(sm(256 + t, 2, 8), [[128, 2]], 8192 - (t + 1) * int(TAG), 1)
+        fill(r("LS"), 0)
+        mset(r("LS", 0, 96, 6), -2.0 ** 40)
+        mset(r("LW2"), -2.0 ** 40)
+        fill(r("LW2", 2, 96, 6), 0)
+        act(sm(80), LW, bias=-3840.0)
+        iota(sm(688, 48), [[0, 3], [16, 16]])
+        ts(r("T80", 0, 48), sm(688, 48), PR, A.add)
+        act(col(94), PR, bias=239.0)
+        fill(r("C16B", 0, 16), 16)
+        act(sm(112, 6), sm(688, 6), bias=PR)
+        act(col(95), col(98), bias=PR, scale=-1.0)
+        act(col(95), col(95), bias=1.0)
+        for j in (1, 2):
+            act(sm(112 + 6 * j, 6), sm(688, 6), bias=col(95))
+        act(sm(112, 18), sm(112, 18), bias=4096.0, scale=8192.0)
         for j in range(3):
-            cp(sm(130 + 6 * j, 6), sm(0, 6))
-        ts(sm(148, 12), sm(130, 12), -2048.0, A.add)
-        iota(r("KR", 0, 96), [[2, 48], [0, 2]], 1)
+            act(sm(130 + 6 * j, 6), sm(0, 6), bias=-2048.0)
+        iota(r("KR", 0, 96), [[16384, 48], [0, 2]], 8192)
 
     def r2w(b, lo, items, out):
         o = lo
         for sel, src in items:
             n = src[5]
-            mm([(ps(b, o, o + n), r("IDb"), r("NRM", 0, n), True, False)])
+            mm([(ps(b, o, o + n), ID, r("NRM", 0, n), True, False)])
             mm([(ps(b, o, o + n), sel, src, False, True)], acc=True)
             o += n
         scan(out, r("RESET", 0, o - lo), ps(b, lo, o), A.add, A.min)
 
-    live = sm(160)
+    live, ends = r("T80", 48, 64), sm(448, 48)
 
     def lanes(t):
         s = (STEP * t) & 2047
         if t == 0:
             k8 = slice(0, 8)
-            mm([(ps(0, 0, 128), r("B0", 15 - j, 143 - j, p=k8), r("MPP", j, 2048, 16, p=k8), j == 0, j == 15) for j in range(16)])
+            mms([(ps(0, 0, 128), r("B0", 15 - j, 143 - j, p=k8), r("MPP", j, 2048, 16, p=k8), j == 0, j == 15) for j in range(16)])
         else:
             mm([(ps(0, 0, 128), ZERO, ones(128), True, False)])
             items = []
@@ -493,210 +508,258 @@ def build(g, T, topo, core):
                 sel = r("B10", 15 - j, 143 - j)
                 items += [(ps(0, 0, nb), sel, r("ST", s + j, 2048, 16), False, False),
                           (ps(0, nb, 128), sel, r("ST", x, x + 16 * (128 - nb), 16), False, j == 15)]
-            mm(items, acc=True)
-        act(r("FW"), ps(0, 0, 128), F.Copy)
+            mms(items)
+        scaled(r("FW"), ps(0, 0, 128), 1.0)
         mm([(ps(1, 0, 128), r("FW"), r("BLKb"), True, True)])
-        act(r("CTX"), ps(1, 0, 128), F.Copy)
+        scaled(r("CTX"), ps(1, 0, 128), 1.0)
         mm([(ps(1, 128, 136), r("TRI"), r("CTX", 0, 128, 16), True, True),
             (ps(1, 136, 144), r("ONES", 0, 128), r("CTX", 0, 128, 16), True, True)])
         mm([(ps(0, 128, 256), r("TRIB"), r("FW"), True, False), (ps(0, 128, 256), r("CTX"), r("TRIx"), False, True)])
-        ts(sm(192, 8), ps(1, 128, 136), -1.0, A.mult, 0.5, A.add)
-        act(r("PFW", 0, 128), ps(0, 128, 256), F.Copy)
-        ts(col(62), col(60), s / 8.0, A.add)
-        for f in FIRST:
-            o = 8 * f
-            part = lambda a, b, n: (a, "IND", o + b, o + b + n, None, 128)
+        act(sm(192, 8), ps(1, 128, 136), bias=0.5, scale=-1.0)
+        for f in range(NS):
+            act(r("X3", 128 * f + 15, 128 * f + 128, 16), ps(1, 136, 144), F.Relu, bias=col(120 + f), scale=-2.0 ** 40)
+        scaled(r("PFW", 0, 128), ps(0, 128, 256), 1.0)
+        for f, (lo, hi) in enumerate(STREAMS):
+            o, z, b = lo // 16, hi // 16, 2 + f % 2
+            part = lambda a, k, n: (a, "IND", 8 * f + k, 8 * f + k + n, None, hi - lo)
+            act(col(116 + f), col(104 + f), bias=float(s), scale=8.0)
             for k in range(8):
-                x = part(T.IND[:, o:o + 8, 16 * k:16 * k + 16], k, 1)
-                if k < 8 - S_IND:
-                    ts(x, JB3(f), ps(1, 128 + k, 129 + k), A.is_ge, 2.0, A.mult)
+                x = part(T.IND[:, o:z, 16 * k:16 * k + 16], k, 1)
+                if k < 8 - S_IND[f]:
+                    ts(x, r3s("JB3", o, z, 0, 16), sm(192 + k, 1), A.add, 0.0, A.is_gt)
                 else:
-                    act(x, JB3(f), F.Sign, bias=sm(192 + k, 1))
-            mm([(ps(2 + f, q, q + 1), part(T.IND[:, o + q, :], 0, 8), r("ONES", 0, 1), True, True) for q in range(8)])
-            ts(lst(bL, f), ps(2 + f, 0, 8), col(60), A.add, 0.5, A.mult)
-            ts(sm(224 + o, 8), ps(2 + f, 0, 8), col(62), A.add, 8.0, A.mult)
-            i2 = r("IND2", 128 * f, 128 * f + 128)
-            tt(i2, ind(r("PFW"), lst(bL, f)), r("JF", 128 * f, 128 * f + 128), A.is_le)
-            mm([(ps(2 + f, 16, 24), r("B2", 15 - j, 143 - j), r("IND2", 128 * f + j, 128 * f + 128, 16), j == 0, j == 15)
-                for j in range(16)])
-            tt(r("BD", 16 + o, 24 + o), sm(224 + o, 8), ps(2 + f, 16, 24), A.add)
-            ts(r("PI", 8 + o, 16 + o), r("BD", 16 + o, 24 + o), 2047, A.bitwise_and)
-            cp(lst(aL, f), r("PI", 8 + o, 16 + o))
-        for f in range(2):
-            ts(r("X3", 128 * f + 15, 128 * f + 128, 16), ps(1, 136, 144), lane[f], A.is_le, 2.0 ** 40, A.mult)
-        ts(live, r("BD", 16, 32), 2048.0 + s, A.is_lt)
-        tt(sm(240), r("PI", 8, 24), LW, A.subtract)
-        tt(sm(448), sm(240), live, A.mult)
-        tt(sm(176), sm(448), LW, A.add)
-        cp(lst(aS), sm(176))
+                    act(x, r3s("JB3", o, z, 0, 16), F.Sign, bias=sm(192 + k, 1))
+            mm([(ps(b, q, q + 1), part(T.IND[:, q, :], 0, 8), r("ONES", 0, 1), True, True) for q in range(o, z)])
+            ts(lst(bL, f), ps(b, o, z), col(104 + f), A.add, col(108 + f), A.mult)
+            act(sm(224 + o, z - o), ps(b, o, z), bias=col(116 + f), scale=col(112 + f))
+            tt(r("IND2", lo, hi), ind(r("PFW"), lst(bL, f)), r("JF", lo, hi), A.is_le)
+            mms([(ps(b, 16 + o, 16 + z), r("B2", 15 - j, 143 - j), r("IND2", lo + j, hi, 16), j == 0, j == 15) for j in range(16)], 8)
+            tt(r("BD", 16 + o, 16 + z), sm(224 + o, z - o), ps(b, 16 + o, 16 + z), A.add)
+            ts(r("PI", 8 + o, 8 + z), r("BD", 16 + o, 16 + z), 2047, A.bitwise_and)
+            cp(lst(aL, f), r("PI", 8 + o, 8 + z))
+        ts(live, r("BD", 16, 32), 2048.0 + s, A.is_lt, 8192.0, A.mult)
+        tt(sm(240), LW, live, A.subtract)
+        tt(sm(448), r("PI", 8, 24), sm(240), A.max)
+        cp(lst(aS), sm(448))
 
     stage = [0]
 
     def hop(t, h, f):
-        lo, hi = 128 * f, 128 * f + 128
+        lo, hi = STREAMS[f]
+        n, e, o, end = hi - lo, HO * f + h, lo // 16, h == HO - 1
         c = lambda name: r(name, lo, hi)
-        e, o, end = 2 * h + f, 8 * f, h == HO - 1
-        raw, kb = ps(f, 0, 128), 2 + f
-        key, ee = ps(kb, 0, 152), ps(kb, 152, 304)
-        w0 = 0 if h else 256
-        mm([(raw, Mp, ones(128), True, False)])
-        mm([(raw, r("W16", w0 + 128, w0 + 256), c("Y"), False, False), (raw, r("IDb"), r("NM"), False, False),
-            (raw, r("W16", w0, w0 + 128), c("Y"), False, True)], acc=True)
-        scan(r("SC", 768 + lo, 768 + hi), r("RESET", 0, 128), raw, A.add, A.min)
-        ts(lst(uL, f), r("SC", 768 + lo + 15, 768 + hi, 16), 2048.0, A.add)
+        p = slice(0, n)
+        raw, wr, key, ee = ps(f, 0, n), ps(f, 128, 128 + n // 16), ps(f, 136, 288, p=p), ps(f, 288, 440, p=p)
+        named = [len(ops)]
+
+        def name(text):
+            for x, nm in zip(ops[named[0]:], text.split()):
+                x["hop"] = (NS * (HO * t + h) + f, nm)
+            named[0] = len(ops)
+
+        def part(x, a=0, z=None, step=1):
+            return (x[0][p, a:z:step],) + x[1:5] + (len(range(a, z or x[5], step)),)
+        if h:
+            mm([(raw, Mp, ones(n), True, False)])
+            mm([(raw, blk("W16", 1), c("Y"), False, False), (raw, ID, r("NM", 0, n), False, False),
+                (raw, blk("W16", 0), c("Y"), False, True)], acc=True)
+        else:
+            mm([(raw, r("BLKf"), r("CN", 0, n), True, False)])
+            mm([(raw, blk("W16", 3), c("QA"), False, False), (raw, Mp, ones(n), False, False),
+                (raw, ID, r("NM", 0, n), False, False), (raw, blk("W16", 2), c("QA"), False, True)], acc=True)
+        scan(r("SC", 768 + lo, 768 + hi), r("RESET", 0, n), raw, A.add, A.min)
+        ts(lst(uL, f), r("SC", 768 + lo + 15, 768 + hi, 16), 2048.0 if h else col(14), A.add)
         cp(c("C16"), ind(r("CT"), lst(uL, f)))
         ts(c("CF"), c("C16"), -2048.0, A.add)
         tt(c("EQ"), c("CF"), ps(6, lo, hi), A.is_equal)
-        key_end = lambda e: r3("PM", e, KW - 1, 152, KW)
-        c_end = lambda e: r3("CS", e, KW - 1, 152, KW)
-        slot = lambda j: ps(kb, 152 + j, 304, KW)
-        if end:
-            tt(sm(368 + o, 8), c_end(f), c_end(2 + f), A.subtract)
+        key_end = lambda e: part(r3("PM", e), KW - 1, 152, KW)
+        c_end = lambda e: part(r3("CS", e), KW - 1, 152, KW)
+        slot = lambda j: ps(f, 288 + j, 440, KW, p=p)
+        idf, nidf = part(IDf, 0, n), part(nIDf, 0, n)
         mm([(ee, c("CF"), r("DIFF"), True, not end)] +
-           ([(slot(1), r("IDf"), sm(368 + o, 8), False, False), (slot(2), r("IDf"), c_end(2 + f), False, True)] if end else []))
-        mm([(key, r("IDb"), r("MRH", 152 * h, 152 * h + 152), True, False), (key, c("EQ"), r("I65"), False, False)] +
-           ([(ps(kb, j, 152, KW), r("IDf"), key_end(2 * j + f), False, False) for j in range(2)] if end else []))
+           ([(slot(1), idf, c_end(e - 2), False, False), (slot(1), nidf, c_end(e - 1), False, False),
+             (slot(2), idf, c_end(e - 1), False, True)] if end else []))
+        mm([(key, r("IDb", 0, n), blk("MRH", h, 152), True, False), (key, c("EQ"), r("I65"), False, False)] +
+           ([(ps(f, 136 + j, 288, KW, p=p), idf, key_end(e - 2 + j), False, False) for j in range(2)] if end else []))
+        name("M U sU tU C CF EQ ee key")
 
         def sums(src, j0, j1, bo, stop):
-            x, z, p = 2048 * f + 512 * j0, 2048 * f + 512 * j1, slice(32 * j0, 32 * j1)
-            mm([(ps(kb, i + 2, 152, KW, p=p), r(src, x + i, z, 16), bo, False, stop and i == 15) for i in range(16)], acc=True)
-        for j, mode in enumerate(MODES[f]):
-            a, b = 2048 * f + 512 * j, 2048 * f + 512 * j + 512
-            got = ind(r("Q"), r("C16", lo + 32 * j, lo + 32 * j + 32))
-            arep = r("AREP", a, b)
-            if mode == "S":
-                bank = ps((4, 5, 7)[stage[0] % 3])
+            x, z = CUTS[f][j0], CUTS[f][j1]
+            mms([(ps(f, 138 + i, 288, KW, p=slice(x, z)), r(src, 16 * (lo + x) + i, 16 * (lo + z), 16), bo, False, stop and i == 15)
+                 for i in range(16)], 8)
+            name("%s%da %s%db" % (src[0], j0, src[0], j0))
+        got = lambda x, z: ind(r("Q"), r("C16", x // 16, z // 16))
+        bank, todo = {}, [set(range(j0, j1)) for j0, j1 in PARTS]
+        for step in (LAST_STEPS if end and f == NS - 1 else STEPS).split():
+            kind, j = step[0], int(step[1])
+            a, b = 16 * (lo + CUTS[f][j]), 16 * (lo + CUTS[f][j + 1])
+            if kind == "g":
+                bank[j] = ps(STAGE[stage[0] % len(STAGE)], 0, b - a)
                 stage[0] += 1
-                act(r("XG", a, b), got, F.Copy)
-                mm([(bank, r("nIDb"), arep, True, False)])
-                mm([(bank, r("IDb"), r("XG", a, b), False, True)], acc=True)
-                act(r("AB", a, b), bank, F.Abs)
+                act(r("XG", a, b), got(a, b), F.Copy)
+                mm([(bank[j], r("nIDb"), r("AREP", a, b), True, False)])
+                mm([(bank[j], ID, r("XG", a, b), False, True)], acc=True)
+                name("g%d n%d x%d" % (j, j, j))
+            elif kind == "s":
+                for x in range(a, b, V_CUT):
+                    tt(r("XG", x, x + V_CUT), got(x, x + V_CUT), r("AREP", x, x + V_CUT), A.subtract)
+                name("s%da s%db" % (j, j))
+            elif kind == "a":
+                act(r("AB", a, b), bank.get(j) or r("XG", a, b), F.Abs)
+                name(step)
             else:
-                tt(r("XG", a, b), got, arep, A.subtract)
-                if mode == "M":
-                    act(r("AB", a, b), r("XG", a, b), F.Abs)
-                else:
-                    ts(r("AB", a, b), r("XG", a, b), 0.0, A.max, 2.0, A.mult)
-                    sums("XG", j, j + 1, r("BO", 8, 16), False)
-            for j0, j1 in PARTS:
-                if j1 == j + 1:
-                    sums("AB", j0, j1, r("BO", 0, 8), True)
-        scan(r3("PM", e), r("RS"), key, A.add, A.min)
-        stp, wr = r("STP", 152 * f, 152 * f + 152), ps(f, 128, 136)
-        tt(stp, key, r3("PM", e), A.not_equal)
-        scan(r3("CS", e), ee, stp, A.add, A.mult)
-        tt(c("XH"), ind(r3("CS", e), LBC), r("RM", 0, 128), A.mult)
-        mm([(wr, c("XH"), Q8, True, True)])
+                ts(r("AB", a, b), r("XG", a, b), 0.0, A.max, 2.0, A.mult)
+                name(step)
+                sums("XG", j, j + 1, blk("BO", 1, 8), False)
+            if kind in "ar":
+                for (j0, j1), left in zip(PARTS, todo):
+                    if j in left:
+                        left.remove(j)
+                        if not left:
+                            sums("AB", j0, j1, blk("BO", 0, 8), True)
+        pm, stp = part(r3("PM", e)), part(blk("STP", f, 152))
+        scan(pm, part(r("RS")), key, A.add, A.min)
+        tt(stp, key, pm, A.not_equal)
+        scan(part(r3("CS", e)), ee, stp, A.add, A.mult)
+        tt(blk("XH", f), ind(r3("CS", e), LBC), r("RM", 0, 128), A.mult)
+        mm([(wr, part(blk("XH", f)), part(Q8, 0, n // 16), True, True)])
+        name("PM NE CS XH wr")
         if not end:
             ts(lst(hL, f), wr, 2048.0, A.add)
-            act(c("GM"), ind(r("ST"), lst(hL, f)), F.Copy)
-            r2w(f, 256, [(SELMP, c("GM"))], c("SC"))
+            if GM_V:
+                cp(c("GM"), ind(r("ST"), lst(hL, f)))
+            else:
+                act(c("GM"), ind(r("ST"), lst(hL, f)), F.Copy)
+            r2w(f, 0, [(SELMP, c("GM"))], c("SC"))
             ts(lst(mpL, f), r("SC", lo + 15, hi, 16), 2048.0, A.add)
             tt(c("Y"), ind(r("Q"), lst(mpL, f)), c("A2"), A.add)
+            name("tH GM N SEL sM tM Y")
             return
         cl = lst(cL, f)
         ts(cl, wr, 2048.0, A.add)
-        tt(sm(464 + o, 8), wr, sm(48 + o, 8), A.subtract)
-        bd, nk, z = r("BD", o, o + 8), sm(592 + o, 8), ps(f, 256, 384)
-        x2 = lambda j: r("X2", lo + j, hi, 16)
-        ts(bd, key_end(e), -31.5, A.add, 1.0 / 64, A.mult)
-        ts(x2(15), key_end(e), 8.0, A.add, 2.0 ** 19, A.mult)
-        ts(x2(12), bd, M64, A.add, M64, A.subtract)
-        tt(x2(13), bd, x2(12), A.subtract)
+        name("tH")
+        act(sm(464 + o, n // 16), wr, bias=2048.0)
+        d64 = part(sm(320 + 8 * f, 8))
+        x2 = lambda j: part(blk("X2", f), j, 128, 16)
+        ts(d64, key_end(e), M64, A.add, M64, A.subtract)
+        act(x2(15), key_end(e), bias=2.0 ** 24, scale=2.0 ** 19)
+        ts(x2(12), d64, M4096, A.add, M4096, A.subtract)
+        tt(x2(13), d64, x2(12), A.subtract)
         act(c("GSC"), ind(r("ST"), cl), F.Copy)
-        ts(c("GB"), ind(r("BITS"), cl), col(82 + t), A.add)
-        mm([(z, c("X2"), r("IDf"), True, False), (z, c("X3"), r("IDb"), False, False)])
-        mm([(z, r("SELJ"), c("GSC"), False, True)], acc=True)
-        tt(c("U2"), c("GB"), z, A.max)
-        ts(r("GB", 256 + lo, 256 + hi), c("GB"), col(81), A.mult)
+        if f < NS - 1:
+            act(c("GB"), ind(r("BITS"), cl), bias=col(82 + t))
+        else:
+            ts(c("GB"), ind(r("BITS"), cl), col(82 + t), A.add)
+        mm([(raw, part(blk("X2", f)), idf, True, False), (raw, part(blk("X3", f)), part(ID, 0, n), False, False)])
+        mm([(raw, r("SELJ"), c("GSC"), False, True)], acc=True)
+        tt(c("U2"), c("GB"), raw, A.max)
+        scaled(r("GB", 256 + lo, 256 + hi), c("GB"), col(99))
         cp(ind(r("K1"), lst(aS, f)), c("U2"))
-        ts(nk, bd, 256.0, A.mult, sm(96 + o + t, 1), A.add)
-        ts(sm(608 + o, 8), nk, 12 * BETA * BETA + (t + 1) ** 2 - 1.0 - (t + 1) * TAG, A.add)
-        tt(c("XE"), ind(sm(608 + o, 8), LCOL), r("RM", 0, 128), A.mult)
-        mm([(ps(6, 256 + o, 264 + o), c("XE"), r("Q8f"), True, True)])
+        for j in range(2):
+            a, z = max(lo, 128 * j), min(hi, 128 * j + 128)
+            if a < z and n < 128:
+                mm([(ps(6, 448 + 8 * j, 456 + 8 * j, p=slice(a - 128 * j, z - 128 * j)), part(IDf, a - lo, z - lo), d64, True, True)])
+            if lo < 128 * j + 128 <= hi:
+                d = d64 if n == 128 else ps(6, 448 + 8 * j, 456 + 8 * j)
+                act(r("LS", 48 * j + 2, 48 * j + 48, 6), d, bias=sm(96 + 8 * j + t, 1), scale=4.0)
+                act(sm(608 + 8 * j, 8), d, bias=sm(256 + 8 * j + t, 1), scale=4.0)
+                if j == 0:
+                    pairs(0, 0, [("GB", 0, 128), ("GA", 0, 128)], PAIRS[0])
+                    pairs(1, 0, [("GA", 0, 128)], PAIRS[1])
 
-    def swap(b, lo, n, m, src, first, last):
-        return [(ps(b, lo, lo + n, 2), m, src(1), first, first), (ps(b, lo + 1, lo + n, 2), m, src(0), first, last)]
+    turn = {}
+
+    def pairs(j, slot, items, plan):
+        wide = sum(z - x for _, x, z in items)
+        for who, banks, groups in plan:
+            for k0 in range(0, len(groups), 512 // wide):
+                turn[banks] = turn.get(banks, -1) + 1
+                b, some = banks[turn[banks] % len(banks)], groups[k0:k0 + 512 // wide]
+                for i, k in enumerate(some):
+                    p = slice(16 * k, 16 * k + 16) if k % 2 == 0 else slice(16 * k - 16, 16 * k + 16)
+                    u0, o, got = 256 * (k % 2) + 128 * j, wide * i, []
+                    for name, x, z in items:
+                        got.append((ps(b, o, o + z - x), r(name, u0, u0 + 128, p=p), r("U2", x, z, p=p), True, True))
+                        o += z - x
+                    mm(got, acc=i > 0 and k // 2 == some[i - 1] // 2)
+                for i, k in enumerate(some):
+                    at, a = 48 * j + 6 * k, ps(b, wide * i, wide * i + wide)
+                    if who == "v":
+                        red(r("LW2", at + slot, at + slot + 1), a, A.max)
+                    else:
+                        act(r("JUNK", 512 * (b % 2), 512 * (b % 2) + wide), a, F.Relu, bias=r("LS", at + 2, at + 3),
+                            accum=r("LS", at + 3 + slot, at + 4 + slot))
+
+    def swap(b, lo, n, ms, src, first, last):
+        out = [(ps(b, lo + j, lo + n, 2), m, src(1 - j), first, first) for m in ms for j in range(2)]
+        return out[:-1] + [out[-1][:4] + (last,)]
 
     def put_out(out, b, n, sel, o):
-        mm([(ps(b, 0, n), r(sel, 15 - j, 143 - j), r("ST", n * j, n * j + n), j == 0, j == 15) for j in range(16)])
-        act(r("BLD", o, o + n), ps(b, 0, n), bias=col(12))
+        mms([(ps(b, 0, n), r(sel, 15 - j, 143 - j), blk("ST", j, n), j == 0, j == 15) for j in range(16)], 2)
+        act(r("BLD", o, o + n), ps(b, 0, n), bias=2048.0)
         dma("y", out, T.BLD[:, o:o + n], [r("BLD", o, o + n)], [], 2500)
 
     later = [None]
     lanes(0)
+    bonus[0] = 0.0
     start_mates()
     for t in range(RO):
         last = t == RO - 1
-        for f in FIRST:
-            lo, hi = 128 * f, 128 * f + 128
-            bonus[0] = SKEW * (f == FIRST[0])
-            al, ax = lst(aL, f), ps(7, 256 + lo, 256 + hi)
-            ts(r("Y", lo, hi), ind(r("Q"), al), 2.0, A.mult, OFFX, A.add)
-            act(r("QA", lo, hi), ind(r("Q"), al), F.Copy)
-            mm([(ax, r("XP"), r("QA", lo, hi), True, True)])
-            rep = lambda i: (T.AREP[:, 16 * lo + i:16 * hi:16], "AREP", 16 * lo, 16 * hi, i, 128)
-            for i in range(16):
-                if i < A_S:
-                    act(rep(i), ax, F.Copy)
-                else:
-                    cp(rep(i), rep(0))
-            act(r("A2", lo, hi), ax, bias=OFFA)
-            act(r("GSA", lo, hi), ind(r("ST", 0, 2048), al), F.Copy)
+        for f, (lo, hi) in enumerate(STREAMS):
+            bonus[0] = SKEW * (NS - 1 - f)
+            act(r("QA", lo, hi), ind(r("Q"), lst(aL, f)), F.Copy)
+            act(r("GSA", lo, hi), ind(r("ST", 0, 2048), lst(aL, f)), F.Copy)
             mm([(ps(6, lo, hi), SELID, r("GSA", lo, hi), True, True)])
+            for (x, z), n in zip(A_RUNS, A_S):
+                if z == hi:
+                    ax = ps(7, 256 + x, 256 + z)
+                    mm([(ax, r("XP"), r("QA", x, z), True, True)])
+                    rep = lambda i: (T.AREP[:, 16 * x + i:16 * z:16], "AREP", 16 * x, 16 * z, i, z - x)
+                    for i in range(16):
+                        if i < n:
+                            act(rep(i), ax, F.Copy)
+                        else:
+                            cp(rep(i), rep(0))
+                    act(r("A2", x, z), ax, bias=OFFA)
         bonus[0] = 0.0
         if t:
             later[0]()
         for h in range(HO):
-            for f in FIRST:
-                bonus[0] = SKEW * (f == FIRST[0])
+            for f in range(NS):
+                bonus[0] = SKEW * (NS - 1 - f)
                 hop(t, h, f)
             bonus[0] = 0.0
             if h == 0:
                 if t == 0:
+                    bonus[0] = -30000.0
                     late_constants()
+                    bonus[0] = 0.0
                 act(r("GA", 0, 256), ind(r("BITS"), lst(aL)), bias=col(82 + t))
-                ts(r("GA", 256, 512), r("GA", 0, 256), col(81), A.mult)
+                scaled(r("GA", 256, 512), r("GA", 0, 256), col(99))
         act(r("GK"), ind(r("K1"), lst(cL)), F.Copy)
-        r2w(4, 256, [(r("KSEL"), r("GK"))], r("SC", 0, 256))
+        mm([(ps(6, 256, 272), nIDf, sm(608), True, False)])
+        mm([(ps(6, 256 + 8 * f, 264 + 8 * f), blk("GK", f), KS8, False, f == 1) for f in range(2)], acc=True)
+        act(r("LS", 5, 96, 6), ps(6, 256, 272), F.Relu, scale=-2.0)
         r2w(7, 0, [(SELP, r("GSC"))], r("SC", 256, 512))
-        tt(sm(480), r("SC", 271, 512, 16), LWm, A.subtract)
-        w2 = sm(544)
-        tt(w2, ps(6, 256, 272), r("SC", 15, 256, 16), A.is_lt)
-        tt(sm(688, 48), ind(w2, LPR), sm(448, 48), A.mult)
-        nv = ns = 0
-        for f in FIRST:
-            o, v = 8 * f, V_PAIR[f]
-            for k in sorted(range(8), key=lambda k: k * 8 / (8 - v) if k < 8 - v else (k - 8 + v) * 8 / v + 0.5):
-                p = slice(16 * k, 16 * k + 16) if k % 2 == 0 else slice(16 * k - 16, 16 * k + 16)
-                u0 = 256 * (k % 2) + 128 * f
-                if k >= 8 - v:
-                    b, nv = 2 + nv % 2, nv + 1
-                else:
-                    b, ns = ns % 2, ns + 1
-                mm([(ps(b, 256 * x, 256 * x + 256), r(("GB", "GA")[x], u0, u0 + 128, p=p), r("U2", p=p), True, True) for x in range(2)])
-                if k >= 8 - v:
-                    red(sm(640 + o + k, 1), ps(b), A.max)
-                else:
-                    act(r("JUNK", 512 * b, 512 * b + 512), ps(b), F.Relu, bias=sm(592 + o + k, 1), accum=r("LS", o + k, o + k + 1))
-            tt(r("LS", o + 8 - v, o + 8), sm(648 + o - v, v), sm(600 + o - v, v), A.add)
-            xs_ = r("XS", 128 * f, 128 * f + 128)
-            tt(xs_, ind(r("LS", o, o + 8), LCOL), r("RMH"), A.is_equal)
-            mm([(ps(6, 272 + 16 * j + o, 280 + 16 * j + o), xs_, Q8, True, True) for j in range(3)])
+        act(sm(480), r("SC", 271, 512, 16), bias=2048.0)
+        mm([(ps(6, 272, 336), ID, r("T80"), True, False), (ps(6, 272, 320), M4K, ones(48), False, False)])
+        pairs(0, 1, [("GB", 128, 256), ("GA", 128, 256)], PAIRS[2])
+        pairs(1, 1, [("GB", 0, 256), ("GA", 128, 256)], PAIRS[3])
+        for f in range(2):
+            o = 8 * f
+            scan(blk("LO", f, 48), blk("LS", f, 48), blk("LW2", f, 48), A.add, A.max)
+            tt(blk("XS", f), ind(blk("LO", f, 48), L3), r("RMH"), A.is_equal)
+            mm([(ps(6, 272 + 16 * j + o, 280 + 16 * j + o), blk("XS", f), Q8n, False, j == 3 and f == 1) for j in range(4)], acc=True)
         act(r("QC"), ind(r("Q"), lst(cL)), F.Copy)
-        tt(r("TMP", 48, 96), ps(6, 272, 320), sm(688, 48), A.mult)
-        tt(r("TMP", 96, 144), r("TMP", 48, 96), sm(0, 48), A.add)
-        cp(r("P16", 0, 48), r("TMP", 96, 144))
+        tt(r("TMP", 0, 48), ps(6, 272, 320), ends, A.max)
+        cp(r("P16", 0, 48), r("TMP", 0, 48))
         jA, jC, jO = r("P16", 0, 16), r("P16", 16, 32), r("P16", 32, 48)
-        tt(sm(736), ps(6, 272, 288), w2, A.mult)
-        tt(sm(752), live, sm(736), A.subtract)
-        tt(sm(768), sm(752), sm(80), A.mult)
-        mm([(ps(4, 0, 256), r("PO"), r("GSC"), True, True)])
-        act(r("YS"), ps(4, 0, 256), bias=col(90))
+        mm([(ps(7, 256, 512), blk("PO", j), r("GSC"), j == 0, j == 1) for j in range(2)])
+        act(r("YS"), ps(7, 256, 512), bias=col(90))
         for j, (x, z) in enumerate((("GSC", "GSA"), ("GSA", "GSC"))):
             o = ps(5, 256 * j, 256 * j + 256)
             mm([(o, r("KEEP"), r(x), True, False), (o, r("SHIFT"), r(z), False, False), (o, r("DM"), r("U2"), False, True)])
-        act(r("VV"), ps(5), F.Copy)
+        act(r("VV"), ps(5), bias=col(100))
         mm([(ps(7, 0, 256), r("XP"), r("QC"), True, False), (ps(7, 0, 256), r("nIDb"), r("QA"), False, True)])
         mm([(ps(7, 256, 512), r("XP"), r("QA"), True, False), (ps(7, 256, 512), r("nIDb"), r("QC"), False, True)])
         act(r("SGN"), ps(7), F.Sign)
@@ -704,19 +767,15 @@ def build(g, T, topo, core):
         cp(ind(r("ST"), jC), r("VV", 0, 256))
         act(r("GS2"), ind(r("ST"), lst(aL)), F.Copy)
         cp(ind(r("ST"), jA), r("VV", 256, 512))
-        if last:
-            put_out(T.yp[:], 0, 256, "B23", 0)
+        bonus[0] = 2000.0
         r2w(4, 0, [(SELLO, r("GS2"))], r("SC", 0, 256))
         t1 = r("T16", 0, 16)
-        tt(r("RF"), r("SC", 15, 256, 16), sm(752), A.mult)
-        tt(t1, r("SC", 15, 256, 16), sm(768), A.mult)
+        tt(r("RF"), r("SC", 15, 256, 16), ps(6, 320, 336), A.mult)
+        tt(t1, r("RF"), sm(80), A.mult)
         mm([(ps(4, 256, 272), r("TRIB"), r("RF"), True, False), (ps(4, 257, 272), r("NTM"), r("RF", 0, 15), False, False),
-            (ps(4, 256, 272), r("nIDb"), t1, False, False), (ps(4, 257, 272), r("IDb"), r("T16", 0, 15), False, True),
-            (ps(4, 272, 288), r("BLKb"), r("RF"), True, True)])
-        scan(sm(384), r("C16B"), ps(4, 256, 272), A.add, A.add, col(94))
+            (ps(4, 256, 272), r("nIDb"), t1, False, False), (ps(4, 257, 272), ID, r("T16", 0, 15), False, True)])
+        scan(sm(384), r("C16B", 0, 16), ps(4, 256, 272), A.add, A.add, col(94))
         cp(dL, sm(384))
-        n = sm(303, 1)
-        red(n, ps(4, 272, 288), A.add)
         cp(ind(r3("SBQ", t), dL), r("QA"))
         tr = []
         for d in range(1, NR):
@@ -727,44 +786,48 @@ def build(g, T, topo, core):
                                         src=T.SBQ[:, t, 32 * (d - 1):32 * d], dst=T.LAND[:, t, 32 * (d - 1):32 * d]))
         add("g", [lambda tr=tr: g.remote_dma_fused(tr, local_sem=T.sem.sent)], [r3("SBQ", t, 0, 96)], [r3("LAND", t)], 300.0,
             sem="arr%d" % t, val=4 * (NR - 1), lat=2500.0, remote=True)
+        bonus[0] = 0.0
+        n = sm(303, 1)
+        mm([(ps(5, 496, 512), r("BLKb"), r("RF"), True, True)])
+        act(sm(272), ps(5, 496, 512), F.Copy, scale=-8192.0, accum=n)
         cp(ind(r("SG"), dL), r("GSA"))
         tt(ind(r("Q"), jA), r("SGN", 0, 256), r("QA"), A.add)
         tt(ind(r("Q"), jC), r("SGN", 256, 512), r("QC"), A.add)
-        if not last:
+        if last:
+            put_out(T.yp[:], 0, 256, "B23", 0)
+        else:
             lanes(t + 1)
         r2w(5, 288, [(SELID, r("SG", 0, 96)), (SELM, r("SG", 0, 96))], r("SC", 256, 448))
-        ts(sm(512, 18), sm(112, 18), n, A.is_lt)
-        ts(r("KR", 96, 192), r("KR", 0, 96), n, A.is_lt)
-        tt(sm(544, 12), r("SC", 271, 448, 16), sm(148, 12), A.subtract)
-        tt(sm(560, 6), sm(544, 6), sm(512, 6), A.mult)
-        tt(sm(566, 12), sm(544, 12), sm(518, 12), A.mult)
-        tt(sm(592, 18), sm(560, 18), sm(130, 18), A.add)
-        cp(r("L16", kL, kL + 18), sm(592, 18))
+        act(sm(512, 18), sm(112, 18), bias=n)
+        tt(sm(544, 18), sm(512, 18), sm(130, 18), A.min)
+        ts(r("KR", 96, 192), r("KR", 0, 96), n, A.add, 0.0, A.is_lt)
+        tt(sm(568, 6), r("SC", 271, 352, 16), sm(544, 6), A.max)
+        tt(sm(574, 12), r("SC", 271, 448, 16), sm(550, 12), A.max)
+        ts(r("L16", kL, kL + 18), sm(568, 18), 2048.0, A.add)
         sL, vsL, vmL, pmL = [r("L16", kL + 6 * j, kL + 6 * j + 6) for j in range(4)]
         act(r("QM", 0, 96), ind(r("Q"), vmL), F.Copy)
         sg = lambda j: r("SG", j, 96, 2)
-        mm(swap(5, 0, 96, r("MSW", 0, 128), sg, True, True) + swap(5, 96, 96, r("MSW", 128, 256), sg, True, True) +
-           [(ps(5, 192, 288), r("MSW", 384, 512), r("SG", 0, 96), True, False)] +
-           swap(5, 192, 96, r("MSW", 256, 384), sg, False, True))
+        mm(swap(5, 0, 96, [blk("MSW", 0)], sg, True, True) + swap(5, 96, 96, [blk("MSW", 1)], sg, True, True) +
+           [(ps(5, 192, 288), blk("MSW", 4), r("SG", 0, 96), True, False)] +
+           swap(5, 192, 96, [blk("MSW", 2), blk("MSW", 3)], sg, False, True))
         act(r("SW"), ps(5, 0, 288), F.Copy)
-        mm([(ps(4, 0, 96), r("LOW"), r("QM", 0, 96), True, False)] + swap(4, 0, 96, r("UP"), lambda j: r("QM", j, 96, 2), False, True))
+        UP, nUP, LOW = (blk("UP", j) for j in range(3))
+        mm([(ps(4, 0, 96), LOW, r("QM", 0, 96), True, False)] + swap(4, 0, 96, [UP], lambda j: r("QM", j, 96, 2), False, True))
         act(r("QM", 96, 192), ps(4, 0, 96), F.Copy)
         cp(ind(r("Q"), vmL), r("QM", 96, 192))
-        m3 = lambda name, j: r("ROT", 384 * ("ROT", "RN", "RU", "nRU").index(name) + 128 * j,
-                               384 * ("ROT", "RN", "RU", "nRU").index(name) + 128 * j + 128)
         land = lambda j, x=0, s=1: r3("LAND", t, 32 * j + x, 32 * j + 32, s)
-        mm([(ps(7, 0, 96), r("IDb"), r3("SBQ", t, 0, 96), True, False)])
-        mm([(ps(7, 32 * j, 32 * j + 32), m3("RN", j), land(j), False, j == 2) for j in range(3)], acc=True)
-        ts(r("RR"), ps(7, 0, 96), -255.0, A.add, 0.0, A.max)
-        mm([(ps(6, 320, 416), ZERO, ones(96), True, False)])
-        mm([(ps(6, 320 + 32 * j, 352 + 32 * j), m3("ROT", j), land(j), False, False) for j in range(3)], acc=True)
-        mm([(ps(6, 320, 416), r("IDb"), r("RR"), False, True)], acc=True)
-        act(r("RA"), ps(6, 320, 416), F.Copy)
+        mm([(ps(7, 0, 96), ID, r3("SBQ", t, 0, 96), True, False)])
+        mm([(ps(7, 32 * j, 32 * j + 32), blk("ROT", 3 + j), land(j), False, j == 2) for j in range(3)], acc=True)
+        act(r("RR"), ps(7, 0, 96), F.Relu, bias=-255.0)
+        mm([(ps(6, 352, 448), ZERO, ones(96), True, False)])
+        mm([(ps(6, 352 + 32 * j, 384 + 32 * j), blk("ROT", j), land(j), False, False) for j in range(3)], acc=True)
+        mm([(ps(6, 352, 448), ID, r("RR"), False, True)], acc=True)
+        act(r("RA"), ps(6, 352, 448), F.Copy)
         mm([(ps(4, 384, 480), ZERO, ones(96), True, False)])
-        mm([x for j in range(3) for x in [(ps(4, 384 + 32 * j, 416 + 32 * j), m3("nRU", j), land(j), False, False)] +
-            swap(4, 384 + 32 * j, 32, m3("RU", j), lambda x, j=j: land(j, x, 2), False, False)], acc=True)
-        mm([(ps(4, 384, 480), r("nUP"), r("RR"), False, False)] +
-           swap(4, 384, 96, r("UP"), lambda j: r("RR", j, 96, 2), False, True), acc=True)
+        mm([x for j in range(3) for x in [(ps(4, 384 + 32 * j, 416 + 32 * j), blk("ROT", 9 + j), land(j), False, False)] +
+            swap(4, 384 + 32 * j, 32, [blk("ROT", 6 + j)], lambda x, j=j: land(j, x, 2), False, False)], acc=True)
+        mm([(ps(4, 384, 480), nUP, r("RR"), False, False)] +
+           swap(4, 384, 96, [UP], lambda j: r("RR", j, 96, 2), False, True), acc=True)
         tt(r("TQ"), ps(4, 384, 480), r("KR", 96, 192), A.mult)
         tt(ind(r("Q"), sL), r("TQ"), r("RA"), A.add)
         if last:
@@ -779,17 +842,15 @@ def build(g, T, topo, core):
                 act(gm, ind(r("ST"), vmL), F.Copy, scale=col(91))
                 tt(ind(r("ST"), vmL), gm, r("SW", 0, 96), A.add)
                 r2w(4, 0, [(SELP, gm)], r("SC", 512, 608))
-                tt(sm(624, 6), r("SC", 527, 608, 16), sm(148, 6), A.subtract)
-                tt(sm(632, 6), sm(624, 6), sm(518, 6), A.mult)
-                tt(sm(640, 6), sm(632, 6), sm(130, 6), A.add)
-                cp(pmL, sm(640, 6))
+                tt(sm(624, 6), r("SC", 527, 608, 16), sm(550, 6), A.max)
+                ts(pmL, sm(624, 6), 2048.0, A.add)
                 act(gp, ind(r("ST"), pmL), F.Copy, scale=col(92))
                 tt(ind(r("ST"), pmL), gp, r("SW", 96, 192), A.add)
             later[0] = mend
     return ops
 
 
-def depend(ops):
+def depend(ops, turns=None):
     hist = {}
     for i, o in enumerate(ops):
         deps = {}
@@ -815,6 +876,12 @@ def depend(ops):
                 keep.append((i, kind, lo, hi, row))
                 hist[name] = keep
         o["deps"] = deps
+    for text in (turns or {}).values():
+        place = {x.rstrip("'"): (x.count("'"), k) for k, x in enumerate(text.split())}
+        turn = sorted((o["hop"][0] // (len(STREAMS) * HO), o["hop"][0] + place[o["hop"][1]][0], place[o["hop"][1]][1], i)
+                      for i, o in enumerate(ops) if o.get("hop") and o["hop"][1] in place)
+        for a, b in zip(turn, turn[1:]):
+            ops[b[3]]["deps"].setdefault(a[3], False)
 
 
 def schedule(ops):
@@ -828,8 +895,15 @@ def schedule(ops):
         if not ops[i]["deps"][j]:
             return 0.0
         return ops[j]["lat"] + (SAME if ops[j]["eng"] == ops[i]["eng"] else CROSS)
+    left = [len(o["deps"]) for o in ops]
+    line = [i for i in range(n) if not left[i]]
+    for i in line:
+        for s in succ[i]:
+            left[s] -= 1
+            if not left[s]:
+                line.append(s)
     prio = [0.0] * n
-    for i in range(n - 1, -1, -1):
+    for i in reversed(line):
         prio[i] = ops[i]["cost"] + max([ops[i]["lat"]] + [gap(i, s) + prio[s] for s in succ[i]])
     left = [len(o["deps"]) for o in ops]
     rdy = {i: 0.0 for i in range(n) if not left[i]}
@@ -854,12 +928,111 @@ def schedule(ops):
     return order
 
 
+def polish(ops, order):
+    n = len(ops)
+    cost, lat, eng = ([o[k] for o in ops] for k in ("cost", "lat", "eng"))
+    pred = [[(j, cost[j] + (lat[j] + (SAME if eng[j] == eng[i] else CROSS) if hard else 0.0)) for j, hard in o["deps"].items()]
+            for i, o in enumerate(ops)]
+    succ = [[] for _ in ops]
+    for i in range(n):
+        for j, w in pred[i]:
+            succ[j].append((i, w))
+    seed = [12345]
+
+    def draw():
+        seed[0] = (seed[0] * 1103515245 + 12345) & 0x7FFFFFFF
+        return seed[0] / 2147483648.0
+
+    def window(a):
+        head, tail, free, after = [0.0] * n, [0.0] * n, {}, {}
+        for i in order:
+            head[i] = max([free.get(eng[i], 0.0)] + [head[j] + w for j, w in pred[i]])
+            free[eng[i]] = head[i] + cost[i]
+        for i in reversed(order):
+            tail[i] = max([cost[i] + lat[i], cost[i] + after.get(eng[i], 0.0)] + [w + tail[s] for s, w in succ[i]])
+            after[eng[i]] = tail[i]
+        order.sort(key=lambda i: head[i])
+        win = order[a:a + WINDOW]
+        inside = set(win)
+        free = {eng[i]: head[i] + cost[i] for i in order[:a]}
+        after = {eng[i]: tail[i] for i in reversed(order[a + WINDOW:])}
+        rel = {i: max([0.0] + [head[j] + w for j, w in pred[i] if j not in inside]) for i in win}
+        out = {i: max([cost[i] + lat[i]] + [w + tail[s] for s, w in succ[i] if s not in inside]) for i in win}
+        ins = {i: [(j, w) for j, w in pred[i] if j in inside] for i in win}
+        seq = {}
+        for i in win:
+            seq.setdefault(eng[i], []).append(i)
+        pool = [eng[i] for i in win]
+
+        def value():
+            h, pos, fr, left, top, tot = {}, {e: 0 for e in seq}, {e: free.get(e, 0.0) for e in seq}, len(win), 0.0, 0.0
+            while left:
+                was = left
+                for e, s in seq.items():
+                    k, f = pos[e], fr[e]
+                    while k < len(s):
+                        i = s[k]
+                        t = rel[i] if rel[i] > f else f
+                        for j, w in ins[i]:
+                            x = h.get(j)
+                            if x is None:
+                                break
+                            if x + w > t:
+                                t = x + w
+                        else:
+                            h[i], f, k, left = t, t + cost[i], k + 1, left - 1
+                            t += out[i]
+                            tot += t
+                            if t > top:
+                                top = t
+                            continue
+                        break
+                    pos[e], fr[e] = k, f
+                if left == was:
+                    return None, None
+            return max([top] + [fr[e] + after.get(e, 0.0) for e in seq]) + 0.05 * tot / len(win), h
+        now, h = value()
+        best = (now, h)
+        for it in range(TRIES):
+            s = seq[pool[int(draw() * len(pool))]]
+            i, k = int(draw() * len(s)), 1 + int(draw() ** 2 * 6)
+            j = i + k if draw() < 0.5 else i - k
+            if not 0 <= j < len(s) or any(s[i] in ops[y]["deps"] for y in s[i + 1:j + 1]) or any(y in ops[s[i]]["deps"] for y in s[j:i]):
+                continue
+            s.insert(j, s.pop(i))
+            v, h = value()
+            if v is not None and (v <= now or draw() < math.exp((now - v) / (HEAT * (1.02 - it / TRIES)))):
+                now = v
+                if v < best[0]:
+                    best = (v, h)
+            else:
+                s.insert(i, s.pop(j))
+        order[a:a + WINDOW] = sorted(win, key=lambda i: best[1][i])
+    for _ in range(SWEEPS):
+        for a in range(0, n, WINDOW // 2):
+            window(a)
+    return order
+
+
+ORDER = []
+
+
+def plan(ops):
+    if not ORDER:
+        depend(ops, TEMPLATE)
+        first = schedule(ops)
+        depend(ops)
+        ORDER.extend(polish(ops, first))
+    else:
+        depend(ops)
+    return ORDER
+
+
 def rank_program(g, core, T, topo):
     if T.rank_of(core) is None:
         return
     ops = build(g, T, topo, core)
-    depend(ops)
-    order = schedule(ops)
+    order = plan(ops)
     queue = {"v": g.vector, "s": g.scalar, "t": g.tensor, "g": g, "y": g.sync}
     count = {e: 0 for e in "vstg"}
     seen = {e: {} for e in queue}

@@ -7,18 +7,19 @@ WD = 4352
 STREAMS = ((0, 128), (128, 256))
 CUTS = ((0, 32, 64, 96, 128),) * 2
 STEPS = "g0 s2 g3 s1 a0 r1 a2 a3"
-LAST_STEPS = "g0 s2 g3 s1 a0 r2 r1 a3"
+LAST_STEPS = STEPS
 STAGE = (4, 5, 7)
 GM_V = False
 EARLY = 9000.0
-TEMPLATE = {"v": "s2a' tH'' s1a' s1b' sM'' tM'' Y'' r1' sU tU C s2b PM' CF NE' EQ CS' XH'", "s": "a3' g3 g0 GM' a0 a2"}
+LATE = "PM"
+TEMPLATE = {"v": "sM'' s2a' tM'' Y'' r1' sU tU C PM' CF NE' CS' EQ XH' s1b tH' s1a s2b", "s": "a2' g0 g3 GM' a0 a3"}
 PAIRS = ([("s", (3,), (0, 1, 2, 3, 4, 5)), ("v", (2, 0), (6, 7))], [("v", (2, 0), (0, 1, 2, 3, 4, 5, 6, 7))],
          [("s", (3, 1, 5), (0, 1, 2, 3)), ("v", (2, 0, 4), (4, 5, 6, 7))],
          [("s", (3, 1, 5), (0, 2, 4, 6)), ("v", (2, 0, 4), (1, 3, 5, 7))])
-PARTS = ((0, 3), (3, 4))
+PARTS = ((0, 4),)
 S_IND = (5, 8, 8)
-A_RUNS = STREAMS
-A_S = (5, 6)
+A_REP = ("-vv-", "-ss-")
+A_BANK = ((0, 5, 2, 0), (0, 2, 3, 0))
 V_CUT = 256
 LOOK, SKEW, SAME, CROSS, PE = 250.0, 800.0, 100.0, 180.0, 0.5
 WINDOW, TRIES, SWEEPS, HEAT = 140, 6000, 2, 60.0
@@ -26,6 +27,8 @@ TAG = float(1 << 21)
 BETA = 1024.0
 M64 = 1.5 * 2.0 ** 29
 M4096 = 1.5 * 2.0 ** 35
+M1 = 1.5 * 2.0 ** 23
+Q0 = 128
 KW = 19
 
 SCRATCH = {}
@@ -37,16 +40,16 @@ def _decl(dt_, spec):
         SCRATCH[name] = ("sbuf", [128] + [int(x) for x in n.split("x")], dt_)
 
 
-_decl("bfloat16", "Q:4352 ST:4352 K1:4352 BITS:4096 XG:4096 AB:4096 AREP:4096 MT:4096 MPP:4096 AV:2048 SBQ:5x768 "
-      "LAND:5x96 SG:768 BH:1024 IDb:128 nIDb:128 BLKb:128 XP:128 I65:152 DIFF:152 MRH:456 RS:152 RESET:256 "
+_decl("bfloat16", "Q:4480 ST:4352 K1:4352 BITS:4096 XG:4096 AB:4096 AREP:4096 MT:4096 MPP:4096 AV:2048 SBQ:5x768 "
+      "LAND:5x96 SG:96 BH:1024 IDb:128 nIDb:128 BLKb:128 XP:128 I65:152 DIFF:152 MRH:456 RS:152 RESET:256 "
       "NRM:256 RM:256 RMH:128 NM:128 MC:512 ONES:512 Q8:24 BO:16 B2:144 B0:144 B10:144 B23:144 B45:144 TRI:128 TRIx:128 "
       "TRIB:128 NTM:128 SEL:640 SELJ:128 DG:640 DM:128 KEEP:128 SHIFT:128 PO:256 MSW:640 ROT:1536 "
-      "UP:384 STP:456 X3:384 QA:256 QC:256 GSA:256 GSC:256 GM:256 GS2:256 EQ:256 GA:512 MR:256 MG:256 DJ:128 "
+      "UP:384 STP:456 X3:384 QA:256 QC:256 GSA:256 GSC:256 GM:256 EQ:256 GA:512 MR:256 MG:256 DJ:128 "
       "GB:512 U2:256 GK:256 SGN:512 JUNK:1024 YS:256 VV:512 FW:128 CTX:128 IND:16x128 JB3:16x16 IND2:256 XS:256 "
-      "RF:16 RR:96 RA:96 TQ:96 QM:192 SW:288 GMM:192 KR:192 C16B:32")
-_decl("float16", "RW:4096 W16:512 Y:256 CF:256 XH:384 KM:128 H16:768 T16:32 T80:64")
+      "RF:16 RR:288 QM:192 SW:288 GMM:192 KR:192 C16B:32 AT:256 REP:512")
+_decl("float16", "RW:4096 W16:512 Y:256 CF:256 XH:384 KM:128 H16:768 T16:32 T80:80")
 _decl("float32", "CT:4112 JF:256 COL:128 IDf:256 BLKf:128 CN:128 Q8f:8 TMP:512 BLD:768 A2:256 PM:9x152 "
-      "CS:9x152 X2:384 SC:1024 SM:832 LS:96 LW2:96 LO:96 PFW:136")
+      "CS:9x152 X2:384 SC:1024 SM:832 LS:96 LW2:96 LO:96 PFW:136 SGF:1280")
 _decl("int32", "IB:400 SI:512 BD:32 PI:32")
 _decl("uint16", "C16:256 L16:192 P16:384")
 for _b in range(8):
@@ -219,8 +222,10 @@ def build(g, T, topo, core):
     dma("g", T.IB[:, 388:389], T.kk[:], [], [r("IB", 388, 392)], 2000, True)
     mset(r("IB", 392, 396), 0)
     dma("g", T.IB[8:128:16, 392:393], T.th[:], [], [r("IB", 392, 396)], 2000, True)
-    dma("s", T.Q[:, 0:2048], T.rec[:, 0:2048], [], [r("Q", 0, 2048)], 4500)
-    dma("y", T.Q[:, 2048:4096], T.rec[:, 2048:4096], [], [r("Q", 2048, 4096)], 4500)
+    QW = r("Q", Q0)
+    for j, q in enumerate("sy"):
+        x = r("Q", Q0 + 2048 * j, Q0 + 2048 * j + 2048)
+        dma(q, x[0], T.rec[:, 2048 * j:2048 * j + 2048], [], [x], 4500)
     NS = len(STREAMS)
     bonus[0] = 9000.0
     iota(r("PI", 0, 1), [[0, 1]], 0, 1)
@@ -331,7 +336,7 @@ def build(g, T, topo, core):
     select(r("TRI"), r("ONES", 0, 128), 0, A.is_ge)
     select(r("TRIx"), r("ONES", 0, 128), 0, A.is_gt)
     select(r("TRIB"), r("BLKb"), 0, A.is_ge)
-    fill(r("Q", 4096, WD), 0)
+    fill(r("Q", Q0 + 4096), 0)
     LW = sm(0)
     ts(LW, r("JF", 0, 256, 16), PR, A.add, 4096.0, A.add)
     act(col(52), PG, bias=2.0, scale=KW - 16.0)
@@ -359,6 +364,10 @@ def build(g, T, topo, core):
     for j in range(4):
         scaled(blk("SEL", j), r("BLKb"), col(56 + j))
     SELID, SELP, SELM, SELMP, SELLO = [blk("SEL", j) for j in range(5)]
+    iota(r("SGN"), [[1, 32], [0, 16]])
+    ts(r("PI", 7, 8), r("PI", 0, 1), 31, A.bitwise_and)
+    cp(col(62), r("PI", 7, 8))
+    ts(r("REP"), r("SGN"), col(62), A.is_equal)
     fill(r("PFW", 128, 136), 4096)
     for f in range(NS):
         ts(col(104 + f), PG, 8.0 - S_IND[f], A.is_ge, 128.0, A.mult)
@@ -402,14 +411,16 @@ def build(g, T, topo, core):
         fill(r("K1", 0, 2176), 5)
         dma("y", T.K1[:, 2176:WD], T.K1[:, 0:2176], [r("K1", 0, 2176)], [r("K1", 2176, WD)], 4000)
         cp(L3, r("JF", 5, 48, 6))
-        act(col(61), oh(10), scale=1.0 / 8192)
+        act(col(61), oh(0), bias=oh(14), scale=2.0 ** 20)
         scaled(SELLO, r("BLKb"), col(61))
+        ts(col(63), PR, 12.0, A.is_ge)
+        ts(sm(288, RO), r("JF", 1, RO + 1), -1.0, A.mult, oh(0), A.mult)
         scaled(r("B10"), r("B2"), oh(10))
         scaled(r("B23"), r("B2"), col(57))
         scaled(r("B45"), r("B2"), col(58))
         select(r("NTM"), r("BLKb"), 0, A.is_gt, sign=-1)
         iota(r3s("SBQ", 0, RO, 0, 96), [[0, RO * 96]], -1)
-        fill(r("SG", 0, 96), 0)
+        fill(r("SGF", 0, 96), 4096)
         act(col(64, 12), col(16, 12), bias=1.0, scale=-2.0)
         act(col(76), oh(12), bias=oh(13))
         act(col(77), col(76), bias=oh(14), scale=4.0)
@@ -471,6 +482,7 @@ def build(g, T, topo, core):
         act(sm(80), LW, bias=-3840.0)
         iota(sm(688, 48), [[0, 3], [16, 16]])
         ts(r("T80", 0, 48), sm(688, 48), PR, A.add)
+        cp(r("T80", 48, 64), sm(80))
         act(col(94), PR, bias=239.0)
         fill(r("C16B", 0, 16), 16)
         act(sm(112, 6), sm(688, 6), bias=PR)
@@ -492,7 +504,7 @@ def build(g, T, topo, core):
             o += n
         scan(out, r("RESET", 0, o - lo), ps(b, lo, o), A.add, A.min)
 
-    live, ends = r("T80", 48, 64), sm(448, 48)
+    live, ends = r("T80", 64, 80), sm(448, 64)
 
     def lanes(t):
         s = (STEP * t) & 2047
@@ -544,6 +556,10 @@ def build(g, T, topo, core):
 
     stage = [0]
 
+    def minus_a(f, j):
+        p = slice(32 * j, 32 * j + 32)
+        return r("AT", 128 * f, 128 * f + 128, p=p), r("REP", p=p)
+
     def hop(t, h, f):
         lo, hi = STREAMS[f]
         n, e, o, end = hi - lo, HO * f + h, lo // 16, h == HO - 1
@@ -588,7 +604,7 @@ def build(g, T, topo, core):
             mms([(ps(f, 138 + i, 288, KW, p=slice(x, z)), r(src, 16 * (lo + x) + i, 16 * (lo + z), 16), bo, False, stop and i == 15)
                  for i in range(16)], 8)
             name("%s%da %s%db" % (src[0], j0, src[0], j0))
-        got = lambda x, z: ind(r("Q"), r("C16", x // 16, z // 16))
+        got = lambda x, z: ind(QW, r("C16", x // 16, z // 16))
         bank, todo = {}, [set(range(j0, j1)) for j0, j1 in PARTS]
         for step in (LAST_STEPS if end and f == NS - 1 else STEPS).split():
             kind, j = step[0], int(step[1])
@@ -597,12 +613,12 @@ def build(g, T, topo, core):
                 bank[j] = ps(STAGE[stage[0] % len(STAGE)], 0, b - a)
                 stage[0] += 1
                 act(r("XG", a, b), got(a, b), F.Copy)
-                mm([(bank[j], r("nIDb"), r("AREP", a, b), True, False)])
-                mm([(bank[j], ID, r("XG", a, b), False, True)], acc=True)
+                mm([(bank[j],) + minus_a(f, j) + (True, False)])
+                mm([(bank[j], ID, r("XG", a, b), False, True)])
                 name("g%d n%d x%d" % (j, j, j))
             elif kind == "s":
                 for x in range(a, b, V_CUT):
-                    tt(r("XG", x, x + V_CUT), got(x, x + V_CUT), r("AREP", x, x + V_CUT), A.subtract)
+                    tt(r("XG", x, x + V_CUT), got(x, x + V_CUT), r("AREP", x, x + V_CUT), A.add)
                 name("s%da s%db" % (j, j))
             elif kind == "a":
                 act(r("AB", a, b), bank.get(j) or r("XG", a, b), F.Abs)
@@ -632,7 +648,7 @@ def build(g, T, topo, core):
                 act(c("GM"), ind(r("ST"), lst(hL, f)), F.Copy)
             r2w(f, 0, [(SELMP, c("GM"))], c("SC"))
             ts(lst(mpL, f), r("SC", lo + 15, hi, 16), 2048.0, A.add)
-            tt(c("Y"), ind(r("Q"), lst(mpL, f)), c("A2"), A.add)
+            tt(c("Y"), ind(QW, lst(mpL, f)), c("A2"), A.add)
             name("tH GM N SEL sM tM Y")
             return
         cl = lst(cL, f)
@@ -654,7 +670,8 @@ def build(g, T, topo, core):
         mm([(raw, r("SELJ"), c("GSC"), False, True)], acc=True)
         tt(c("U2"), c("GB"), raw, A.max)
         scaled(r("GB", 256 + lo, 256 + hi), c("GB"), col(99))
-        cp(ind(r("K1"), lst(aS, f)), c("U2"))
+        act(c("GM"), c("U2"), bias=sm(288 + t, 1), scale=col(63))
+        cp(ind(r("K1"), lst(aS, f)), c("GM"))
         for j in range(2):
             a, z = max(lo, 128 * j), min(hi, 128 * j + 128)
             if a < z and n < 128:
@@ -687,12 +704,15 @@ def build(g, T, topo, core):
                     if who == "v":
                         red(r("LW2", at + slot, at + slot + 1), a, A.max)
                     else:
-                        act(r("JUNK", 512 * (b % 2), 512 * (b % 2) + wide), a, F.Relu, bias=r("LS", at + 2, at + 3),
+                        act(r("MPP", 512 * k, 512 * k + wide), a, F.Relu, bias=r("LS", at + 2, at + 3),
                             accum=r("LS", at + 3 + slot, at + 4 + slot))
 
     def swap(b, lo, n, ms, src, first, last):
         out = [(ps(b, lo + j, lo + n, 2), m, src(1 - j), first, first) for m in ms for j in range(2)]
         return out[:-1] + [out[-1][:4] + (last,)]
+
+    def silu(win, to, more=0):
+        add("s", [lambda: g.scalar.activation(ind(win, to)[0], T.A2[:], F.Silu)], [r("A2"), to], [win], 65 + 3.8 * 256 + more)
 
     def put_out(out, b, n, sel, o):
         mms([(ps(b, 0, n), r(sel, 15 - j, 143 - j), blk("ST", j, n), j == 0, j == 15) for j in range(16)], 2)
@@ -707,20 +727,19 @@ def build(g, T, topo, core):
         last = t == RO - 1
         for f, (lo, hi) in enumerate(STREAMS):
             bonus[0] = SKEW * (NS - 1 - f)
-            act(r("QA", lo, hi), ind(r("Q"), lst(aL, f)), F.Copy)
+            act(r("QA", lo, hi), ind(QW, lst(aL, f)), F.Copy)
             act(r("GSA", lo, hi), ind(r("ST", 0, 2048), lst(aL, f)), F.Copy)
             mm([(ps(6, lo, hi), SELID, r("GSA", lo, hi), True, True)])
-            for (x, z), n in zip(A_RUNS, A_S):
-                if z == hi:
-                    ax = ps(7, 256 + x, 256 + z)
-                    mm([(ax, r("XP"), r("QA", x, z), True, True)])
-                    rep = lambda i: (T.AREP[:, 16 * x + i:16 * z:16], "AREP", 16 * x, 16 * z, i, z - x)
-                    for i in range(16):
-                        if i < n:
-                            act(rep(i), ax, F.Copy)
-                        else:
-                            cp(rep(i), rep(0))
-                    act(r("A2", x, z), ax, bias=OFFA)
+            ax, at = ps(7, 256 + lo, 256 + hi), ps(2 + f, 128, 256)
+            mm([(at, r("QA", lo, hi), r("XP"), True, True)])
+            scaled(blk("AT", f), at, -1.0)
+            for j, who in enumerate(A_REP[f]):
+                if who != "-":
+                    b = ps(A_BANK[f][j])
+                    mm([(b,) + minus_a(f, j) + (True, True)])
+                    (cp if who == "v" else lambda o, a: scaled(o, a, 1.0))(blk("AREP", 4 * f + j, 512), b)
+            mm([(ax, r("XP"), r("QA", lo, hi), True, True)])
+            act(r("A2", lo, hi), ax, bias=OFFA)
         bonus[0] = 0.0
         if t:
             later[0]()
@@ -731,9 +750,11 @@ def build(g, T, topo, core):
             bonus[0] = 0.0
             if h == 0:
                 if t == 0:
-                    bonus[0] = -30000.0
+                    n0 = len(ops)
                     late_constants()
-                    bonus[0] = 0.0
+                    for x in ops[n0:]:
+                        if x["eng"] in "sv":
+                            x["after"] = max(i for i in range(n0) if ops[i].get("hop") == (0, LATE))
                 act(r("GA", 0, 256), ind(r("BITS"), lst(aL)), bias=col(82 + t))
                 scaled(r("GA", 256, 512), r("GA", 0, 256), col(99))
         act(r("GK"), ind(r("K1"), lst(cL)), F.Copy)
@@ -742,18 +763,22 @@ def build(g, T, topo, core):
         act(r("LS", 5, 96, 6), ps(6, 256, 272), F.Relu, scale=-2.0)
         r2w(7, 0, [(SELP, r("GSC"))], r("SC", 256, 512))
         act(sm(480), r("SC", 271, 512, 16), bias=2048.0)
-        mm([(ps(6, 272, 336), ID, r("T80"), True, False), (ps(6, 272, 320), M4K, ones(48), False, False)])
+        r2w(7, 0, [(SELLO, r("GK"))], r("SC", 0, 256))
+        act(sm(336), r("SC", 15, 256, 16), bias=(t + 1) * 2.0 ** 20)
+        tt(sm(496), sm(336), sm(80), A.min)
+        fill(r("SGF", 768, 1024), 0)
+        mm([(ps(6, 272, 352), ID, r("T80"), True, False), (ps(6, 272, 320), M4K, ones(48), False, False)])
         pairs(0, 1, [("GB", 128, 256), ("GA", 128, 256)], PAIRS[2])
         pairs(1, 1, [("GB", 0, 256), ("GA", 128, 256)], PAIRS[3])
         for f in range(2):
             o = 8 * f
             scan(blk("LO", f, 48), blk("LS", f, 48), blk("LW2", f, 48), A.add, A.max)
             tt(blk("XS", f), ind(blk("LO", f, 48), L3), r("RMH"), A.is_equal)
-            mm([(ps(6, 272 + 16 * j + o, 280 + 16 * j + o), blk("XS", f), Q8n, False, j == 3 and f == 1) for j in range(4)], acc=True)
-        act(r("QC"), ind(r("Q"), lst(cL)), F.Copy)
-        tt(r("TMP", 0, 48), ps(6, 272, 320), ends, A.max)
-        cp(r("P16", 0, 48), r("TMP", 0, 48))
-        jA, jC, jO = r("P16", 0, 16), r("P16", 16, 32), r("P16", 32, 48)
+            mm([(ps(6, 272 + 16 * j + o, 280 + 16 * j + o), blk("XS", f), Q8n, False, j == 4 and f == 1) for j in range(5)], acc=True)
+        act(r("QC"), ind(QW, lst(cL)), F.Copy)
+        tt(r("TMP", 0, 64), ps(6, 272, 336), ends, A.max)
+        cp(r("P16", 0, 64), r("TMP", 0, 64))
+        jA, jC, jO, jL = (blk("P16", j, 16) for j in range(4))
         mm([(ps(7, 256, 512), blk("PO", j), r("GSC"), j == 0, j == 1) for j in range(2)])
         act(r("YS"), ps(7, 256, 512), bias=col(90))
         for j, (x, z) in enumerate((("GSC", "GSA"), ("GSA", "GSC"))):
@@ -762,15 +787,19 @@ def build(g, T, topo, core):
         act(r("VV"), ps(5), bias=col(100))
         mm([(ps(7, 0, 256), r("XP"), r("QC"), True, False), (ps(7, 0, 256), r("nIDb"), r("QA"), False, True)])
         mm([(ps(7, 256, 512), r("XP"), r("QA"), True, False), (ps(7, 256, 512), r("nIDb"), r("QC"), False, True)])
+        act(r("A2"), r("GSA"), bias=4096.0)
+        bonus[0] = 4000.0
+        silu(r("SGF", 768, 1280), jL, 0 if t else 1300)
+        bonus[0] = 0.0
         act(r("SGN"), ps(7), F.Sign)
         cp(ind(r("ST"), jO), r("YS"))
         cp(ind(r("ST"), jC), r("VV", 0, 256))
-        act(r("GS2"), ind(r("ST"), lst(aL)), F.Copy)
+        bonus[0] = 3000.0
         cp(ind(r("ST"), jA), r("VV", 256, 512))
-        bonus[0] = 2000.0
-        r2w(4, 0, [(SELLO, r("GS2"))], r("SC", 0, 256))
+        bonus[0] = 5000.0
+        r2w(4, 0, [(r("BLKf"), r("SGF", 768, 1024))], r("SC", 0, 256))
         t1 = r("T16", 0, 16)
-        tt(r("RF"), r("SC", 15, 256, 16), ps(6, 320, 336), A.mult)
+        tt(r("RF"), r("SC", 15, 256, 16), ps(6, 336, 352), A.is_lt)
         tt(t1, r("RF"), sm(80), A.mult)
         mm([(ps(4, 256, 272), r("TRIB"), r("RF"), True, False), (ps(4, 257, 272), r("NTM"), r("RF", 0, 15), False, False),
             (ps(4, 256, 272), r("nIDb"), t1, False, False), (ps(4, 257, 272), ID, r("T16", 0, 15), False, True)])
@@ -790,9 +819,13 @@ def build(g, T, topo, core):
         n = sm(303, 1)
         mm([(ps(5, 496, 512), r("BLKb"), r("RF"), True, True)])
         act(sm(272), ps(5, 496, 512), F.Copy, scale=-8192.0, accum=n)
-        cp(ind(r("SG"), dL), r("GSA"))
-        tt(ind(r("Q"), jA), r("SGN", 0, 256), r("QA"), A.add)
-        tt(ind(r("Q"), jC), r("SGN", 256, 512), r("QC"), A.add)
+        silu(r("SGF", 0, 768), dL)
+        act(r("TMP", 128, 224), r("SGF", 0, 96), bias=M1 - 4096.0)
+        act(r("SG", 0, 96), r("TMP", 128, 224), bias=-M1)
+        bonus[0] = -3000.0
+        tt(ind(QW, jA), r("SGN", 0, 256), r("QA"), A.add)
+        tt(ind(QW, jC), r("SGN", 256, 512), r("QC"), A.add)
+        bonus[0] = 0.0
         if last:
             put_out(T.yp[:], 0, 256, "B23", 0)
         else:
@@ -805,7 +838,7 @@ def build(g, T, topo, core):
         tt(sm(574, 12), r("SC", 271, 448, 16), sm(550, 12), A.max)
         ts(r("L16", kL, kL + 18), sm(568, 18), 2048.0, A.add)
         sL, vsL, vmL, pmL = [r("L16", kL + 6 * j, kL + 6 * j + 6) for j in range(4)]
-        act(r("QM", 0, 96), ind(r("Q"), vmL), F.Copy)
+        act(r("QM", 0, 96), ind(QW, vmL), F.Copy)
         sg = lambda j: r("SG", j, 96, 2)
         mm(swap(5, 0, 96, [blk("MSW", 0)], sg, True, True) + swap(5, 96, 96, [blk("MSW", 1)], sg, True, True) +
            [(ps(5, 192, 288), blk("MSW", 4), r("SG", 0, 96), True, False)] +
@@ -814,25 +847,35 @@ def build(g, T, topo, core):
         UP, nUP, LOW = (blk("UP", j) for j in range(3))
         mm([(ps(4, 0, 96), LOW, r("QM", 0, 96), True, False)] + swap(4, 0, 96, [UP], lambda j: r("QM", j, 96, 2), False, True))
         act(r("QM", 96, 192), ps(4, 0, 96), F.Copy)
-        cp(ind(r("Q"), vmL), r("QM", 96, 192))
+        cp(ind(QW, vmL), r("QM", 96, 192))
         land = lambda j, x=0, s=1: r3("LAND", t, 32 * j + x, 32 * j + 32, s)
         mm([(ps(7, 0, 96), ID, r3("SBQ", t, 0, 96), True, False)])
         mm([(ps(7, 32 * j, 32 * j + 32), blk("ROT", 3 + j), land(j), False, j == 2) for j in range(3)], acc=True)
-        act(r("RR"), ps(7, 0, 96), F.Relu, bias=-255.0)
+        RR, RA, TQ = (blk("RR", j, 96) for j in range(3))
+        act(RR, ps(7, 0, 96), F.Relu, bias=-255.0)
         mm([(ps(6, 352, 448), ZERO, ones(96), True, False)])
         mm([(ps(6, 352 + 32 * j, 384 + 32 * j), blk("ROT", j), land(j), False, False) for j in range(3)], acc=True)
-        mm([(ps(6, 352, 448), ID, r("RR"), False, True)], acc=True)
-        act(r("RA"), ps(6, 352, 448), F.Copy)
-        mm([(ps(4, 384, 480), ZERO, ones(96), True, False)])
-        mm([x for j in range(3) for x in [(ps(4, 384 + 32 * j, 416 + 32 * j), blk("ROT", 9 + j), land(j), False, False)] +
-            swap(4, 384 + 32 * j, 32, [blk("ROT", 6 + j)], lambda x, j=j: land(j, x, 2), False, False)], acc=True)
-        mm([(ps(4, 384, 480), nUP, r("RR"), False, False)] +
-           swap(4, 384, 96, [UP], lambda j: r("RR", j, 96, 2), False, True), acc=True)
-        tt(r("TQ"), ps(4, 384, 480), r("KR", 96, 192), A.mult)
-        tt(ind(r("Q"), sL), r("TQ"), r("RA"), A.add)
+        mm([(ps(6, 352, 448), ID, RR, False, True)], acc=True)
+        act(RA, ps(6, 352, 448), F.Copy)
+        mm([(ps(1, 384, 480), ZERO, ones(96), True, False)])
+        mm([x for j in range(3) for x in [(ps(1, 384 + 32 * j, 416 + 32 * j), blk("ROT", 9 + j), land(j), False, False)] +
+            swap(1, 384 + 32 * j, 32, [blk("ROT", 6 + j)], lambda x, j=j: land(j, x, 2), False, False)], acc=True)
+        mm([(ps(1, 384, 480), nUP, RR, False, False)] +
+           swap(1, 384, 96, [UP], lambda j: r("RR", j, 96, 2), False, True), acc=True)
+        tt(TQ, ps(1, 384, 480), r("KR", 96, 192), A.mult)
         if last:
-            dma("y", T.yq[:, 0:2048], T.Q[:, 0:2048], [r("Q", 0, 2048)], [], 4000)
-            dma("s", T.yq[:, 2048:4096], T.Q[:, 2048:4096], [r("Q", 2048, 4096)], [], 4000)
+            dma("y", T.yq[:, 2048:4096], T.Q[:, Q0 + 2048:Q0 + 4096], [r("Q", Q0 + 2048, Q0 + 4096)], [], 4000)
+            act(sm(624, 6), sm(512, 6), scale=-1.0)
+            act(sm(632, 6), sm(0, 6), bias=-6144.0 - Q0)
+            tt(sm(640, 6), sm(624, 6), sm(632, 6), A.max)
+            tt(sm(648, 6), r("SC", 271, 352, 16), sm(640, 6), A.min)
+            ts(pmL, sm(648, 6), 2048.0 + Q0, A.add)
+            tt(ind(r("Q", 0, Q0 + 2048), pmL), TQ, RA, A.add)
+            for j, q in enumerate("ys"):
+                dma(q, T.yq[:, 1024 * j:1024 * j + 1024], T.Q[:, Q0 + 1024 * j:Q0 + 1024 * j + 1024],
+                    [r("Q", Q0 + 1024 * j, Q0 + 1024 * j + 1024)], [], 3000)
+        else:
+            tt(ind(QW, sL), TQ, RA, A.add)
         cp(ind(r("ST"), vsL), r("SW", 192, 288))
         if last:
             put_out(T.ym[:], 1, 128, "B45", 256)
@@ -841,7 +884,7 @@ def build(g, T, topo, core):
                 gm, gp = r("GMM", 0, 96), r("GMM", 96, 192)
                 act(gm, ind(r("ST"), vmL), F.Copy, scale=col(91))
                 tt(ind(r("ST"), vmL), gm, r("SW", 0, 96), A.add)
-                r2w(4, 0, [(SELP, gm)], r("SC", 512, 608))
+                r2w(3, 0, [(SELP, gm)], r("SC", 512, 608))
                 tt(sm(624, 6), r("SC", 527, 608, 16), sm(550, 6), A.max)
                 ts(pmL, sm(624, 6), 2048.0, A.add)
                 act(gp, ind(r("ST"), pmL), F.Copy, scale=col(92))
@@ -875,6 +918,8 @@ def depend(ops, turns=None):
                     keep.append(e)
                 keep.append((i, kind, lo, hi, row))
                 hist[name] = keep
+        if turns and "after" in o:
+            deps.setdefault(o["after"], False)
         o["deps"] = deps
     for text in (turns or {}).values():
         place = {x.rstrip("'"): (x.count("'"), k) for k, x in enumerate(text.split())}

@@ -10,19 +10,23 @@ STEPS = "g0 s2 g3 s1 a0 r1 a2 a3"
 LAST_STEPS = STEPS
 STAGE = (4, 5, 7)
 GM_V = False
-EARLY = 9000.0
+C_CUT = 32
+EARLY, TABLE, FIRST, WRAP, MATES, MP_V = 5000.0, 12000.0, 5000.0, 0.0, 2000.0, 2
 LATE = "PM"
-TEMPLATE = {"v": "sM'' s2a' tM'' Y'' r1' sU tU C PM' CF NE' CS' EQ XH' s1b tH' s1a s2b", "s": "a2' g0 g3 GM' a0 a3"}
+TEMPLATE = {"v": "sM'' tM'' Y'' r1' sU tU C PM' C2 NE' CF CS' EQ XH' s1a tH' s2a s2b s1b", "s": "a2' g0 g3 GM' a0 a3"}
 PAIRS = ([("s", (3,), (0, 1, 2, 3, 4, 5)), ("v", (2, 0), (6, 7))], [("v", (2, 0), (0, 1, 2, 3, 4, 5, 6, 7))],
-         [("s", (3, 1, 5), (0, 1, 2, 3)), ("v", (2, 0, 4), (4, 5, 6, 7))],
+         [("s", (3, 1, 5), (0, 1)), ("v", (2, 0, 4), (2, 3, 4, 5, 6, 7))],
          [("s", (3, 1, 5), (0, 2, 4, 6)), ("v", (2, 0, 4), (1, 3, 5, 7))])
 PARTS = ((0, 4),)
-S_IND = (5, 8, 8)
+S_IND = (3, 4)
 A_REP = ("-vv-", "-ss-")
 A_BANK = ((0, 5, 2, 0), (0, 2, 3, 0))
+AT_BANK = (2, 3)
 V_CUT = 256
-LOOK, SKEW, SAME, CROSS, PE = 250.0, 800.0, 100.0, 180.0, 0.5
-WINDOW, TRIES, SWEEPS, HEAT = 140, 6000, 2, 60.0
+LOOK, SKEW, SAME, CROSS, PE = 350.0, 800.0, 110.0, 195.0, 0.5
+FAR, REACH = 3500.0, 8
+URGE = (6000.0, 3000.0, 5000.0)
+WINDOW, TRIES, SWEEPS, HEAT = 100, 6000, 4, 70.0
 TAG = float(1 << 21)
 BETA = 1024.0
 M64 = 1.5 * 2.0 ** 29
@@ -40,21 +44,21 @@ def _decl(dt_, spec):
         SCRATCH[name] = ("sbuf", [128] + [int(x) for x in n.split("x")], dt_)
 
 
-_decl("bfloat16", "Q:4480 ST:4352 K1:4352 BITS:4096 XG:4096 AB:4096 AREP:4096 MT:4096 MPP:4096 AV:2048 SBQ:5x768 "
-      "LAND:5x96 SG:96 BH:1024 IDb:128 nIDb:128 BLKb:128 XP:128 I65:152 DIFF:152 MRH:456 RS:152 RESET:256 "
+_decl("bfloat16", "Q:4480 ST:4352 BITS:4096 XG:4096 AB:4096 AREP:4096 MT:4096 MPP:4096 AV:2048 SBQ:5x768 "
+      "LAND:5x96 SG:96 BH:1024 IDb:128 nIDb:128 BLKb:128 XP:128 I65:152 DIFF:152 MRH:456 RS:152 RESET:512 "
       "NRM:256 RM:256 RMH:128 NM:128 MC:512 ONES:512 Q8:24 BO:16 B2:144 B0:144 B10:144 B23:144 B45:144 TRI:128 TRIx:128 "
       "TRIB:128 NTM:128 SEL:640 SELJ:128 DG:640 DM:128 KEEP:128 SHIFT:128 PO:256 MSW:640 ROT:1536 "
-      "UP:384 STP:456 X3:384 QA:256 QC:256 GSA:256 GSC:256 GM:256 EQ:256 GA:512 MR:256 MG:256 DJ:128 "
+      "UP:384 STP:456 X3:384 QA:256 QC:256 GSA:256 GSC:256 GM:256 EQ:256 GA:512 MR:256 MG:128 DJ:128 "
       "GB:512 U2:256 GK:256 SGN:512 JUNK:1024 YS:256 VV:512 FW:128 CTX:128 IND:16x128 JB3:16x16 IND2:256 XS:256 "
-      "RF:16 RR:288 QM:192 SW:288 GMM:192 KR:192 C16B:32 AT:256 REP:512")
+      "RF:16 RR:288 QM:192 SW:288 GMM:192 KR:192 C16B:32 AT:384 REP:512")
 _decl("float16", "RW:4096 W16:512 Y:256 CF:256 XH:384 KM:128 H16:768 T16:32 T80:80")
 _decl("float32", "CT:4112 JF:256 COL:128 IDf:256 BLKf:128 CN:128 Q8f:8 TMP:512 BLD:768 A2:256 PM:9x152 "
-      "CS:9x152 X2:384 SC:1024 SM:832 LS:96 LW2:96 LO:96 PFW:136 SGF:1280")
+      "CS:9x152 X2:384 SC:1024 SM:832 LS:96 LW2:96 LO:96 PFW:136 SGF:1792 K1:4352")
 _decl("int32", "IB:400 SI:512 BD:32 PI:32")
 _decl("uint16", "C16:256 L16:192 P16:384")
 for _b in range(8):
     SCRATCH["ps%d" % _b] = ("psum", [128, 512], "float32")
-NDMA = 36
+NDMA = 46
 SEMAPHORES = ["ev", "es", "et", "eg", "sent"] + ["arr%d" % t for t in range(RO)] + ["d%d" % i for i in range(NDMA)]
 
 
@@ -217,27 +221,33 @@ def build(g, T, topo, core):
 
     bonus[0] = 20000.0
     dma("y", T.IB[:, 0:256], T.pr[:], [], [r("IB", 0, 256)], 2000)
-    dma("g", T.IB[:, 384:385], T.w[:], [], [r("IB", 384, 388)], 2000, True)
+    dma("s", T.IB[:, 384:385], T.w[:], [], [r("IB", 384, 388)], 2000)
     dma("y", T.IB[:, 256:384], T.mt[:], [], [r("IB", 256, 384)], 2000)
-    dma("g", T.IB[:, 388:389], T.kk[:], [], [r("IB", 388, 392)], 2000, True)
+    dma("s", T.IB[:, 388:389], T.kk[:], [], [r("IB", 388, 392)], 2000)
     mset(r("IB", 392, 396), 0)
-    dma("g", T.IB[8:128:16, 392:393], T.th[:], [], [r("IB", 392, 396)], 2000, True)
+    dma("s", T.IB[8:128:16, 392:393], T.th[:], [], [r("IB", 392, 396)], 2000)
     QW = r("Q", Q0)
     for j, q in enumerate("sy"):
         x = r("Q", Q0 + 2048 * j, Q0 + 2048 * j + 2048)
         dma(q, x[0], T.rec[:, 2048 * j:2048 * j + 2048], [], [x], 4500)
     NS = len(STREAMS)
-    bonus[0] = 9000.0
+    bonus[0] = 30000.0
     iota(r("PI", 0, 1), [[0, 1]], 0, 1)
     iota(r("JF"), [[1, 256]])
-    iota(r("MG"), [[1, 16], [0, 16]])
+    iota(r("MG"), [[1, 8], [0, 16]])
     iota(r("MR"), [[0, 16], [1, 16]])
     iota(r("DJ"), [[1, 128]], 0, -1)
+    iota(r("AV"), [[8, 16], [0, 8], [128, 16]], -2048)
+    rows(r("AV", row=5), r("MG"))
     bonus[0] = EARLY
     iota(r3s("JB3", 0, 16, 0, 16), [[1, 256]])
     PF, PR, PG = col(0), col(1), col(2)
     DJ, ID = r("DJ"), r("IDb")
-    mset(r("ST"), 0.0)
+    for row in (6, 7, 11, 12, 13, 14, 15):
+        dma("y", T.ST[row:128:16, 0:4096], T.rec[0:8, :], [], [r("ST", 0, 4096, row=row)], 2500)
+    for row in (4, 5):
+        dma("y", T.ST[row:128:16, 2048:4096], T.rec[0:8, 0:2048], [], [r("ST", 2048, 4096, row=row)], 2500)
+    mset(r("ST", 4096), 0.0)
     dma("y", T.MT[:, 0:2048], T.rec[:, 0:2048], [], [r("MT", 0, 2048)], 4500)
     ts(r("PI", 1, 2), r("PI", 0, 1), 15, A.bitwise_and)
     ts(r("PI", 2, 3), r("PI", 0, 1), 4, A.logical_shift_right)
@@ -251,8 +261,10 @@ def build(g, T, topo, core):
     scaled(col(4), PR, 256.0)
     act(ids, r("JF"), bias=col(4))
     lob = r("XS")
+    bonus[0] = FIRST
     tt(lob, r("IB", 0, 256), ids, A.is_equal)
     rows(r("MPP", p=slice(0, 8)), lob)
+    bonus[0] = EARLY
     ts(ID, DJ, 0.0, A.is_equal)
     scaled(blk("IDf", 0), ID, 1.0)
     scaled(blk("IDf", 1), ID, -1.0)
@@ -270,6 +282,7 @@ def build(g, T, topo, core):
     OFF, OFFA = col(13), col(15)
     act(OFF, col(8), bias=2048.0, scale=-4608.0)
     act(OFFA, col(8), bias=2047.5, scale=-4608.0)
+    bonus[0] = EARLY + TABLE
     cp(col(5, 3), r("IB", 384, 396, 4))
     ts(r("TMP", 0, 1), col(5), 0.5, A.mult, OFF, A.mult)
     scaled(r("TMP", 1, 2), col(7), 1.0)
@@ -282,7 +295,8 @@ def build(g, T, topo, core):
     scaled(col(33), r("C16B", 16, 17), 1.0)
     tt(col(34), ps(7, 1, 2), col(33), A.subtract)
     scaled(col(38), ps(3, 0, 1), 1.0)
-    ts(r("CN"), r("ONES", 0, 128), r("TMP", 0, 1), A.mult, -1.0, A.mult)
+    act(col(11), r("TMP", 0, 1), scale=-1.0)
+    scaled(r("CN"), r("ONES", 0, 128), col(11))
     for j, (x, v) in enumerate(((5, 0.5), (5, -0.5), (38, 1.0), (38, -1.0))):
         ts(blk("W16", j), r("BLKb"), col(x), A.mult, v, A.mult)
     ts(r("SI", 0, 256), ids, col(32), A.add)
@@ -311,6 +325,7 @@ def build(g, T, topo, core):
              (b, Mn, ones(512), False, False), (b, r("KM", p=k24), x, False, True)], 1)
         act(blk("CT", j, 512), b, bias=2047.5)
     scaled(r("CT", 4096, 4097), r("CT", 0, 1), 1.0)
+    bonus[0] = EARLY
     ts(xs, r("IB", 0, 384), -2048.0, A.add)
     hi_, lo_ = r("JUNK", 0, 384), r("JUNK", 384, 768)
     scaled(hi_, xs, 1.0)
@@ -355,7 +370,8 @@ def build(g, T, topo, core):
         fill(r("MRH", 304 + j, 456, KW), 0)
     fill(r("RS"), 0)
     fill(r("RS", 0, 152, KW), 1 << 23)
-    act(r("RESET"), r("MR"), F.Relu, bias=2.0 ** 31, scale=-2.0 ** 31)
+    act(r("RESET", 0, 256), r("MR"), F.Silu, bias=2.0 ** 31, scale=-2.0 ** 31)
+    ops[-1]["cost"] += 1300
     ts(r("RM"), r("MR"), PR, A.is_equal)
     act(r("RMH"), r("RM", 0, 128), bias=0.5, scale=0.5)
     act(r("NRM"), r("RM"), bias=2.0 ** 25, scale=-2.0 ** 25)
@@ -374,7 +390,6 @@ def build(g, T, topo, core):
         act(col(108 + f), col(104 + f), bias=1.0, scale=-1.0 / 256)
         act(col(112 + f), col(108 + f), scale=16.0)
         act(col(120 + f), PF, bias=(STREAMS[f][0] + 1.0) * 2.0 ** 40, scale=2.0 ** 40)
-        iota(r3s("CS", HO * f, HO * f + HO, 0, 152), [[0, HO * 152]])
     fill(r("X3"), 0)
     fill(r("X3", 13, 128 * NS, 16), 2048)
     L3, LBC = r("L16", 16, 24), r("L16", 8, 16)
@@ -389,38 +404,39 @@ def build(g, T, topo, core):
         k16 = slice(0, 16)
         mms([(ps(6, 256, 512), r("B0", 15 - j, 143 - j, p=k16), r("AB", j, 4096, 16, p=k16), j == 0, j == 15) for j in range(16)], 2)
         ts(r("P16", 0, 256), ps(6, 256, 512), 2048.0, A.add)
+        ts(r("P16", 256, 384), r("IB", 256, 384), -2048.0, A.add)
+        bonus[0] = MATES
         for j in range(8):
-            ts(r("P16", 256 + 16 * j, 272 + 16 * j), r("IB", 256 + j, 384, 8), -2048.0, A.add)
-        iota(r("GM"), [[8, 16], [128, 16]], -2048)
-        scaled(r("GK"), r("GM"), oh(4))
-        ts(sm(64, 8), r("JF", 0, 8), oh(5), A.mult)
-        for j in range(8):
-            act(blk("AV", j, 256), r("GK"), bias=sm(64 + j, 1))
             cp(ind(r("MT", 2048, 4096), r("P16", 256 + 16 * j, 272 + 16 * j)), blk("AV", j, 256))
         bonus[0] = 0.0
         for j in range(16):
-            if j % 3 == 2:
+            if j % MP_V == 1:
                 cp(blk("MPP", j, 256), ind(r("MT"), blk("P16", j, 16)))
             else:
                 act(blk("MPP", j, 256), ind(r("MT"), blk("P16", j, 16)), F.Copy)
+
+    def start_rows():
         for j in range(2):
             rows(r("ST", 0, 4096, row=6 + j), r("MPP", 0, 4096, row=4 + j))
             rows(r("ST", 2048, 4096, row=4 + j), r("MT", 2048, 4096, row=4 + j))
 
     def late_constants():
-        fill(r("K1", 0, 2176), 5)
+        fill(r("K1", 0, 2176), 8192)
         dma("y", T.K1[:, 2176:WD], T.K1[:, 0:2176], [r("K1", 0, 2176)], [r("K1", 2176, WD)], 4000)
         cp(L3, r("JF", 5, 48, 6))
         act(col(61), oh(0), bias=oh(14), scale=2.0 ** 20)
         scaled(SELLO, r("BLKb"), col(61))
         ts(col(63), PR, 12.0, A.is_ge)
-        ts(sm(288, RO), r("JF", 1, RO + 1), -1.0, A.mult, oh(0), A.mult)
+        scaled(sm(296, RO), r("JF", 1, RO + 1), oh(0))
+        act(sm(288, RO), sm(296, RO), bias=64.0, scale=-1.0)
         scaled(r("B10"), r("B2"), oh(10))
         scaled(r("B23"), r("B2"), col(57))
         scaled(r("B45"), r("B2"), col(58))
         select(r("NTM"), r("BLKb"), 0, A.is_gt, sign=-1)
         iota(r3s("SBQ", 0, RO, 0, 96), [[0, RO * 96]], -1)
         fill(r("SGF", 0, 96), 4096)
+        fill(r("SGF", 1280, 1536), 0)
+        scaled(r("RESET", 256, 512), r("RESET", 0, 256), -1.0)
         act(col(64, 12), col(16, 12), bias=1.0, scale=-2.0)
         act(col(76), oh(12), bias=oh(13))
         act(col(77), col(76), bias=oh(14), scale=4.0)
@@ -535,18 +551,19 @@ def build(g, T, topo, core):
             o, z, b = lo // 16, hi // 16, 2 + f % 2
             part = lambda a, k, n: (a, "IND", 8 * f + k, 8 * f + k + n, None, hi - lo)
             act(col(116 + f), col(104 + f), bias=float(s), scale=8.0)
+            mm([(ps(b, 32, 40), r("TRI"), r("CTX", 0, 128, 16), True, True)])
             for k in range(8):
                 x = part(T.IND[:, o:z, 16 * k:16 * k + 16], k, 1)
                 if k < 8 - S_IND[f]:
-                    ts(x, r3s("JB3", o, z, 0, 16), sm(192 + k, 1), A.add, 0.0, A.is_gt)
+                    ts(x, r3s("JB3", o, z, 0, 16), ps(b, 32 + k, 33 + k), A.is_ge)
                 else:
                     act(x, r3s("JB3", o, z, 0, 16), F.Sign, bias=sm(192 + k, 1))
             mm([(ps(b, q, q + 1), part(T.IND[:, q, :], 0, 8), r("ONES", 0, 1), True, True) for q in range(o, z)])
             ts(lst(bL, f), ps(b, o, z), col(104 + f), A.add, col(108 + f), A.mult)
             act(sm(224 + o, z - o), ps(b, o, z), bias=col(116 + f), scale=col(112 + f))
             tt(r("IND2", lo, hi), ind(r("PFW"), lst(bL, f)), r("JF", lo, hi), A.is_le)
-            mms([(ps(b, 16 + o, 16 + z), r("B2", 15 - j, 143 - j), r("IND2", lo + j, hi, 16), j == 0, j == 15) for j in range(16)], 8)
-            tt(r("BD", 16 + o, 16 + z), sm(224 + o, z - o), ps(b, 16 + o, 16 + z), A.add)
+            r2w(0, 256, [(r("BLKb"), r("IND2", lo, hi))], r("SC", 768 + lo, 768 + hi))
+            tt(r("BD", 16 + o, 16 + z), sm(224 + o, z - o), r("SC", 768 + lo + 15, 768 + hi, 16), A.add)
             ts(r("PI", 8 + o, 8 + z), r("BD", 16 + o, 16 + z), 2047, A.bitwise_and)
             cp(lst(aL, f), r("PI", 8 + o, 8 + z))
         ts(live, r("BD", 16, 32), 2048.0 + s, A.is_lt, 8192.0, A.mult)
@@ -557,8 +574,9 @@ def build(g, T, topo, core):
     stage = [0]
 
     def minus_a(f, j):
-        p = slice(32 * j, 32 * j + 32)
-        return r("AT", 128 * f, 128 * f + 128, p=p), r("REP", p=p)
+        x, z = CUTS[f][j:j + 2]
+        p = slice(x - x % 32, x - x % 32 + 32)
+        return r("AT", 128 * f, 128 * f + 128, p=p), r("REP", 16 * (x % 32), 16 * (x % 32 + z - x), p=p)
 
     def hop(t, h, f):
         lo, hi = STREAMS[f]
@@ -585,7 +603,10 @@ def build(g, T, topo, core):
                 (raw, ID, r("NM", 0, n), False, False), (raw, blk("W16", 2), c("QA"), False, True)], acc=True)
         scan(r("SC", 768 + lo, 768 + hi), r("RESET", 0, n), raw, A.add, A.min)
         ts(lst(uL, f), r("SC", 768 + lo + 15, 768 + hi, 16), 2048.0 if h else col(14), A.add)
-        cp(c("C16"), ind(r("CT"), lst(uL, f)))
+        name("M U sU tU")
+        for x, z in ((lo, lo + C_CUT), (lo + C_CUT, hi)) if C_CUT else ((lo, hi),):
+            cp(r("C16", x, z), ind(r("CT"), r("L16", uL + x // 16, uL + z // 16)))
+        name("C C2")
         ts(c("CF"), c("C16"), -2048.0, A.add)
         tt(c("EQ"), c("CF"), ps(6, lo, hi), A.is_equal)
         key_end = lambda e: part(r3("PM", e), KW - 1, 152, KW)
@@ -597,7 +618,7 @@ def build(g, T, topo, core):
              (slot(2), idf, c_end(e - 1), False, True)] if end else []))
         mm([(key, r("IDb", 0, n), blk("MRH", h, 152), True, False), (key, c("EQ"), r("I65"), False, False)] +
            ([(ps(f, 136 + j, 288, KW, p=p), idf, key_end(e - 2 + j), False, False) for j in range(2)] if end else []))
-        name("M U sU tU C CF EQ ee key")
+        name("CF EQ ee key")
 
         def sums(src, j0, j1, bo, stop):
             x, z = CUTS[f][j0], CUTS[f][j1]
@@ -642,11 +663,8 @@ def build(g, T, topo, core):
         name("PM NE CS XH wr")
         if not end:
             ts(lst(hL, f), wr, 2048.0, A.add)
-            if GM_V:
-                cp(c("GM"), ind(r("ST"), lst(hL, f)))
-            else:
-                act(c("GM"), ind(r("ST"), lst(hL, f)), F.Copy)
-            r2w(f, 0, [(SELMP, c("GM"))], c("SC"))
+            act(c("GM"), ind(r("ST" if t else "MPP"), lst(hL, f)), F.Copy)
+            r2w(f, 0, [(SELMP if t else SELM, c("GM"))], c("SC"))
             ts(lst(mpL, f), r("SC", lo + 15, hi, 16), 2048.0, A.add)
             tt(c("Y"), ind(QW, lst(mpL, f)), c("A2"), A.add)
             name("tH GM N SEL sM tM Y")
@@ -659,7 +677,8 @@ def build(g, T, topo, core):
         x2 = lambda j: part(blk("X2", f), j, 128, 16)
         ts(d64, key_end(e), M64, A.add, M64, A.subtract)
         act(x2(15), key_end(e), bias=2.0 ** 24, scale=2.0 ** 19)
-        ts(x2(12), d64, M4096, A.add, M4096, A.subtract)
+        act(part(sm(352 + 8 * f, 8)), d64, bias=M4096)
+        act(x2(12), part(sm(352 + 8 * f, 8)), bias=-M4096)
         tt(x2(13), d64, x2(12), A.subtract)
         act(c("GSC"), ind(r("ST"), cl), F.Copy)
         if f < NS - 1:
@@ -670,8 +689,9 @@ def build(g, T, topo, core):
         mm([(raw, r("SELJ"), c("GSC"), False, True)], acc=True)
         tt(c("U2"), c("GB"), raw, A.max)
         scaled(r("GB", 256 + lo, 256 + hi), c("GB"), col(99))
-        act(c("GM"), c("U2"), bias=sm(288 + t, 1), scale=col(63))
-        cp(ind(r("K1"), lst(aS, f)), c("GM"))
+        keys = r("SGF", 1536 + lo, 1536 + hi)
+        act(keys, c("U2"), bias=sm(288 + t, 1), scale=col(63))
+        silu(r("K1"), lst(aS, f), keys)
         for j in range(2):
             a, z = max(lo, 128 * j), min(hi, 128 * j + 128)
             if a < z and n < 128:
@@ -711,17 +731,18 @@ def build(g, T, topo, core):
         out = [(ps(b, lo + j, lo + n, 2), m, src(1 - j), first, first) for m in ms for j in range(2)]
         return out[:-1] + [out[-1][:4] + (last,)]
 
-    def silu(win, to, more=0):
-        add("s", [lambda: g.scalar.activation(ind(win, to)[0], T.A2[:], F.Silu)], [r("A2"), to], [win], 65 + 3.8 * 256 + more)
+    def silu(win, to, a, more=0):
+        add("s", [lambda: g.scalar.activation(ind(win, to)[0], a[0], F.Silu)], [a, to], [win], 65 + 3.8 * a[5] + more)
 
     def put_out(out, b, n, sel, o):
         mms([(ps(b, 0, n), r(sel, 15 - j, 143 - j), blk("ST", j, n), j == 0, j == 15) for j in range(16)], 2)
         act(r("BLD", o, o + n), ps(b, 0, n), bias=2048.0)
         dma("y", out, T.BLD[:, o:o + n], [r("BLD", o, o + n)], [], 2500)
 
-    later = [None]
+    later = [start_rows]
+    bonus[0] = FIRST
     lanes(0)
-    bonus[0] = 0.0
+    bonus[0] = WRAP
     start_mates()
     for t in range(RO):
         last = t == RO - 1
@@ -730,19 +751,20 @@ def build(g, T, topo, core):
             act(r("QA", lo, hi), ind(QW, lst(aL, f)), F.Copy)
             act(r("GSA", lo, hi), ind(r("ST", 0, 2048), lst(aL, f)), F.Copy)
             mm([(ps(6, lo, hi), SELID, r("GSA", lo, hi), True, True)])
-            ax, at = ps(7, 256 + lo, 256 + hi), ps(2 + f, 128, 256)
+            p = slice(0, hi - lo)
+            ax, at = ps(7, 256 + lo, 256 + hi), ps(AT_BANK[f], 128, 256, p=p)
             mm([(at, r("QA", lo, hi), r("XP"), True, True)])
-            scaled(blk("AT", f), at, -1.0)
+            scaled(r("AT", 128 * f, 128 * f + 128, p=p), at, -1.0)
             for j, who in enumerate(A_REP[f]):
                 if who != "-":
-                    b = ps(A_BANK[f][j])
+                    x, z = 16 * (lo + CUTS[f][j]), 16 * (lo + CUTS[f][j + 1])
+                    b = ps(A_BANK[f][j], 0, z - x)
                     mm([(b,) + minus_a(f, j) + (True, True)])
-                    (cp if who == "v" else lambda o, a: scaled(o, a, 1.0))(blk("AREP", 4 * f + j, 512), b)
+                    (cp if who == "v" else lambda o, a: scaled(o, a, 1.0))(r("AREP", x, z), b)
             mm([(ax, r("XP"), r("QA", lo, hi), True, True)])
             act(r("A2", lo, hi), ax, bias=OFFA)
         bonus[0] = 0.0
-        if t:
-            later[0]()
+        later[0]()
         for h in range(HO):
             for f in range(NS):
                 bonus[0] = SKEW * (NS - 1 - f)
@@ -757,7 +779,7 @@ def build(g, T, topo, core):
                             x["after"] = max(i for i in range(n0) if ops[i].get("hop") == (0, LATE))
                 act(r("GA", 0, 256), ind(r("BITS"), lst(aL)), bias=col(82 + t))
                 scaled(r("GA", 256, 512), r("GA", 0, 256), col(99))
-        act(r("GK"), ind(r("K1"), lst(cL)), F.Copy)
+        act(r("GK"), ind(r("K1"), lst(cL)), bias=-64.0)
         mm([(ps(6, 256, 272), nIDf, sm(608), True, False)])
         mm([(ps(6, 256 + 8 * f, 264 + 8 * f), blk("GK", f), KS8, False, f == 1) for f in range(2)], acc=True)
         act(r("LS", 5, 96, 6), ps(6, 256, 272), F.Relu, scale=-2.0)
@@ -766,7 +788,7 @@ def build(g, T, topo, core):
         r2w(7, 0, [(SELLO, r("GK"))], r("SC", 0, 256))
         act(sm(336), r("SC", 15, 256, 16), bias=(t + 1) * 2.0 ** 20)
         tt(sm(496), sm(336), sm(80), A.min)
-        fill(r("SGF", 768, 1024), 0)
+        scaled(r("SGF", 768, 1024), r("RM"), 1.0 / 8192)
         mm([(ps(6, 272, 352), ID, r("T80"), True, False), (ps(6, 272, 320), M4K, ones(48), False, False)])
         pairs(0, 1, [("GB", 128, 256), ("GA", 128, 256)], PAIRS[2])
         pairs(1, 1, [("GB", 0, 256), ("GA", 128, 256)], PAIRS[3])
@@ -789,17 +811,18 @@ def build(g, T, topo, core):
         mm([(ps(7, 256, 512), r("XP"), r("QA"), True, False), (ps(7, 256, 512), r("nIDb"), r("QC"), False, True)])
         act(r("A2"), r("GSA"), bias=4096.0)
         bonus[0] = 4000.0
-        silu(r("SGF", 768, 1280), jL, 0 if t else 1300)
+        silu(r("SGF", 768, 1280), jL, r("SGF", 1280, 1536))
         bonus[0] = 0.0
         act(r("SGN"), ps(7), F.Sign)
         cp(ind(r("ST"), jO), r("YS"))
+        bonus[0] = URGE[0]
         cp(ind(r("ST"), jC), r("VV", 0, 256))
-        bonus[0] = 3000.0
+        bonus[0] = URGE[1]
         cp(ind(r("ST"), jA), r("VV", 256, 512))
-        bonus[0] = 5000.0
-        r2w(4, 0, [(r("BLKf"), r("SGF", 768, 1024))], r("SC", 0, 256))
+        bonus[0] = URGE[2]
+        scan(r("SC", 0, 256), r("RESET", 256, 512), r("SGF", 768, 1024), A.add, A.max)
         t1 = r("T16", 0, 16)
-        tt(r("RF"), r("SC", 15, 256, 16), ps(6, 336, 352), A.is_lt)
+        tt(r("RF"), r("SC", 15, 256, 16), ps(6, 336, 352), A.mult)
         tt(t1, r("RF"), sm(80), A.mult)
         mm([(ps(4, 256, 272), r("TRIB"), r("RF"), True, False), (ps(4, 257, 272), r("NTM"), r("RF", 0, 15), False, False),
             (ps(4, 256, 272), r("nIDb"), t1, False, False), (ps(4, 257, 272), ID, r("T16", 0, 15), False, True)])
@@ -814,12 +837,12 @@ def build(g, T, topo, core):
             tr.append(RemoteDMATransfer(dst_ids=[DstId(rid=rid, pnc=pid)], dma_engine_mask=mask, remote_sem=T.sem["arr%d" % t],
                                         src=T.SBQ[:, t, 32 * (d - 1):32 * d], dst=T.LAND[:, t, 32 * (d - 1):32 * d]))
         add("g", [lambda tr=tr: g.remote_dma_fused(tr, local_sem=T.sem.sent)], [r3("SBQ", t, 0, 96)], [r3("LAND", t)], 300.0,
-            sem="arr%d" % t, val=4 * (NR - 1), lat=2500.0, remote=True)
+            sem="arr%d" % t, val=4 * (NR - 1), lat=FAR, remote=True)
         bonus[0] = 0.0
         n = sm(303, 1)
         mm([(ps(5, 496, 512), r("BLKb"), r("RF"), True, True)])
         act(sm(272), ps(5, 496, 512), F.Copy, scale=-8192.0, accum=n)
-        silu(r("SGF", 0, 768), dL)
+        silu(r("SGF", 0, 768), dL, r("A2"))
         act(r("TMP", 128, 224), r("SGF", 0, 96), bias=M1 - 4096.0)
         act(r("SG", 0, 96), r("TMP", 128, 224), bias=-M1)
         bonus[0] = -3000.0
@@ -1009,8 +1032,18 @@ def polish(ops, order):
             seq.setdefault(eng[i], []).append(i)
         pool = [eng[i] for i in win]
 
-        def value():
-            h, pos, fr, left, top, tot = {}, {e: 0 for e in seq}, {e: free.get(e, 0.0) for e in seq}, len(win), 0.0, 0.0
+        def value(old, since, limit):
+            h, pos, fr, left, top, tot = {}, {}, {}, len(win), 0.0, 0.0
+            for e, s in seq.items():
+                k, f = 0, free.get(e, 0.0)
+                while k < len(s) and old[s[k]] < since:
+                    i = s[k]
+                    h[i] = t = old[i]
+                    f, k, t = t + cost[i], k + 1, t + out[i]
+                    tot += t
+                    if t > top:
+                        top = t
+                pos[e], fr[e], left = k, f, left - k
             while left:
                 was = left
                 for e, s in seq.items():
@@ -1033,21 +1066,22 @@ def polish(ops, order):
                             continue
                         break
                     pos[e], fr[e] = k, f
-                if left == was:
+                if left == was or top > limit:
                     return None, None
             return max([top] + [fr[e] + after.get(e, 0.0) for e in seq]) + 0.05 * tot / len(win), h
-        now, h = value()
-        best = (now, h)
+        now, times = value(head, -1.0, 1e30)
+        best = (now, times)
         for it in range(TRIES):
             s = seq[pool[int(draw() * len(pool))]]
-            i, k = int(draw() * len(s)), 1 + int(draw() ** 2 * 6)
+            i, k = int(draw() * len(s)), 1 + int(draw() ** 3 * REACH)
             j = i + k if draw() < 0.5 else i - k
             if not 0 <= j < len(s) or any(s[i] in ops[y]["deps"] for y in s[i + 1:j + 1]) or any(y in ops[s[i]]["deps"] for y in s[j:i]):
                 continue
+            since, limit = times[s[min(i, j)]], now - HEAT * (1.02 - it / TRIES) * math.log(draw() + 1e-9)
             s.insert(j, s.pop(i))
-            v, h = value()
-            if v is not None and (v <= now or draw() < math.exp((now - v) / (HEAT * (1.02 - it / TRIES)))):
-                now = v
+            v, h = value(times, since, limit / 1.04)
+            if v is not None and v <= limit:
+                now, times = v, h
                 if v < best[0]:
                     best = (v, h)
             else:

import math
from concourse.bass import DstId, RemoteDMATransfer
from concourse.mybir import AluOpType as A, AxisListType as AX, ActivationFunctionType as F

RO, HO, STEP, NR = 5, 3, 341, 4
WD = 4352
STREAMS = ((0, 128), (128, 256))
CUTS = ((0, 32, 64, 96, 128),) * 2
STEPS = "g0 s2 g3 s1 a0 r1 a2 a3"
LAST_STEPS = STEPS
STAGE = (4, 5, 7)
GM_V = False
C_CUT = 32
EARLY, TABLE, FIRST, WRAP, MATES, MP_V = 5000.0, 12000.0, 5000.0, 0.0, 2000.0, 2
LATE = "PM"
TEMPLATE = {"v": "sM'' tM'' Y'' r1' sU tU C PM' C2 NE' CF CS' EQ XH' s1a tH' s2a s2b s1b", "s": "a2' g0 g3 GM' a0 a3"}
PAIRS = ([("s", (3,), (0, 1, 2, 3, 4, 5)), ("v", (2, 0), (6, 7))], [("v", (2, 0), (0, 1, 2, 3, 4, 5, 6, 7))],
         [("s", (3, 1, 5), (0, 1)), ("v", (2, 0, 4), (2, 3, 4, 5, 6, 7))],
         [("s", (3, 1, 5), (0, 2, 4, 6)), ("v", (2, 0, 4), (1, 3, 5, 7))])
PARTS = ((0, 4),)
S_IND = (3, 4)
A_REP = ("-vv-", "-ss-")
A_BANK = ((0, 5, 2, 0), (0, 2, 3, 0))
AT_BANK = (2, 3)
V_CUT = 256
LOOK, SKEW, SAME, CROSS, PE = 350.0, 800.0, 110.0, 195.0, 0.5
FAR, REACH = 3500.0, 8
URGE = (6000.0, 3000.0, 5000.0)
WINDOW, TRIES, SWEEPS, HEAT = 100, 6000, 4, 70.0
TAG = float(1 << 21)
BETA = 1024.0
M64 = 1.5 * 2.0 ** 29
M4096 = 1.5 * 2.0 ** 35
M1 = 1.5 * 2.0 ** 23
Q0 = 128
KW = 19

SCRATCH = {}


def _decl(dt_, spec):
    for item in spec.split():
        name, n = item.split(":")
        SCRATCH[name] = ("sbuf", [128] + [int(x) for x in n.split("x")], dt_)


_decl("bfloat16", "Q:4480 ST:4352 BITS:4096 XG:4096 AB:4096 AREP:4096 MT:4096 MPP:4096 AV:2048 SBQ:5x768 "
      "LAND:5x96 SG:96 BH:1024 IDb:128 nIDb:128 BLKb:128 XP:128 I65:152 DIFF:152 MRH:456 RS:152 RESET:512 "
      "NRM:256 RM:256 RMH:128 NM:128 MC:512 ONES:512 Q8:24 BO:16 B2:144 B0:144 B10:144 B23:144 B45:144 TRI:128 TRIx:128 "
      "TRIB:128 NTM:128 SEL:640 SELJ:128 DG:640 DM:128 KEEP:128 SHIFT:128 PO:256 MSW:640 ROT:1536 "
      "UP:384 STP:456 X3:384 QA:256 QC:256 GSA:256 GSC:256 GM:256 EQ:256 GA:512 MR:256 MG:128 DJ:128 "
      "GB:512 U2:256 GK:256 SGN:512 JUNK:1024 YS:256 VV:512 FW:128 CTX:128 IND:16x128 JB3:16x16 IND2:256 XS:256 "
      "RF:16 RR:288 QM:192 SW:288 GMM:192 KR:192 C16B:32 AT:384 REP:512")
_decl("float16", "RW:4096 W16:512 Y:256 CF:256 XH:384 KM:128 H16:768 T16:32 T80:80")
_decl("float32", "CT:4112 JF:256 COL:128 IDf:256 BLKf:128 CN:128 Q8f:8 TMP:512 BLD:768 A2:256 PM:9x152 "
      "CS:9x152 X2:384 SC:1024 SM:832 LS:96 LW2:96 LO:96 PFW:136 SGF:1792 K1:4352")
_decl("int32", "IB:400 SI:512 BD:32 PI:32")
_decl("uint16", "C16:256 L16:192 P16:384")
for _b in range(8):
    SCRATCH["ps%d" % _b] = ("psum", [128, 512], "float32")
NDMA = 46
SEMAPHORES = ["ev", "es", "et", "eg", "sent"] + ["arr%d" % t for t in range(RO)] + ["d%d" % i for i in range(NDMA)]


def build(g, T, topo, core):
    ops = []
    rank = T.rank_of(core)
    bonus = [0.0]

    def r(name, lo=0, hi=None, step=1, row=None, p=None):
        if hi is None:
            hi = T[name].shape[1]
        ps_ = slice(None) if p is None else p
        if row is not None:
            ps_ = slice(row, 128, 16)
        return (T[name][ps_, lo:hi:step], name, lo, hi, row, (hi - lo + step - 1) // step)

    def r3(name, i, lo=0, hi=None, step=1):
        w = T[name].shape[2]
        if hi is None:
            hi = w
        return (T[name][:, i, lo:hi:step], name, i * w + lo, i * w + hi, None, (hi - lo + step - 1) // step)

    def r3s(name, i0, i1, lo, hi):
        w = T[name].shape[2]
        return (T[name][:, i0:i1, lo:hi], name, i0 * w, i1 * w, None, (i1 - i0) * (hi - lo))

    def blk(name, j, n=128):
        return r(name, n * j, n * j + n)

    def ind(win, off):
        return (win[0].indirect(off[0]), win, off, 16 * off[5])

    def isind(x):
        return len(x) == 4

    def regs(*xs):
        out = []
        for x in xs:
            if isinstance(x, tuple):
                out += [x[1], x[2]] if isind(x) else [x]
        return out

    def ap(x):
        return x[0] if isinstance(x, tuple) else x

    def two(x):
        return not isind(x) and x[1][:2] != "ps" and SCRATCH[x[1]][2] in ("bfloat16", "uint16", "float16")

    def add(eng, fns, reads, writes, cost, **kw):
        o = dict(eng=eng, fns=fns, reads=reads, writes=writes, cost=cost, acc=False, sem=None, lat=0.0, bonus=bonus[0])
        o.update(kw)
        ops.append(o)

    def vop(fn, out, ins, f):
        rd, wr = regs(*ins), [out]
        if isind(out):
            rd, wr = rd + [out[2]], [out[1]]
            c = 50 + 3.8 * out[3]
        elif isind(ins[0]):
            c = 50 + 1.56 * out[5]
        else:
            c = 20 + max(64, f * out[5])
        add("v", [fn], rd, wr, c)

    def cp(out, a):
        vop(lambda: g.vector.tensor_copy(out[0], a[0]), out, [a], 0.5 if two(out) and two(a) else 1)

    def tt(out, a, b, op):
        f = 1 if isind(a) or a[1][:2] == "ps" or b[1][:2] == "ps" else 2
        vop(lambda: g.vector.tensor_tensor(out[0], a[0], b[0], op), out, [a, b], f)

    def ts(out, a, s1, op0, s2=None, op1=None):
        f = 0.5 if two(out) and two(a) else 1
        if op1 is None:
            vop(lambda: g.vector.tensor_scalar(out[0], a[0], ap(s1), None, op0), out, [a, s1], f)
        else:
            vop(lambda: g.vector.tensor_scalar(out[0], a[0], ap(s1), ap(s2), op0, op1), out, [a, s1, s2], f)

    def scan(out, d0, d1, op0, op1, init=0.0):
        vop(lambda: g.vector.tensor_tensor_scan(out[0], d0[0], d1[0], ap(init), op0, op1), out, [d0, d1, init], 1)

    def red(out, a, op):
        add("v", [lambda: g.vector.tensor_reduce(out[0], a[0], AX.X, op)], [a], [out], 20 + max(64, a[5]))

    def mset(out, v):
        add("v", [lambda: g.vector.memset(out[0], v)], [], [out], 20 + max(64, out[5] * (0.5 if two(out) else 1)))

    def act(out, a, fn=F.Identity, bias=None, scale=None, accum=None):
        kw = {}
        if bias is not None:
            kw["bias"] = ap(bias)
        if scale is not None:
            kw["scale"] = ap(scale)
        if accum is not None:
            kw["accum_out"] = accum[0]
        c = 65 + 1.56 * out[5] if isind(a) else 40 + max(64, out[5])
        add("s", [lambda: g.scalar.activation(out[0], a[0], fn, **kw)], regs(a, bias, scale),
            [out] + ([accum] if accum else []), c + (20 if accum else 0))

    def mm(items, acc=False):
        fns, rd, wr, c = [], [], [], 20.0
        for (o, l, rr, st, sp) in items:
            fns.append(lambda o=o, l=l, rr=rr, st=st, sp=sp: g.tensor.matmul(o[0], l[0], rr[0], st, sp))
            rd += [l, rr]
            wr.append(o)
            c += 10 + PE * max(min(64, l[5]), rr[5]) * (1 if two(l) else 4)
        add("t", fns, rd, wr, c, acc=acc)

    def mms(items, n=4):
        for j in range(0, len(items), n):
            mm(items[j:j + n], acc=j > 0 or not items[0][3])

    def iota(out, pat, base=0, cm=0):
        if SCRATCH[out[1]][2] == "int32":
            fn = lambda: g.iota(out[0], pat, base, cm)
        else:
            fn = lambda: g.iota(out[0], pat, base, cm, allow_small_or_imprecise_dtypes=True)
        add("g", [fn], [], [out], 130 + 2 * out[5])

    def fill(out, v):
        iota(out, [[0, out[5]]], v)

    def select(out, a, k, op=A.is_equal, other=0.0, sign=1):
        add("g", [lambda: g.affine_select(out[0], a[0], [[sign, out[5]]], op, other, -sign * k, -sign)], [a], [out], 170 + 2 * out[5])

    nd = [0]

    def dma(q, out, a, rd, wr, lat, slow=False):
        sem = "d%d" % nd[0]
        nd[0] += 1
        if slow:
            fn = lambda: g.dma_start(out, a, allow_slow_non_contiguous=True)
        else:
            fn = lambda: {"g": g, "y": g.sync, "s": g.scalar}[q].dma_start(out, a)
        add(q, [fn], rd, wr, 100.0, sem=sem, val=16, lat=lat)

    def rows(out, a, q="y"):
        dma(q, out[0], a[0], [a], [out], 2500)

    def ps(b, lo=0, hi=512, step=1, p=None):
        return r("ps%d" % b, lo, hi, step, p=p)

    def col(i, n=1):
        return r("COL", i, i + n)

    def sm(lo, n=16, step=1):
        return r("SM", lo, lo + n * step, step)

    def oh(f):
        return col(16 + f)

    def scaled(out, a, s):
        act(out, a, F.Copy, scale=s)

    one = slice(0, 1)
    Mp, Mn, ZERO, M4K = (r("MC", 128 * j, 128 * j + 128, p=one) for j in range(4))

    def ones(n):
        return r("ONES", 0, n, p=one)

    bonus[0] = 20000.0
    dma("y", T.IB[:, 0:256], T.pr[:], [], [r("IB", 0, 256)], 2000)
    dma("s", T.IB[:, 384:385], T.w[:], [], [r("IB", 384, 388)], 2000)
    dma("y", T.IB[:, 256:384], T.mt[:], [], [r("IB", 256, 384)], 2000)
    dma("s", T.IB[:, 388:389], T.kk[:], [], [r("IB", 388, 392)], 2000)
    mset(r("IB", 392, 396), 0)
    dma("s", T.IB[8:128:16, 392:393], T.th[:], [], [r("IB", 392, 396)], 2000)
    QW = r("Q", Q0)
    for j, q in enumerate("sy"):
        x = r("Q", Q0 + 2048 * j, Q0 + 2048 * j + 2048)
        dma(q, x[0], T.rec[:, 2048 * j:2048 * j + 2048], [], [x], 4500)
    NS = len(STREAMS)
    bonus[0] = 30000.0
    iota(r("PI", 0, 1), [[0, 1]], 0, 1)
    iota(r("JF"), [[1, 256]])
    iota(r("MG"), [[1, 8], [0, 16]])
    iota(r("MR"), [[0, 16], [1, 16]])
    iota(r("DJ"), [[1, 128]], 0, -1)
    iota(r("AV"), [[8, 16], [0, 8], [128, 16]], -2048)
    rows(r("AV", row=5), r("MG"))
    bonus[0] = EARLY
    iota(r3s("JB3", 0, 16, 0, 16), [[1, 256]])
    PF, PR, PG = col(0), col(1), col(2)
    DJ, ID = r("DJ"), r("IDb")
    for row in (6, 7, 11, 12, 13, 14, 15):
        dma("y", T.ST[row:128:16, 0:4096], T.rec[0:8, :], [], [r("ST", 0, 4096, row=row)], 2500)
    for row in (4, 5):
        dma("y", T.ST[row:128:16, 2048:4096], T.rec[0:8, 0:2048], [], [r("ST", 2048, 4096, row=row)], 2500)
    mset(r("ST", 4096), 0.0)
    dma("y", T.MT[:, 0:2048], T.rec[:, 0:2048], [], [r("MT", 0, 2048)], 4500)
    ts(r("PI", 1, 2), r("PI", 0, 1), 15, A.bitwise_and)
    ts(r("PI", 2, 3), r("PI", 0, 1), 4, A.logical_shift_right)
    ts(r("PI", 3, 4), r("PI", 0, 1), 7, A.bitwise_and)
    cp(col(0, 4), r("PI", 0, 4))
    ts(col(16, 16), r("JF", 0, 16), PR, A.is_equal)
    mset(r("ONES"), 1.0)
    for j, v in enumerate((M4096, -M4096, 0.0, 4096.0)):
        mset(r("MC", 128 * j, 128 * j + 128, p=one), v)
    ids, xs = r("BLD", 0, 256), r("BLD", 256, 640)
    scaled(col(4), PR, 256.0)
    act(ids, r("JF"), bias=col(4))
    lob = r("XS")
    bonus[0] = FIRST
    tt(lob, r("IB", 0, 256), ids, A.is_equal)
    rows(r("MPP", p=slice(0, 8)), lob)
    bonus[0] = EARLY
    ts(ID, DJ, 0.0, A.is_equal)
    scaled(blk("IDf", 0), ID, 1.0)
    scaled(blk("IDf", 1), ID, -1.0)
    scaled(r("nIDb"), ID, -1.0)
    IDf, nIDf = blk("IDf", 0), blk("IDf", 1)
    ts(r("BLKb"), r("MG", 0, 128), PG, A.is_equal)
    scaled(r("BLKf"), r("BLKb"), 1.0)
    Q8, Q8n, KS8 = r("Q8", 0, 8), r("Q8", 8, 16), r("Q8", 16, 24)
    ts(r("Q8f"), r("JF", 0, 8), PG, A.is_equal)
    scaled(Q8, r("Q8f"), 1.0)
    scaled(Q8n, r("Q8f"), -8192.0)
    ts(col(8), PR, 8.0, A.is_ge)
    act(col(9), col(8), bias=8.0, scale=-16.0)
    ts(r("XP"), DJ, col(9), A.is_equal)
    OFF, OFFA = col(13), col(15)
    act(OFF, col(8), bias=2048.0, scale=-4608.0)
    act(OFFA, col(8), bias=2047.5, scale=-4608.0)
    bonus[0] = EARLY + TABLE
    cp(col(5, 3), r("IB", 384, 396, 4))
    ts(r("TMP", 0, 1), col(5), 0.5, A.mult, OFF, A.mult)
    scaled(r("TMP", 1, 2), col(7), 1.0)
    mm([(ps(7, 0, 2), r("BLKf"), r("TMP", 0, 2), True, True)])
    cp(r("T16", 0, 1), col(5))
    mm([(ps(3, 0, 1), r("XP"), r("T16", 0, 1), True, True)])
    act(col(32), ps(7, 0, 1), bias=-2048.0, scale=-1.0)
    act(col(14), ps(7, 0, 1), bias=2048.0)
    scaled(r("C16B", 16, 17), ps(7, 1, 2), 1.0)
    scaled(col(33), r("C16B", 16, 17), 1.0)
    tt(col(34), ps(7, 1, 2), col(33), A.subtract)
    scaled(col(38), ps(3, 0, 1), 1.0)
    act(col(11), r("TMP", 0, 1), scale=-1.0)
    scaled(r("CN"), r("ONES", 0, 128), col(11))
    for j, (x, v) in enumerate(((5, 0.5), (5, -0.5), (38, 1.0), (38, -1.0))):
        ts(blk("W16", j), r("BLKb"), col(x), A.mult, v, A.mult)
    ts(r("SI", 0, 256), ids, col(32), A.add)
    ts(r("SI", 256, 512), r("SI", 0, 256), 4095, A.bitwise_and)
    cp(r("TMP", 256, 512), r("SI", 256, 512))
    ts(r("H16", 0, 256), r("SI", 256, 512), -2048.0, A.add)
    act(r("SC", 0, 256), r("TMP", 256, 512), F.Square)
    ts(r("SI", 0, 256), r("SC", 0, 256), -12.0, A.add, 1.0 / 32, A.mult)
    ts(r("SI", 256, 512), r("SI", 0, 256), 4095, A.bitwise_and)
    ts(r("H16", 256, 512), r("SI", 256, 512), -2048.0, A.add)
    ts(r("H16", 512, 768), r("ONES", 0, 256), 0.5, A.mult)
    for j in (2, 0, 1):
        dma("y", T.RW[8 * j:8 * j + 8, :], T.H16[:, 256 * j:256 * j + 256], [blk("H16", j, 256)], [(None, "RW", 0, 4096, j, 4096)], 2500)
    ts(r("T16", 24, 32), r("JF", 0, 8), 0.0, A.is_equal)
    ts(r("T16", 8, 16), r("Q8f"), col(6), A.mult)
    cp(r("T16", 16, 24), r("Q8f"))
    ts(r("PI", 4, 5), r("IB", 388, 389), 1, A.bitwise_and)
    ts(r("T16", 25, 26), r("PI", 4, 5), 4096.0, A.mult)
    k24 = slice(0, 24)
    mm([(ps(6, 0, 128, p=k24), r("T16", 8, 32), ID, True, True)])
    cp(r("KM", p=k24), ps(6, 0, 128, p=k24))
    ts(r("Y", 0, 128, p=k24), ps(6, 0, 128, p=k24), -1.0, A.mult)
    for j in range(8):
        b, x = ps((4, 5, 7)[j % 3]), r("RW", 512 * j, 512 * j + 512, p=k24)
        mms([(b, Mp, ones(512), True, False), (b, r("Y", 0, 128, p=k24), x, False, False),
             (b, Mn, ones(512), False, False), (b, r("KM", p=k24), x, False, True)], 1)
        act(blk("CT", j, 512), b, bias=2047.5)
    scaled(r("CT", 4096, 4097), r("CT", 0, 1), 1.0)
    bonus[0] = EARLY
    ts(xs, r("IB", 0, 384), -2048.0, A.add)
    hi_, lo_ = r("JUNK", 0, 384), r("JUNK", 384, 768)
    scaled(hi_, xs, 1.0)
    tt(lo_, xs, hi_, A.subtract)
    iota(r("GA", 0, 256), [[64, 4], [0, 64]], -2048)
    act(blk("BH", 0, 256), r("GA", 0, 256), bias=col(4))
    iota(blk("BH", 1, 256), [[0, 4], [1, 64]])
    scaled(blk("BH", 2, 256), r("ONES", 0, 256), col(33))
    scaled(blk("BH", 3, 256), r("ONES", 0, 256), col(34))
    for j, row in enumerate((0, 1, 8, 9)):
        rows(r("ST", 0, 4096, row=row), blk("BH", j, 256))
    rows(r("ST", 0, 4096, row=10), lob)
    for j, x in enumerate((hi_, lo_)):
        o = x[2]
        dma("y", T.AB[8 * j:8 * j + 8, :], T.JUNK[:, o:o + 256], [x], [(None, "AB", 0, 4096, j, 4096)], 2500)
        rows(r("ST", 0, 4096, row=2 + j), r("JUNK", o, o + 256))
        rows(r("ST", 0, 2048, row=4 + j), r("JUNK", o + 256, o + 384))
        rows(r("MT", 0, 2048, row=4 + j), r("JUNK", o + 256, o + 384))
    act(col(50), col(3), bias=15.0, scale=16.0)
    ts(r("B0"), r("JF", 0, 144), col(50), A.is_equal)
    act(col(51), PG, bias=15.0, scale=16.0)
    ts(r("B2"), r("JF", 0, 144), col(51), A.is_equal)
    select(r("TRI"), r("ONES", 0, 128), 0, A.is_ge)
    select(r("TRIx"), r("ONES", 0, 128), 0, A.is_gt)
    select(r("TRIB"), r("BLKb"), 0, A.is_ge)
    fill(r("Q", Q0 + 4096), 0)
    LW = sm(0)
    ts(LW, r("JF", 0, 256, 16), PR, A.add, 4096.0, A.add)
    act(col(52), PG, bias=2.0, scale=KW - 16.0)
    act(col(53), PF, bias=col(52))
    ts(r("I65"), r("JF", 0, 152), col(53), A.is_equal, 262144.0, A.mult)
    fill(r("EQ", 0, 1), 0)
    scaled(r("EQ", 1, 153), r("I65"), 1.0 / 262144)
    tt(r("DIFF"), r("EQ", 0, 152), r("EQ", 1, 153), A.subtract)
    for j, v in enumerate((64.0, -64.0)):
        scaled(blk("BO", j, 8), r("Q8f"), v)
    for h in range(HO):
        iota(blk("MRH", h, 152), [[0, 8], [1, KW]], 16 * h - 26)
    fill(r("MRH", KW - 1, 456, KW), int(TAG))
    for j in range(2):
        fill(r("MRH", j, 304, KW), int(TAG))
        fill(r("MRH", 304 + j, 456, KW), 0)
    fill(r("RS"), 0)
    fill(r("RS", 0, 152, KW), 1 << 23)
    act(r("RESET", 0, 256), r("MR"), F.Silu, bias=2.0 ** 31, scale=-2.0 ** 31)
    ops[-1]["cost"] += 1300
    ts(r("RM"), r("MR"), PR, A.is_equal)
    act(r("RMH"), r("RM", 0, 128), bias=0.5, scale=0.5)
    act(r("NRM"), r("RM"), bias=2.0 ** 25, scale=-2.0 ** 25)
    act(r("NM"), r("RM", 0, 128), bias=2.0 ** 30 - M4096, scale=-2.0 ** 30)
    tt(col(56, 5), r("COL", 16, 26, 2), r("COL", 17, 26, 2), A.add)
    for j in range(4):
        scaled(blk("SEL", j), r("BLKb"), col(56 + j))
    SELID, SELP, SELM, SELMP, SELLO = [blk("SEL", j) for j in range(5)]
    iota(r("SGN"), [[1, 32], [0, 16]])
    ts(r("PI", 7, 8), r("PI", 0, 1), 31, A.bitwise_and)
    cp(col(62), r("PI", 7, 8))
    ts(r("REP"), r("SGN"), col(62), A.is_equal)
    fill(r("PFW", 128, 136), 4096)
    for f in range(NS):
        ts(col(104 + f), PG, 8.0 - S_IND[f], A.is_ge, 128.0, A.mult)
        act(col(108 + f), col(104 + f), bias=1.0, scale=-1.0 / 256)
        act(col(112 + f), col(108 + f), scale=16.0)
        act(col(120 + f), PF, bias=(STREAMS[f][0] + 1.0) * 2.0 ** 40, scale=2.0 ** 40)
    fill(r("X3"), 0)
    fill(r("X3", 13, 128 * NS, 16), 2048)
    L3, LBC = r("L16", 16, 24), r("L16", 8, 16)
    cp(LBC, r("JF", KW - 1, 152, KW))
    aL, cL, mpL, hL, bL, dL, kL, uL, aS = 32, 48, 64, 80, 96, r("L16", 112, 128), 128, 176, 160

    def lst(base, f=None):
        lo, hi = (0, 256) if f is None else STREAMS[f]
        return r("L16", base + lo // 16, base + hi // 16)

    def start_mates():
        k16 = slice(0, 16)
        mms([(ps(6, 256, 512), r("B0", 15 - j, 143 - j, p=k16), r("AB", j, 4096, 16, p=k16), j == 0, j == 15) for j in range(16)], 2)
        ts(r("P16", 0, 256), ps(6, 256, 512), 2048.0, A.add)
        ts(r("P16", 256, 384), r("IB", 256, 384), -2048.0, A.add)
        bonus[0] = MATES
        for j in range(8):
            cp(ind(r("MT", 2048, 4096), r("P16", 256 + 16 * j, 272 + 16 * j)), blk("AV", j, 256))
        bonus[0] = 0.0
        for j in range(16):
            if j % MP_V == 1:
                cp(blk("MPP", j, 256), ind(r("MT"), blk("P16", j, 16)))
            else:
                act(blk("MPP", j, 256), ind(r("MT"), blk("P16", j, 16)), F.Copy)

    def start_rows():
        for j in range(2):
            rows(r("ST", 0, 4096, row=6 + j), r("MPP", 0, 4096, row=4 + j))
            rows(r("ST", 2048, 4096, row=4 + j), r("MT", 2048, 4096, row=4 + j))

    def late_constants():
        fill(r("K1", 0, 2176), 8192)
        dma("y", T.K1[:, 2176:WD], T.K1[:, 0:2176], [r("K1", 0, 2176)], [r("K1", 2176, WD)], 4000)
        cp(L3, r("JF", 5, 48, 6))
        act(col(61), oh(0), bias=oh(14), scale=2.0 ** 20)
        scaled(SELLO, r("BLKb"), col(61))
        ts(col(63), PR, 12.0, A.is_ge)
        scaled(sm(296, RO), r("JF", 1, RO + 1), oh(0))
        act(sm(288, RO), sm(296, RO), bias=64.0, scale=-1.0)
        scaled(r("B10"), r("B2"), oh(10))
        scaled(r("B23"), r("B2"), col(57))
        scaled(r("B45"), r("B2"), col(58))
        select(r("NTM"), r("BLKb"), 0, A.is_gt, sign=-1)
        iota(r3s("SBQ", 0, RO, 0, 96), [[0, RO * 96]], -1)
        fill(r("SGF", 0, 96), 4096)
        fill(r("SGF", 1280, 1536), 0)
        scaled(r("RESET", 256, 512), r("RESET", 0, 256), -1.0)
        act(col(64, 12), col(16, 12), bias=1.0, scale=-2.0)
        act(col(76), oh(12), bias=oh(13))
        act(col(77), col(76), bias=oh(14), scale=4.0)
        ts(col(78), PR, 12.0, A.is_lt, BETA, A.mult)
        act(r("BITS", 0, 1), col(77), bias=col(78), scale=-1.0)
        for k in range(12):
            for x in range(0, 1 << k, 512):
                ts(r("BITS", (1 << k) + x, (1 << k) + min(1 << k, x + 512)), r("BITS", x, min(1 << k, x + 512)), col(64 + k), A.mult)
        act(col(80), oh(15), bias=col(77), scale=TAG)
        scaled(KS8, r("Q8f"), col(80))
        ts(r("PI", 5, 7), r("PI", 1, 3), 1, A.bitwise_and)
        cp(col(98, 2), r("PI", 5, 7))
        act(col(79), oh(15), scale=-1.0)
        scaled(col(82, RO), r("JF", 1, RO + 1), col(79))
        fill(r("SELJ"), 0)
        act(col(87), col(60), scale=-2.0 ** 25)
        scaled(r("SELJ", 15, 128, 16), r("Q8f"), col(87))
        for j, k in enumerate((-4, 2, -2, 4, 6)):
            select(blk("DG", j), r("ONES", 0, 128), k)
        act(col(81), col(76), scale=1.0 / 64)
        scaled(r("DM"), blk("DG", 0), col(81))
        act(col(88), col(56), bias=col(58))
        act(col(89), col(57), bias=col(59))
        scaled(r("KEEP"), ID, col(88))
        scaled(r("SHIFT"), blk("DG", 1), col(88))
        scaled(blk("PO", 0), ID, col(89))
        scaled(blk("PO", 1), blk("DG", 2), col(89))
        scaled(blk("MSW", 0), blk("DG", 3), col(56))
        scaled(blk("MSW", 1), blk("DG", 4), col(56))
        scaled(blk("MSW", 2), ID, col(58))
        scaled(blk("MSW", 3), blk("DG", 1), col(58))
        act(col(35), oh(8), bias=oh(10), scale=col(33))
        act(col(90), oh(9), bias=col(35), scale=col(34))
        act(col(91), col(58), bias=1.0, scale=-1.0)
        act(col(92), col(59), bias=1.0, scale=-1.0)
        act(col(93), col(59), bias=col(91), scale=-1.0)
        act(col(100), oh(9), scale=-32.0)
        scaled(blk("MSW", 4), ID, col(93))
        for d in range(1, NR):
            select(blk("ROT", 2 + d), r("ONES", 0, 128), 16 * d)
            select(blk("ROT", d - 1), blk("ROT", 2 + d), 16 * d - 128, A.not_equal, 1.0)
        scaled(blk("ROT", 1, 384), blk("ROT", 0, 384), -256.0)
        scaled(blk("ROT", 2, 384), blk("ROT", 0, 384), col(8))
        scaled(blk("ROT", 3, 384), blk("ROT", 2, 384), -1.0)
        scaled(blk("UP", 0), ID, col(8))
        scaled(blk("UP", 1), blk("UP", 0), -1.0)
        act(col(101), col(8), bias=1.0, scale=-1.0)
        scaled(blk("UP", 2), ID, col(101))
        fill(r("X2"), -(1 << 20))
        for f in range(NS):
            iota(r("X2", 128 * f + 14, 128 * f + 128, 16), [[0, 8]], STREAMS[f][0], 1)
        for t in range(RO):
            iota(sm(96 + t, 2, 8), [[128, 2]], 8193 - int(12 * BETA * BETA) - (t + 1) ** 2, 1)
            iota(sm(256 + t, 2, 8), [[128, 2]], 8192 - (t + 1) * int(TAG), 1)
        fill(r("LS"), 0)
        mset(r("LS", 0, 96, 6), -2.0 ** 40)
        mset(r("LW2"), -2.0 ** 40)
        fill(r("LW2", 2, 96, 6), 0)
        act(sm(80), LW, bias=-3840.0)
        iota(sm(688, 48), [[0, 3], [16, 16]])
        ts(r("T80", 0, 48), sm(688, 48), PR, A.add)
        cp(r("T80", 48, 64), sm(80))
        act(col(94), PR, bias=239.0)
        fill(r("C16B", 0, 16), 16)
        act(sm(112, 6), sm(688, 6), bias=PR)
        act(col(95), col(98), bias=PR, scale=-1.0)
        act(col(95), col(95), bias=1.0)
        for j in (1, 2):
            act(sm(112 + 6 * j, 6), sm(688, 6), bias=col(95))
        act(sm(112, 18), sm(112, 18), bias=4096.0, scale=8192.0)
        for j in range(3):
            act(sm(130 + 6 * j, 6), sm(0, 6), bias=-2048.0)
        iota(r("KR", 0, 96), [[16384, 48], [0, 2]], 8192)

    def r2w(b, lo, items, out):
        o = lo
        for sel, src in items:
            n = src[5]
            mm([(ps(b, o, o + n), ID, r("NRM", 0, n), True, False)])
            mm([(ps(b, o, o + n), sel, src, False, True)], acc=True)
            o += n
        scan(out, r("RESET", 0, o - lo), ps(b, lo, o), A.add, A.min)

    live, ends = r("T80", 64, 80), sm(448, 64)

    def lanes(t):
        s = (STEP * t) & 2047
        if t == 0:
            k8 = slice(0, 8)
            mms([(ps(0, 0, 128), r("B0", 15 - j, 143 - j, p=k8), r("MPP", j, 2048, 16, p=k8), j == 0, j == 15) for j in range(16)])
        else:
            mm([(ps(0, 0, 128), ZERO, ones(128), True, False)])
            items = []
            for j in range(16):
                nb = (2048 - s - j + 15) // 16
                x = s + j + 16 * nb - 2048
                sel = r("B10", 15 - j, 143 - j)
                items += [(ps(0, 0, nb), sel, r("ST", s + j, 2048, 16), False, False),
                          (ps(0, nb, 128), sel, r("ST", x, x + 16 * (128 - nb), 16), False, j == 15)]
            mms(items)
        scaled(r("FW"), ps(0, 0, 128), 1.0)
        mm([(ps(1, 0, 128), r("FW"), r("BLKb"), True, True)])
        scaled(r("CTX"), ps(1, 0, 128), 1.0)
        mm([(ps(1, 128, 136), r("TRI"), r("CTX", 0, 128, 16), True, True),
            (ps(1, 136, 144), r("ONES", 0, 128), r("CTX", 0, 128, 16), True, True)])
        mm([(ps(0, 128, 256), r("TRIB"), r("FW"), True, False), (ps(0, 128, 256), r("CTX"), r("TRIx"), False, True)])
        act(sm(192, 8), ps(1, 128, 136), bias=0.5, scale=-1.0)
        for f in range(NS):
            act(r("X3", 128 * f + 15, 128 * f + 128, 16), ps(1, 136, 144), F.Relu, bias=col(120 + f), scale=-2.0 ** 40)
        scaled(r("PFW", 0, 128), ps(0, 128, 256), 1.0)
        for f, (lo, hi) in enumerate(STREAMS):
            o, z, b = lo // 16, hi // 16, 2 + f % 2
            part = lambda a, k, n: (a, "IND", 8 * f + k, 8 * f + k + n, None, hi - lo)
            act(col(116 + f), col(104 + f), bias=float(s), scale=8.0)
            mm([(ps(b, 32, 40), r("TRI"), r("CTX", 0, 128, 16), True, True)])
            for k in range(8):
                x = part(T.IND[:, o:z, 16 * k:16 * k + 16], k, 1)
                if k < 8 - S_IND[f]:
                    ts(x, r3s("JB3", o, z, 0, 16), ps(b, 32 + k, 33 + k), A.is_ge)
                else:
                    act(x, r3s("JB3", o, z, 0, 16), F.Sign, bias=sm(192 + k, 1))
            mm([(ps(b, q, q + 1), part(T.IND[:, q, :], 0, 8), r("ONES", 0, 1), True, True) for q in range(o, z)])
            ts(lst(bL, f), ps(b, o, z), col(104 + f), A.add, col(108 + f), A.mult)
            act(sm(224 + o, z - o), ps(b, o, z), bias=col(116 + f), scale=col(112 + f))
            tt(r("IND2", lo, hi), ind(r("PFW"), lst(bL, f)), r("JF", lo, hi), A.is_le)
            r2w(0, 256, [(r("BLKb"), r("IND2", lo, hi))], r("SC", 768 + lo, 768 + hi))
            tt(r("BD", 16 + o, 16 + z), sm(224 + o, z - o), r("SC", 768 + lo + 15, 768 + hi, 16), A.add)
            ts(r("PI", 8 + o, 8 + z), r("BD", 16 + o, 16 + z), 2047, A.bitwise_and)
            cp(lst(aL, f), r("PI", 8 + o, 8 + z))
        ts(live, r("BD", 16, 32), 2048.0 + s, A.is_lt, 8192.0, A.mult)
        tt(sm(240), LW, live, A.subtract)
        tt(sm(448), r("PI", 8, 24), sm(240), A.max)
        cp(lst(aS), sm(448))

    stage = [0]

    def minus_a(f, j):
        x, z = CUTS[f][j:j + 2]
        p = slice(x - x % 32, x - x % 32 + 32)
        return r("AT", 128 * f, 128 * f + 128, p=p), r("REP", 16 * (x % 32), 16 * (x % 32 + z - x), p=p)

    def hop(t, h, f):
        lo, hi = STREAMS[f]
        n, e, o, end = hi - lo, HO * f + h, lo // 16, h == HO - 1
        c = lambda name: r(name, lo, hi)
        p = slice(0, n)
        raw, wr, key, ee = ps(f, 0, n), ps(f, 128, 128 + n // 16), ps(f, 136, 288, p=p), ps(f, 288, 440, p=p)
        named = [len(ops)]

        def name(text):
            for x, nm in zip(ops[named[0]:], text.split()):
                x["hop"] = (NS * (HO * t + h) + f, nm)
            named[0] = len(ops)

        def part(x, a=0, z=None, step=1):
            return (x[0][p, a:z:step],) + x[1:5] + (len(range(a, z or x[5], step)),)
        if h:
            mm([(raw, Mp, ones(n), True, False)])
            mm([(raw, blk("W16", 1), c("Y"), False, False), (raw, ID, r("NM", 0, n), False, False),
                (raw, blk("W16", 0), c("Y"), False, True)], acc=True)
        else:
            mm([(raw, r("BLKf"), r("CN", 0, n), True, False)])
            mm([(raw, blk("W16", 3), c("QA"), False, False), (raw, Mp, ones(n), False, False),
                (raw, ID, r("NM", 0, n), False, False), (raw, blk("W16", 2), c("QA"), False, True)], acc=True)
        scan(r("SC", 768 + lo, 768 + hi), r("RESET", 0, n), raw, A.add, A.min)
        ts(lst(uL, f), r("SC", 768 + lo + 15, 768 + hi, 16), 2048.0 if h else col(14), A.add)
        name("M U sU tU")
        for x, z in ((lo, lo + C_CUT), (lo + C_CUT, hi)) if C_CUT else ((lo, hi),):
            cp(r("C16", x, z), ind(r("CT"), r("L16", uL + x // 16, uL + z // 16)))
        name("C C2")
        ts(c("CF"), c("C16"), -2048.0, A.add)
        tt(c("EQ"), c("CF"), ps(6, lo, hi), A.is_equal)
        key_end = lambda e: part(r3("PM", e), KW - 1, 152, KW)
        c_end = lambda e: part(r3("CS", e), KW - 1, 152, KW)
        slot = lambda j: ps(f, 288 + j, 440, KW, p=p)
        idf, nidf = part(IDf, 0, n), part(nIDf, 0, n)
        mm([(ee, c("CF"), r("DIFF"), True, not end)] +
           ([(slot(1), idf, c_end(e - 2), False, False), (slot(1), nidf, c_end(e - 1), False, False),
             (slot(2), idf, c_end(e - 1), False, True)] if end else []))
        mm([(key, r("IDb", 0, n), blk("MRH", h, 152), True, False), (key, c("EQ"), r("I65"), False, False)] +
           ([(ps(f, 136 + j, 288, KW, p=p), idf, key_end(e - 2 + j), False, False) for j in range(2)] if end else []))
        name("CF EQ ee key")

        def sums(src, j0, j1, bo, stop):
            x, z = CUTS[f][j0], CUTS[f][j1]
            mms([(ps(f, 138 + i, 288, KW, p=slice(x, z)), r(src, 16 * (lo + x) + i, 16 * (lo + z), 16), bo, False, stop and i == 15)
                 for i in range(16)], 8)
            name("%s%da %s%db" % (src[0], j0, src[0], j0))
        got = lambda x, z: ind(QW, r("C16", x // 16, z // 16))
        bank, todo = {}, [set(range(j0, j1)) for j0, j1 in PARTS]
        for step in (LAST_STEPS if end and f == NS - 1 else STEPS).split():
            kind, j = step[0], int(step[1])
            a, b = 16 * (lo + CUTS[f][j]), 16 * (lo + CUTS[f][j + 1])
            if kind == "g":
                bank[j] = ps(STAGE[stage[0] % len(STAGE)], 0, b - a)
                stage[0] += 1
                act(r("XG", a, b), got(a, b), F.Copy)
                mm([(bank[j],) + minus_a(f, j) + (True, False)])
                mm([(bank[j], ID, r("XG", a, b), False, True)])
                name("g%d n%d x%d" % (j, j, j))
            elif kind == "s":
                for x in range(a, b, V_CUT):
                    tt(r("XG", x, x + V_CUT), got(x, x + V_CUT), r("AREP", x, x + V_CUT), A.add)
                name("s%da s%db" % (j, j))
            elif kind == "a":
                act(r("AB", a, b), bank.get(j) or r("XG", a, b), F.Abs)
                name(step)
            else:
                ts(r("AB", a, b), r("XG", a, b), 0.0, A.max, 2.0, A.mult)
                name(step)
                sums("XG", j, j + 1, blk("BO", 1, 8), False)
            if kind in "ar":
                for (j0, j1), left in zip(PARTS, todo):
                    if j in left:
                        left.remove(j)
                        if not left:
                            sums("AB", j0, j1, blk("BO", 0, 8), True)
        pm, stp = part(r3("PM", e)), part(blk("STP", f, 152))
        scan(pm, part(r("RS")), key, A.add, A.min)
        tt(stp, key, pm, A.not_equal)
        scan(part(r3("CS", e)), ee, stp, A.add, A.mult)
        tt(blk("XH", f), ind(r3("CS", e), LBC), r("RM", 0, 128), A.mult)
        mm([(wr, part(blk("XH", f)), part(Q8, 0, n // 16), True, True)])
        name("PM NE CS XH wr")
        if not end:
            ts(lst(hL, f), wr, 2048.0, A.add)
            act(c("GM"), ind(r("ST" if t else "MPP"), lst(hL, f)), F.Copy)
            r2w(f, 0, [(SELMP if t else SELM, c("GM"))], c("SC"))
            ts(lst(mpL, f), r("SC", lo + 15, hi, 16), 2048.0, A.add)
            tt(c("Y"), ind(QW, lst(mpL, f)), c("A2"), A.add)
            name("tH GM N SEL sM tM Y")
            return
        cl = lst(cL, f)
        ts(cl, wr, 2048.0, A.add)
        name("tH")
        act(sm(464 + o, n // 16), wr, bias=2048.0)
        d64 = part(sm(320 + 8 * f, 8))
        x2 = lambda j: part(blk("X2", f), j, 128, 16)
        ts(d64, key_end(e), M64, A.add, M64, A.subtract)
        act(x2(15), key_end(e), bias=2.0 ** 24, scale=2.0 ** 19)
        act(part(sm(352 + 8 * f, 8)), d64, bias=M4096)
        act(x2(12), part(sm(352 + 8 * f, 8)), bias=-M4096)
        tt(x2(13), d64, x2(12), A.subtract)
        act(c("GSC"), ind(r("ST"), cl), F.Copy)
        if f < NS - 1:
            act(c("GB"), ind(r("BITS"), cl), bias=col(82 + t))
        else:
            ts(c("GB"), ind(r("BITS"), cl), col(82 + t), A.add)
        mm([(raw, part(blk("X2", f)), idf, True, False), (raw, part(blk("X3", f)), part(ID, 0, n), False, False)])
        mm([(raw, r("SELJ"), c("GSC"), False, True)], acc=True)
        tt(c("U2"), c("GB"), raw, A.max)
        scaled(r("GB", 256 + lo, 256 + hi), c("GB"), col(99))
        keys = r("SGF", 1536 + lo, 1536 + hi)
        act(keys, c("U2"), bias=sm(288 + t, 1), scale=col(63))
        silu(r("K1"), lst(aS, f), keys)
        for j in range(2):
            a, z = max(lo, 128 * j), min(hi, 128 * j + 128)
            if a < z and n < 128:
                mm([(ps(6, 448 + 8 * j, 456 + 8 * j, p=slice(a - 128 * j, z - 128 * j)), part(IDf, a - lo, z - lo), d64, True, True)])
            if lo < 128 * j + 128 <= hi:
                d = d64 if n == 128 else ps(6, 448 + 8 * j, 456 + 8 * j)
                act(r("LS", 48 * j + 2, 48 * j + 48, 6), d, bias=sm(96 + 8 * j + t, 1), scale=4.0)
                act(sm(608 + 8 * j, 8), d, bias=sm(256 + 8 * j + t, 1), scale=4.0)
                if j == 0:
                    pairs(0, 0, [("GB", 0, 128), ("GA", 0, 128)], PAIRS[0])
                    pairs(1, 0, [("GA", 0, 128)], PAIRS[1])

    turn = {}

    def pairs(j, slot, items, plan):
        wide = sum(z - x for _, x, z in items)
        for who, banks, groups in plan:
            for k0 in range(0, len(groups), 512 // wide):
                turn[banks] = turn.get(banks, -1) + 1
                b, some = banks[turn[banks] % len(banks)], groups[k0:k0 + 512 // wide]
                for i, k in enumerate(some):
                    p = slice(16 * k, 16 * k + 16) if k % 2 == 0 else slice(16 * k - 16, 16 * k + 16)
                    u0, o, got = 256 * (k % 2) + 128 * j, wide * i, []
                    for name, x, z in items:
                        got.append((ps(b, o, o + z - x), r(name, u0, u0 + 128, p=p), r("U2", x, z, p=p), True, True))
                        o += z - x
                    mm(got, acc=i > 0 and k // 2 == some[i - 1] // 2)
                for i, k in enumerate(some):
                    at, a = 48 * j + 6 * k, ps(b, wide * i, wide * i + wide)
                    if who == "v":
                        red(r("LW2", at + slot, at + slot + 1), a, A.max)
                    else:
                        act(r("MPP", 512 * k, 512 * k + wide), a, F.Relu, bias=r("LS", at + 2, at + 3),
                            accum=r("LS", at + 3 + slot, at + 4 + slot))

    def swap(b, lo, n, ms, src, first, last):
        out = [(ps(b, lo + j, lo + n, 2), m, src(1 - j), first, first) for m in ms for j in range(2)]
        return out[:-1] + [out[-1][:4] + (last,)]

    def silu(win, to, a, more=0):
        add("s", [lambda: g.scalar.activation(ind(win, to)[0], a[0], F.Silu)], [a, to], [win], 65 + 3.8 * a[5] + more)

    def put_out(out, b, n, sel, o):
        mms([(ps(b, 0, n), r(sel, 15 - j, 143 - j), blk("ST", j, n), j == 0, j == 15) for j in range(16)], 2)
        act(r("BLD", o, o + n), ps(b, 0, n), bias=2048.0)
        dma("y", out, T.BLD[:, o:o + n], [r("BLD", o, o + n)], [], 2500)

    later = [start_rows]
    bonus[0] = FIRST
    lanes(0)
    bonus[0] = WRAP
    start_mates()
    for t in range(RO):
        last = t == RO - 1
        for f, (lo, hi) in enumerate(STREAMS):
            bonus[0] = SKEW * (NS - 1 - f)
            act(r("QA", lo, hi), ind(QW, lst(aL, f)), F.Copy)
            act(r("GSA", lo, hi), ind(r("ST", 0, 2048), lst(aL, f)), F.Copy)
            mm([(ps(6, lo, hi), SELID, r("GSA", lo, hi), True, True)])
            p = slice(0, hi - lo)
            ax, at = ps(7, 256 + lo, 256 + hi), ps(AT_BANK[f], 128, 256, p=p)
            mm([(at, r("QA", lo, hi), r("XP"), True, True)])
            scaled(r("AT", 128 * f, 128 * f + 128, p=p), at, -1.0)
            for j, who in enumerate(A_REP[f]):
                if who != "-":
                    x, z = 16 * (lo + CUTS[f][j]), 16 * (lo + CUTS[f][j + 1])
                    b = ps(A_BANK[f][j], 0, z - x)
                    mm([(b,) + minus_a(f, j) + (True, True)])
                    (cp if who == "v" else lambda o, a: scaled(o, a, 1.0))(r("AREP", x, z), b)
            mm([(ax, r("XP"), r("QA", lo, hi), True, True)])
            act(r("A2", lo, hi), ax, bias=OFFA)
        bonus[0] = 0.0
        later[0]()
        for h in range(HO):
            for f in range(NS):
                bonus[0] = SKEW * (NS - 1 - f)
                hop(t, h, f)
            bonus[0] = 0.0
            if h == 0:
                if t == 0:
                    n0 = len(ops)
                    late_constants()
                    for x in ops[n0:]:
                        if x["eng"] in "sv":
                            x["after"] = max(i for i in range(n0) if ops[i].get("hop") == (0, LATE))
                act(r("GA", 0, 256), ind(r("BITS"), lst(aL)), bias=col(82 + t))
                scaled(r("GA", 256, 512), r("GA", 0, 256), col(99))
        act(r("GK"), ind(r("K1"), lst(cL)), bias=-64.0)
        mm([(ps(6, 256, 272), nIDf, sm(608), True, False)])
        mm([(ps(6, 256 + 8 * f, 264 + 8 * f), blk("GK", f), KS8, False, f == 1) for f in range(2)], acc=True)
        act(r("LS", 5, 96, 6), ps(6, 256, 272), F.Relu, scale=-2.0)
        r2w(7, 0, [(SELP, r("GSC"))], r("SC", 256, 512))
        act(sm(480), r("SC", 271, 512, 16), bias=2048.0)
        r2w(7, 0, [(SELLO, r("GK"))], r("SC", 0, 256))
        act(sm(336), r("SC", 15, 256, 16), bias=(t + 1) * 2.0 ** 20)
        tt(sm(496), sm(336), sm(80), A.min)
        scaled(r("SGF", 768, 1024), r("RM"), 1.0 / 8192)
        mm([(ps(6, 272, 352), ID, r("T80"), True, False), (ps(6, 272, 320), M4K, ones(48), False, False)])
        pairs(0, 1, [("GB", 128, 256), ("GA", 128, 256)], PAIRS[2])
        pairs(1, 1, [("GB", 0, 256), ("GA", 128, 256)], PAIRS[3])
        for f in range(2):
            o = 8 * f
            scan(blk("LO", f, 48), blk("LS", f, 48), blk("LW2", f, 48), A.add, A.max)
            tt(blk("XS", f), ind(blk("LO", f, 48), L3), r("RMH"), A.is_equal)
            mm([(ps(6, 272 + 16 * j + o, 280 + 16 * j + o), blk("XS", f), Q8n, False, j == 4 and f == 1) for j in range(5)], acc=True)
        act(r("QC"), ind(QW, lst(cL)), F.Copy)
        tt(r("TMP", 0, 64), ps(6, 272, 336), ends, A.max)
        cp(r("P16", 0, 64), r("TMP", 0, 64))
        jA, jC, jO, jL = (blk("P16", j, 16) for j in range(4))
        mm([(ps(7, 256, 512), blk("PO", j), r("GSC"), j == 0, j == 1) for j in range(2)])
        act(r("YS"), ps(7, 256, 512), bias=col(90))
        for j, (x, z) in enumerate((("GSC", "GSA"), ("GSA", "GSC"))):
            o = ps(5, 256 * j, 256 * j + 256)
            mm([(o, r("KEEP"), r(x), True, False), (o, r("SHIFT"), r(z), False, False), (o, r("DM"), r("U2"), False, True)])
        act(r("VV"), ps(5), bias=col(100))
        mm([(ps(7, 0, 256), r("XP"), r("QC"), True, False), (ps(7, 0, 256), r("nIDb"), r("QA"), False, True)])
        mm([(ps(7, 256, 512), r("XP"), r("QA"), True, False), (ps(7, 256, 512), r("nIDb"), r("QC"), False, True)])
        act(r("A2"), r("GSA"), bias=4096.0)
        bonus[0] = 4000.0
        silu(r("SGF", 768, 1280), jL, r("SGF", 1280, 1536))
        bonus[0] = 0.0
        act(r("SGN"), ps(7), F.Sign)
        cp(ind(r("ST"), jO), r("YS"))
        bonus[0] = URGE[0]
        cp(ind(r("ST"), jC), r("VV", 0, 256))
        bonus[0] = URGE[1]
        cp(ind(r("ST"), jA), r("VV", 256, 512))
        bonus[0] = URGE[2]
        scan(r("SC", 0, 256), r("RESET", 256, 512), r("SGF", 768, 1024), A.add, A.max)
        t1 = r("T16", 0, 16)
        tt(r("RF"), r("SC", 15, 256, 16), ps(6, 336, 352), A.mult)
        tt(t1, r("RF"), sm(80), A.mult)
        mm([(ps(4, 256, 272), r("TRIB"), r("RF"), True, False), (ps(4, 257, 272), r("NTM"), r("RF", 0, 15), False, False),
            (ps(4, 256, 272), r("nIDb"), t1, False, False), (ps(4, 257, 272), ID, r("T16", 0, 15), False, True)])
        scan(sm(384), r("C16B", 0, 16), ps(4, 256, 272), A.add, A.add, col(94))
        cp(dL, sm(384))
        cp(ind(r3("SBQ", t), dL), r("QA"))
        tr = []
        for d in range(1, NR):
            dst = T.cores[(rank + d) % NR]
            rid, pid = topo.addr(dst)[:2]
            mask = sum(1 << e for e in topo.engines(core, dst)[4 * (d - 1):4 * d])
            tr.append(RemoteDMATransfer(dst_ids=[DstId(rid=rid, pnc=pid)], dma_engine_mask=mask, remote_sem=T.sem["arr%d" % t],
                                        src=T.SBQ[:, t, 32 * (d - 1):32 * d], dst=T.LAND[:, t, 32 * (d - 1):32 * d]))
        add("g", [lambda tr=tr: g.remote_dma_fused(tr, local_sem=T.sem.sent)], [r3("SBQ", t, 0, 96)], [r3("LAND", t)], 300.0,
            sem="arr%d" % t, val=4 * (NR - 1), lat=FAR, remote=True)
        bonus[0] = 0.0
        n = sm(303, 1)
        mm([(ps(5, 496, 512), r("BLKb"), r("RF"), True, True)])
        act(sm(272), ps(5, 496, 512), F.Copy, scale=-8192.0, accum=n)
        silu(r("SGF", 0, 768), dL, r("A2"))
        act(r("TMP", 128, 224), r("SGF", 0, 96), bias=M1 - 4096.0)
        act(r("SG", 0, 96), r("TMP", 128, 224), bias=-M1)
        bonus[0] = -3000.0
        tt(ind(QW, jA), r("SGN", 0, 256), r("QA"), A.add)
        tt(ind(QW, jC), r("SGN", 256, 512), r("QC"), A.add)
        bonus[0] = 0.0
        if last:
            put_out(T.yp[:], 0, 256, "B23", 0)
        else:
            lanes(t + 1)
        r2w(5, 288, [(SELID, r("SG", 0, 96)), (SELM, r("SG", 0, 96))], r("SC", 256, 448))
        act(sm(512, 18), sm(112, 18), bias=n)
        tt(sm(544, 18), sm(512, 18), sm(130, 18), A.min)
        ts(r("KR", 96, 192), r("KR", 0, 96), n, A.add, 0.0, A.is_lt)
        tt(sm(568, 6), r("SC", 271, 352, 16), sm(544, 6), A.max)
        tt(sm(574, 12), r("SC", 271, 448, 16), sm(550, 12), A.max)
        ts(r("L16", kL, kL + 18), sm(568, 18), 2048.0, A.add)
        sL, vsL, vmL, pmL = [r("L16", kL + 6 * j, kL + 6 * j + 6) for j in range(4)]
        act(r("QM", 0, 96), ind(QW, vmL), F.Copy)
        sg = lambda j: r("SG", j, 96, 2)
        mm(swap(5, 0, 96, [blk("MSW", 0)], sg, True, True) + swap(5, 96, 96, [blk("MSW", 1)], sg, True, True) +
           [(ps(5, 192, 288), blk("MSW", 4), r("SG", 0, 96), True, False)] +
           swap(5, 192, 96, [blk("MSW", 2), blk("MSW", 3)], sg, False, True))
        act(r("SW"), ps(5, 0, 288), F.Copy)
        UP, nUP, LOW = (blk("UP", j) for j in range(3))
        mm([(ps(4, 0, 96), LOW, r("QM", 0, 96), True, False)] + swap(4, 0, 96, [UP], lambda j: r("QM", j, 96, 2), False, True))
        act(r("QM", 96, 192), ps(4, 0, 96), F.Copy)
        cp(ind(QW, vmL), r("QM", 96, 192))
        land = lambda j, x=0, s=1: r3("LAND", t, 32 * j + x, 32 * j + 32, s)
        mm([(ps(7, 0, 96), ID, r3("SBQ", t, 0, 96), True, False)])
        mm([(ps(7, 32 * j, 32 * j + 32), blk("ROT", 3 + j), land(j), False, j == 2) for j in range(3)], acc=True)
        RR, RA, TQ = (blk("RR", j, 96) for j in range(3))
        act(RR, ps(7, 0, 96), F.Relu, bias=-255.0)
        mm([(ps(6, 352, 448), ZERO, ones(96), True, False)])
        mm([(ps(6, 352 + 32 * j, 384 + 32 * j), blk("ROT", j), land(j), False, False) for j in range(3)], acc=True)
        mm([(ps(6, 352, 448), ID, RR, False, True)], acc=True)
        act(RA, ps(6, 352, 448), F.Copy)
        mm([(ps(1, 384, 480), ZERO, ones(96), True, False)])
        mm([x for j in range(3) for x in [(ps(1, 384 + 32 * j, 416 + 32 * j), blk("ROT", 9 + j), land(j), False, False)] +
            swap(1, 384 + 32 * j, 32, [blk("ROT", 6 + j)], lambda x, j=j: land(j, x, 2), False, False)], acc=True)
        mm([(ps(1, 384, 480), nUP, RR, False, False)] +
           swap(1, 384, 96, [UP], lambda j: r("RR", j, 96, 2), False, True), acc=True)
        tt(TQ, ps(1, 384, 480), r("KR", 96, 192), A.mult)
        if last:
            dma("y", T.yq[:, 2048:4096], T.Q[:, Q0 + 2048:Q0 + 4096], [r("Q", Q0 + 2048, Q0 + 4096)], [], 4000)
            act(sm(624, 6), sm(512, 6), scale=-1.0)
            act(sm(632, 6), sm(0, 6), bias=-6144.0 - Q0)
            tt(sm(640, 6), sm(624, 6), sm(632, 6), A.max)
            tt(sm(648, 6), r("SC", 271, 352, 16), sm(640, 6), A.min)
            ts(pmL, sm(648, 6), 2048.0 + Q0, A.add)
            tt(ind(r("Q", 0, Q0 + 2048), pmL), TQ, RA, A.add)
            for j, q in enumerate("ys"):
                dma(q, T.yq[:, 1024 * j:1024 * j + 1024], T.Q[:, Q0 + 1024 * j:Q0 + 1024 * j + 1024],
                    [r("Q", Q0 + 1024 * j, Q0 + 1024 * j + 1024)], [], 3000)
        else:
            tt(ind(QW, sL), TQ, RA, A.add)
        cp(ind(r("ST"), vsL), r("SW", 192, 288))
        if last:
            put_out(T.ym[:], 1, 128, "B45", 256)
        else:
            def mend(vmL=vmL, pmL=pmL):
                gm, gp = r("GMM", 0, 96), r("GMM", 96, 192)
                act(gm, ind(r("ST"), vmL), F.Copy, scale=col(91))
                tt(ind(r("ST"), vmL), gm, r("SW", 0, 96), A.add)
                r2w(3, 0, [(SELP, gm)], r("SC", 512, 608))
                tt(sm(624, 6), r("SC", 527, 608, 16), sm(550, 6), A.max)
                ts(pmL, sm(624, 6), 2048.0, A.add)
                act(gp, ind(r("ST"), pmL), F.Copy, scale=col(92))
                tt(ind(r("ST"), pmL), gp, r("SW", 96, 192), A.add)
            later[0] = mend
    return ops


def depend(ops, turns=None):
    hist = {}
    for i, o in enumerate(ops):
        deps = {}
        for kind, xs in (("r", o["reads"]), ("w", o["writes"])):
            for x in xs:
                name, lo, hi, row = x[1:5]
                bank = name[:2] == "ps"
                if bank:
                    lo, hi = 0, 512
                keep = []
                for e in hist.get(name, []):
                    j, k2, l2, h2, r2 = e
                    meet = l2 < hi and lo < h2 and (row is None or r2 is None or row == r2)
                    if meet and j != i:
                        same = ops[j]["eng"] == o["eng"]
                        if kind == "w" or k2 == "w" or (bank and not same):
                            hard = not (bank and same and o["acc"])
                            deps[j] = deps.get(j, False) or hard
                    whole = x[5] >= hi - lo or bank
                    if kind == "w" and whole and meet and lo <= l2 and h2 <= hi and (row is None or row == r2):
                        continue
                    keep.append(e)
                keep.append((i, kind, lo, hi, row))
                hist[name] = keep
        if turns and "after" in o:
            deps.setdefault(o["after"], False)
        o["deps"] = deps
    for text in (turns or {}).values():
        place = {x.rstrip("'"): (x.count("'"), k) for k, x in enumerate(text.split())}
        turn = sorted((o["hop"][0] // (len(STREAMS) * HO), o["hop"][0] + place[o["hop"][1]][0], place[o["hop"][1]][1], i)
                      for i, o in enumerate(ops) if o.get("hop") and o["hop"][1] in place)
        for a, b in zip(turn, turn[1:]):
            ops[b[3]]["deps"].setdefault(a[3], False)


def schedule(ops):
    n = len(ops)
    succ = [[] for _ in ops]
    for i, o in enumerate(ops):
        for j in o["deps"]:
            succ[j].append(i)

    def gap(j, i):
        if not ops[i]["deps"][j]:
            return 0.0
        return ops[j]["lat"] + (SAME if ops[j]["eng"] == ops[i]["eng"] else CROSS)
    left = [len(o["deps"]) for o in ops]
    line = [i for i in range(n) if not left[i]]
    for i in line:
        for s in succ[i]:
            left[s] -= 1
            if not left[s]:
                line.append(s)
    prio = [0.0] * n
    for i in reversed(line):
        prio[i] = ops[i]["cost"] + max([ops[i]["lat"]] + [gap(i, s) + prio[s] for s in succ[i]])
    left = [len(o["deps"]) for o in ops]
    rdy = {i: 0.0 for i in range(n) if not left[i]}
    free = {e: 0.0 for e in "vstgy"}
    end = [0.0] * n
    order = []
    while rdy:
        est = {i: max(rdy[i], free[ops[i]["eng"]]) for i in rdy}
        first = min(est, key=lambda i: (est[i], -prio[i]))
        e = ops[first]["eng"]
        cand = [i for i in rdy if ops[i]["eng"] == e and est[i] <= est[first] + min(LOOK, 0.7 * ops[first]["cost"])]
        i = max(cand, key=lambda i: prio[i] + ops[i]["bonus"])
        end[i] = est[i] + ops[i]["cost"]
        ops[i]["t0"] = est[i]
        free[e] = end[i]
        del rdy[i]
        order.append(i)
        for s in succ[i]:
            left[s] -= 1
            if not left[s]:
                rdy[s] = max(end[j] + gap(j, s) for j in ops[s]["deps"])
    return order


def polish(ops, order):
    n = len(ops)
    cost, lat, eng = ([o[k] for o in ops] for k in ("cost", "lat", "eng"))
    pred = [[(j, cost[j] + (lat[j] + (SAME if eng[j] == eng[i] else CROSS) if hard else 0.0)) for j, hard in o["deps"].items()]
            for i, o in enumerate(ops)]
    succ = [[] for _ in ops]
    for i in range(n):
        for j, w in pred[i]:
            succ[j].append((i, w))
    seed = [12345]

    def draw():
        seed[0] = (seed[0] * 1103515245 + 12345) & 0x7FFFFFFF
        return seed[0] / 2147483648.0

    def window(a):
        head, tail, free, after = [0.0] * n, [0.0] * n, {}, {}
        for i in order:
            head[i] = max([free.get(eng[i], 0.0)] + [head[j] + w for j, w in pred[i]])
            free[eng[i]] = head[i] + cost[i]
        for i in reversed(order):
            tail[i] = max([cost[i] + lat[i], cost[i] + after.get(eng[i], 0.0)] + [w + tail[s] for s, w in succ[i]])
            after[eng[i]] = tail[i]
        order.sort(key=lambda i: head[i])
        win = order[a:a + WINDOW]
        inside = set(win)
        free = {eng[i]: head[i] + cost[i] for i in order[:a]}
        after = {eng[i]: tail[i] for i in reversed(order[a + WINDOW:])}
        rel = {i: max([0.0] + [head[j] + w for j, w in pred[i] if j not in inside]) for i in win}
        out = {i: max([cost[i] + lat[i]] + [w + tail[s] for s, w in succ[i] if s not in inside]) for i in win}
        ins = {i: [(j, w) for j, w in pred[i] if j in inside] for i in win}
        seq = {}
        for i in win:
            seq.setdefault(eng[i], []).append(i)
        pool = [eng[i] for i in win]

        def value(old, since, limit):
            h, pos, fr, left, top, tot = {}, {}, {}, len(win), 0.0, 0.0
            for e, s in seq.items():
                k, f = 0, free.get(e, 0.0)
                while k < len(s) and old[s[k]] < since:
                    i = s[k]
                    h[i] = t = old[i]
                    f, k, t = t + cost[i], k + 1, t + out[i]
                    tot += t
                    if t > top:
                        top = t
                pos[e], fr[e], left = k, f, left - k
            while left:
                was = left
                for e, s in seq.items():
                    k, f = pos[e], fr[e]
                    while k < len(s):
                        i = s[k]
                        t = rel[i] if rel[i] > f else f
                        for j, w in ins[i]:
                            x = h.get(j)
                            if x is None:
                                break
                            if x + w > t:
                                t = x + w
                        else:
                            h[i], f, k, left = t, t + cost[i], k + 1, left - 1
                            t += out[i]
                            tot += t
                            if t > top:
                                top = t
                            continue
                        break
                    pos[e], fr[e] = k, f
                if left == was or top > limit:
                    return None, None
            return max([top] + [fr[e] + after.get(e, 0.0) for e in seq]) + 0.05 * tot / len(win), h
        now, times = value(head, -1.0, 1e30)
        best = (now, times)
        for it in range(TRIES):
            s = seq[pool[int(draw() * len(pool))]]
            i, k = int(draw() * len(s)), 1 + int(draw() ** 3 * REACH)
            j = i + k if draw() < 0.5 else i - k
            if not 0 <= j < len(s) or any(s[i] in ops[y]["deps"] for y in s[i + 1:j + 1]) or any(y in ops[s[i]]["deps"] for y in s[j:i]):
                continue
            since, limit = times[s[min(i, j)]], now - HEAT * (1.02 - it / TRIES) * math.log(draw() + 1e-9)
            s.insert(j, s.pop(i))
            v, h = value(times, since, limit / 1.04)
            if v is not None and v <= limit:
                now, times = v, h
                if v < best[0]:
                    best = (v, h)
            else:
                s.insert(i, s.pop(j))
        order[a:a + WINDOW] = sorted(win, key=lambda i: best[1][i])
    for _ in range(SWEEPS):
        for a in range(0, n, WINDOW // 2):
            window(a)
    return order


ORDER = []


def plan(ops):
    if not ORDER:
        depend(ops, TEMPLATE)
        first = schedule(ops)
        depend(ops)
        ORDER.extend(polish(ops, first))
    else:
        depend(ops)
    return ORDER


def rank_program(g, core, T, topo):
    if T.rank_of(core) is None:
        return
    ops = build(g, T, topo, core)
    order = plan(ops)
    queue = {"v": g.vector, "s": g.scalar, "t": g.tensor, "g": g, "y": g.sync}
    count = {e: 0 for e in "vstg"}
    seen = {e: {} for e in queue}
    total = {}
    for i in order:
        o = ops[i]
        q, need = queue[o["eng"]], {}
        for j, hard in o["deps"].items():
            if hard:
                s, v = ops[j]["done"]
                need[s] = max(need.get(s, 0), v)
        for s, v in need.items():
            if seen[o["eng"]].get(s, 0) < v:
                q.wait_ge(T.sem[s], v)
                seen[o["eng"]][s] = v
        for fn in o["fns"]:
            ins = fn()
        if o["sem"] is None:
            count[o["eng"]] += 1
            o["done"] = ("e" + o["eng"], count[o["eng"]])
            ins.then_inc(T.sem[o["done"][0]], 1)
        else:
            o["done"] = (o["sem"], o["val"])
            if not o.get("remote"):
                ins.then_inc(T.sem[o["sem"]], 16)
        total[o["done"][0]] = o["done"][1]
    total["sent"] = RO * 4 * (NR - 1)
    for s, v in total.items():
        g.wait_ge(T.sem[s], v)
